import numpy as np
import ml_dtypes


def mxq(x, axis, fmt="e4m3"):
    dtype, down = {"e4m3": (ml_dtypes.float8_e4m3fn, 7), "e5m2": (ml_dtypes.float8_e5m2, 14)}[fmt]
    v = np.moveaxis(np.asarray(x, np.float32).astype(ml_dtypes.bfloat16).astype(np.float64), axis, -1)
    blocks = v.reshape(v.shape[:-1] + (-1, 32))
    amax = np.abs(blocks).max(-1, keepdims=True)
    byte = np.maximum(np.where(amax > 0, np.frexp(amax)[1] - 1 + 127, 0) - down, 1)
    scale = np.exp2(byte - 127.0)
    codes = (blocks / scale).astype(np.float32).astype(dtype).astype(np.float64)
    return np.moveaxis((codes * scale).reshape(v.shape), -1, axis)


WIDE = False


def mx_kscale(k):
    if not WIDE:
        return np.ones(k)
    levels = np.array([10, -10, 5, -5, 0])
    if k % 512:
        return np.exp2(np.random.permutation(np.resize(levels, k // 32))).repeat(32)
    a = np.empty((k // 512, 16))
    for p in range(k // 512):
        a[p, :8] = np.random.permutation(np.resize(levels, 8))
        for g in range(8):
            far = levels[np.abs(levels - a[p, g]) >= 10]
            a[p, g + 8] = far[np.random.randint(len(far))]
    return np.exp2(a.ravel()).repeat(32)


def f64(x):
    return np.asarray(x).astype(np.float64)


def striped(idx):
    return np.tile(idx.reshape(-1, 16).T, (8, 1)).astype(np.uint16)


def unstriped(offs):
    return offs[:16].T.reshape(-1).astype(np.int64)


E2M1 = np.array([0.0, 0.5, 1.0, 1.5, 2.0, 3.0, 4.0, 6.0, -0.0, -0.5, -1.0, -1.5, -2.0, -3.0, -4.0, -6.0])


def pack_weight(w, fmt):
    k, n = w.shape
    w = f64(np.asarray(w, np.float32).astype(ml_dtypes.bfloat16)).reshape(k // 32, 32, n)
    amax = np.abs(w).max(1)
    if fmt == "e4m3":
        byte = np.frexp(amax)[1] - 1 + 127 - 7
    else:
        mant, ex = np.frexp(amax / 6.0)
        byte = np.where(mant > 0.5, ex, ex - 1) + 127
    byte = np.clip(np.where(amax > 0, byte, 1), 1, 254)
    scaled = (w * np.exp2(127.0 - byte)[:, None, :]).reshape(k, n).astype(np.float32)
    by_word = np.ascontiguousarray(scaled.reshape(k // 512, 128, 4, n).transpose(0, 1, 3, 2))
    if fmt == "e4m3":
        words = by_word.astype(ml_dtypes.float8_e4m3fn).view(np.uint8)
    else:
        c = by_word.astype(ml_dtypes.float4_e2m1fn).view(np.uint8) & 0xF
        words = (c[..., 0::2] | (c[..., 1::2] << 4)).reshape(k // 512, 128, 2 * n)
    return np.ascontiguousarray(words), np.ascontiguousarray(byte.astype(np.uint8).reshape(k // 512, 16, n))


def unpack_weight(words, scales, fmt):
    g, _, n = scales.shape
    words = np.ascontiguousarray(words).reshape(g, 128, n, -1)
    if fmt == "e4m3":
        vals = words.view(ml_dtypes.float8_e4m3fn).astype(np.float64)
    else:
        nib = np.empty((g, 128, n, 4), np.uint8)
        nib[..., 0::2] = words & 0xF
        nib[..., 1::2] = words >> 4
        vals = E2M1[nib]
    vals = vals * np.repeat(np.exp2(scales.astype(np.float64) - 127.0), 8, axis=1)[..., None]
    return vals.transpose(0, 1, 3, 2).reshape(g * 512, n)


D, T, E, C, H, N = 2, 256, 4, 256, 512, 256


def by_expert(wq, xq):
    return np.concatenate([wq[e].T @ xq[:, e * C:(e + 1) * C] for e in range(E)], axis=1)


def setup_inputs():
    n = np.random.standard_normal
    s = np.tile(mx_kscale(H), D)
    u = mx_kscale(H)
    X = D * T
    first = np.random.permutation(np.repeat(np.arange(E), X // E))
    second = (first + 1 + np.random.permutation(np.repeat(np.arange(E - 1), -(-X // (E - 1)))[:X])) % E
    while np.bincount(second, minlength=E).max() != X // E:
        load = np.bincount(second, minlength=E); hi, lo = int(load.argmax()), int(load.argmin())
        t = np.flatnonzero((second == hi) & (first != lo))[0]; second[t] = lo
    slot_sub = np.empty(E * C, np.int64); pos = np.empty((2, X), np.int64); fill = np.zeros(E, np.int64)
    place = np.stack([np.random.permutation(C) for _ in range(E)])
    for r, deal in enumerate((first, second)):
        for t in np.random.permutation(X):
            e = deal[t]; j = e * C + place[e, fill[e]]; fill[e] += 1; slot_sub[j] = t; pos[r, t] = j
    g = np.random.uniform(0.2, 0.8, X)
    x = pack_weight(n((D * H, T)) * s[:, None], "e4m3")
    w = [pack_weight(m, "e4m3") for m in n((E, H, H)) / np.sqrt(H) / s[None, :H, None] * u]
    wm = pack_weight(n((D * H, N)) / np.sqrt(D * H) / np.tile(u, D)[:, None], "e4m3")
    return {
        "x_words": x[0],
        "x_scales": x[1],
        "w_words": np.stack([m[0] for m in w]),
        "w_scales": np.stack([m[1] for m in w]),
        "wm_words": wm[0],
        "wm_scales": wm[1],
        "gate": np.stack([np.tile(g, (128, 1)), np.tile(1.0 - g, (128, 1))]).astype(np.float32),
        "offs": striped(slot_sub),
        "pos1": striped(pos[0]),
        "pos2": striped(pos[1]),
    }


def reference(x_words, x_scales, w_words, w_scales, wm_words, wm_scales, gate, offs, pos1, pos2):
    w = np.stack([unpack_weight(w_words[e], w_scales[e], "e4m3") for e in range(E)])
    wm = unpack_weight(wm_words, wm_scales, "e4m3")
    idx = unstriped(offs)
    x = unpack_weight(x_words, x_scales, "e4m3")
    sub = x.reshape(D, H, T).transpose(1, 0, 2).reshape(H, D * T)
    y = by_expert(w, sub[:, idx])
    c = sum(f64(gate[r, :1]) * y[:, unstriped(p)] for r, p in enumerate((pos1, pos2)))
    cq = mxq(c, 0, "e4m3").reshape(H, D, T).transpose(1, 0, 2).reshape(D * H, T)
    return wm.T @ cq

@@ -1,0 +1,185 @@
+from contextlib import ExitStack
+
+import concourse.mybir as mybir
+from concourse.masks import make_identity
+
+F32 = mybir.dt.float32
+BF16 = mybir.dt.bfloat16
+I32 = mybir.dt.int32
+U32 = mybir.dt.uint32
+U16 = mybir.dt.uint16
+U8 = mybir.dt.uint8
+FP8X4 = mybir.dt.float8_e4m3fn_x4
+MULT = mybir.AluOpType.mult
+
+P = 128
+D, T, E, C, H, N = 2, 256, 4, 256, 512, 256
+Z = D * T
+S = E * C
+LT = H // P
+ZT = Z // P
+FLOPS = 2 * H * H * S + 2 * D * H * N * T
+
+
+def tile_moe_mhm_none_kernel(
+    tc, x_words, x_scales, w_words, w_scales, wm_words, wm_scales, gate, offs, pos1, pos2, out
+):
+    nc = tc.nc
+    with ExitStack() as ctx:
+        sb = ctx.enter_context(tc.tile_pool(name="sb", bufs=1))
+        ps = ctx.enter_context(tc.psum_pool(name="ps", bufs=1))
+
+        def tile(shape, dtype, name):
+            return sb.tile(shape, dtype, name=name, align_bytes=64)
+
+        def bank(shape, b, name):
+            return ps.tile(shape, F32, name=name, tag="bank%d" % b)
+
+        offs_sb = tile([P, S // 16], U16, "offs_sb")
+        pos_sb = [tile([P, Z // 16], U16, "pos%d_sb" % r) for r in range(2)]
+        xw = tile([P, Z], I32, "xw")
+        xs = tile([P, Z], U8, "xs")
+        ww = [tile([P, 2, H], I32, "ww%d" % i) for i in range(E // 2)]
+        ws = tile([P, H], U8, "ws")
+        mw = tile([P, D, N], I32, "mw")
+        ms = tile([P, N], U8, "ms")
+        gate_sb = tile([P, 2, Z], F32, "gate_sb")
+        ident = tile([P, P], F32, "ident")
+
+        nc.vector.memset(xs[:].bitcast(I32), 0)
+        nc.vector.memset(ws[:].bitcast(I32), 0)
+        nc.vector.memset(ms[:].bitcast(I32), 0)
+
+        nc.sync.dma_start(offs_sb[:], offs)
+        nc.sync.dma_start(
+            xw[:].rearrange("p (o t) -> p o t", o=D),
+            x_words.rearrange("o p t d -> p o (t d)").bitcast(I32),
+        )
+        for q in range(4):
+            nc.scalar.dma_start(
+                xs[32 * q : 32 * q + 4, :].bitcast(I32).rearrange("r (o t) -> r o t", o=D),
+                x_scales[:, 4 * q : 4 * q + 4, :].bitcast(I32).rearrange("o r t -> r o t"),
+            )
+        for q in range(4):
+            nc.scalar.dma_start(
+                ws[32 * q : 32 * q + 4 * E, :].bitcast(I32),
+                w_scales[:, 0, 4 * q : 4 * q + 4, :].bitcast(I32),
+            )
+        for i in range(E // 2):
+            nc.sync.dma_start(ww[i][:], w_words[2 * i : 2 * i + 2, 0].rearrange("e p l d -> p e (l d)").bitcast(I32))
+        nc.sync.dma_start(pos_sb[0][:], pos1)
+        nc.sync.dma_start(pos_sb[1][:], pos2)
+        nc.sync.dma_start(gate_sb[:], gate.rearrange("r p z -> p r z"))
+        nc.sync.dma_start(mw[:], wm_words.rearrange("o p n d -> p o (n d)").bitcast(I32))
+        for q in range(4):
+            nc.scalar.dma_start(
+                ms[32 * q : 32 * q + 4 * D, :].bitcast(I32),
+                wm_scales[:, 4 * q : 4 * q + 4, :].bitcast(I32),
+            )
+        make_identity(nc, ident[:])
+
+        xg = [tile([P, C], U32, "xg%d" % e) for e in range(E)]
+        sg = [tile([P, C], U8, "sg%d" % e) for e in range(E)]
+        for e in range(E):
+            lst = offs_sb[:, e * C // 16 : (e + 1) * C // 16]
+            nc.vector.tensor_copy(xg[e][:], xw[:].bitcast(U32).indirect(lst))
+            nc.vector.tensor_copy(sg[e][:], xs[:].indirect(lst))
+
+        y = [tile([P, S], F32, "y%d" % t) for t in range(LT)]
+        order = [(0, 0), (1, 0), (0, 1), (2, 0), (1, 1), (3, 0), (2, 1), (3, 1)] + [(e, t) for t in range(2, LT) for e in range(E)]
+        for i, (e, t) in enumerate(order):
+            acc = bank([P, C], i % 5, "yacc%d" % i)
+            cols = slice(t * P, (t + 1) * P)
+            nc.tensor.matmul_mx(
+                out=acc[:],
+                lhsT=ww[e // 2][:, e % 2, cols].bitcast(FP8X4),
+                lhsT_scale=ws[4 * e : P, cols],
+                rhs=xg[e][:].bitcast(FP8X4),
+                rhs_scale=sg[e][:],
+                start=True,
+                stop=True,
+            )
+            nc.scalar.copy(y[t][:, e * C : (e + 1) * C], acc[:])
+
+        cT = [tile([P, n, 2, P, 2], BF16, "cT%d" % i) for i, n in enumerate((2, 1, 1))]
+
+        def combine(piece, s0, ns, t, b):
+            zs = slice(s0 * P, (s0 + ns) * P)
+            part = [tile([P, ns * P], F32, "part%d_%d_%d" % (piece, t, r)) for r in range(2)]
+            for r in range(2):
+                lst = pos_sb[r][:, s0 * P // 16 : (s0 + ns) * P // 16]
+                nc.vector.tensor_tensor(part[r][:], y[t][:].indirect(lst), gate_sb[:, r, zs], MULT)
+            turned = bank([P, ns, P], b, "turned%d_%d" % (piece, t))
+            for s in range(ns):
+                for r in range(2):
+                    nc.tensor.matmul(
+                        turned[:, s, :], part[r][:, s * P : (s + 1) * P], ident[:],
+                        start=(r == 0), stop=(r == 1), is_transpose=True,
+                    )
+            nc.scalar.copy(
+                cT[piece][:, :, :, 32 * t : 32 * (t + 1), :].rearrange("z s u q k -> z u s q k"),
+                turned[:].rearrange("z s (q u k) -> z u s q k", u=2, k=2),
+            )
+
+        grouped = [tile([P, n * H], BF16, "grouped%d" % i) for i, n in enumerate((2, 1, 1))]
+        place = [(0, 0), (0, 1), (1, 0), (2, 0)]
+
+        def turn_back(s, b):
+            piece, i = place[s]
+            words = cT[piece][:, i].rearrange("z u p k -> z (u p k)").bitcast(F32)
+            back = bank([P, 2, P], b, "back%d" % s)
+            for u in range(2):
+                nc.tensor.transpose(back[:, u, :], words[:, u * P : (u + 1) * P], ident[:])
+            g, j = place[s]
+            nc.scalar.copy(
+                grouped[g][:, j * H : (j + 1) * H].bitcast(F32).rearrange("p (z u) -> p z u", u=2),
+                back[:].rearrange("p u z -> p z u"),
+            )
+
+        for t in range(LT):
+            combine(0, 0, 2, t, 5 + t % 2)
+        turn_back(0, 7)
+        turn_back(1, 0)
+        for t in range(LT):
+            combine(1, 2, 1, t, 2 + t % 2)
+        turn_back(2, 1)
+        for t in range(LT):
+            combine(2, 3, 1, t, 2 + t % 2)
+        turn_back(3, 7)
+
+        codes = [tile([P, n * P], U32, "codes%d" % i) for i, n in enumerate((2, 1, 1))]
+        planes = [tile([P, n * P], U8, "planes%d" % i) for i, n in enumerate((2, 1, 1))]
+        for g in range(3):
+            nc.vector.quantize_mx(out=codes[g][:].bitcast(FP8X4), scales=planes[g][:], in_=grouped[g][:])
+
+        def merge(acc, half, nh, o):
+            g, j = place[2 * o + half]
+            cols = slice(nh * P, (nh + 1) * P)
+            zc = slice(j * P, (j + 1) * P)
+            nc.tensor.matmul_mx(
+                out=acc,
+                lhsT=mw[:, o, cols].bitcast(FP8X4),
+                lhsT_scale=ms[4 * o : P, cols],
+                rhs=codes[g][:, zc].bitcast(FP8X4),
+                rhs_scale=planes[g][:, zc],
+                start=(o == 0),
+                stop=(o == D - 1),
+            )
+
+        out_v = out.rearrange("(nh p) t -> p nh t", p=P)
+        late = [bank([P, P], 5 + nh, "late%d" % nh) for nh in range(2)]
+        for nh in range(2):
+            merge(late[nh][:], 1, nh, 0)
+        early = bank([P, 2, P], 4, "early")
+        for nh in range(2):
+            for o in range(D):
+                merge(early[:, nh, :], 0, nh, o)
+        for nh in range(2):
+            merge(late[nh][:], 1, nh, 1)
+        res0 = tile([P, 2, P], F32, "res0")
+        res1 = tile([P, 2, P], F32, "res1")
+        nc.vector.tensor_copy(res1[:, 0, :], late[0][:])
+        nc.scalar.copy(res1[:, 1, :], late[1][:])
+        nc.sync.dma_start(out_v[:, :, P : 2 * P], res1[:])
+        nc.scalar.copy(res0[:], early[:])
+        nc.sync.dma_start(out_v[:, :, 0:P], res0[:])

@@ -29,8 +29,8 @@ def tile_moe_mhm_none_kernel(
         sb = ctx.enter_context(tc.tile_pool(name="sb", bufs=1))
         ps = ctx.enter_context(tc.psum_pool(name="ps", bufs=1))
 
-        def tile(shape, dtype, name):
-            return sb.tile(shape, dtype, name=name, align_bytes=64)
+        def tile(shape, dtype, name, tag=None):
+            return sb.tile(shape, dtype, name=name, tag=tag or name, align_bytes=64)
 
         def bank(shape, b, name):
             return ps.tile(shape, F32, name=name, tag="bank%d" % b)
@@ -39,7 +39,7 @@ def tile_moe_mhm_none_kernel(
         pos_sb = [tile([P, Z // 16], U16, "pos%d_sb" % r) for r in range(2)]
         xw = tile([P, Z], I32, "xw")
         xs = tile([P, Z], U8, "xs")
-        ww = [tile([P, 2, H], I32, "ww%d" % i) for i in range(E // 2)]
+        ww = tile([P, E, H], I32, "ww")
         ws = tile([P, H], U8, "ws")
         mw = tile([P, D, N], I32, "mw")
         ms = tile([P, N], U8, "ms")
@@ -49,50 +49,51 @@ def tile_moe_mhm_none_kernel(
         nc.vector.memset(xs[:].bitcast(I32), 0)
         nc.vector.memset(ws[:].bitcast(I32), 0)
         nc.vector.memset(ms[:].bitcast(I32), 0)
-
+        make_identity(nc, ident[:])
         nc.sync.dma_start(offs_sb[:], offs)
         nc.sync.dma_start(
             xw[:].rearrange("p (o t) -> p o t", o=D),
             x_words.rearrange("o p t d -> p o (t d)").bitcast(I32),
         )
+        nc.sync.dma_start(pos_sb[0][:], pos1)
         for q in range(4):
-            nc.scalar.dma_start(
+            nc.sync.dma_start(
                 xs[32 * q : 32 * q + 4, :].bitcast(I32).rearrange("r (o t) -> r o t", o=D),
                 x_scales[:, 4 * q : 4 * q + 4, :].bitcast(I32).rearrange("o r t -> r o t"),
             )
+        nc.sync.dma_start(ww[:], w_words[:, 0].rearrange("e p l d -> p e (l d)").bitcast(I32))
         for q in range(4):
-            nc.scalar.dma_start(
+            nc.sync.dma_start(
                 ws[32 * q : 32 * q + 4 * E, :].bitcast(I32),
                 w_scales[:, 0, 4 * q : 4 * q + 4, :].bitcast(I32),
             )
-        for i in range(E // 2):
-            nc.sync.dma_start(ww[i][:], w_words[2 * i : 2 * i + 2, 0].rearrange("e p l d -> p e (l d)").bitcast(I32))
-        nc.sync.dma_start(pos_sb[0][:], pos1)
         nc.sync.dma_start(pos_sb[1][:], pos2)
         nc.sync.dma_start(gate_sb[:], gate.rearrange("r p z -> p r z"))
         nc.sync.dma_start(mw[:], wm_words.rearrange("o p n d -> p o (n d)").bitcast(I32))
         for q in range(4):
-            nc.scalar.dma_start(
+            nc.sync.dma_start(
                 ms[32 * q : 32 * q + 4 * D, :].bitcast(I32),
                 wm_scales[:, 4 * q : 4 * q + 4, :].bitcast(I32),
             )
-        make_identity(nc, ident[:])
 
         xg = [tile([P, C], U32, "xg%d" % e) for e in range(E)]
         sg = [tile([P, C], U8, "sg%d" % e) for e in range(E)]
+
+        def slots(e):
+            return offs_sb[:, e * C // 16 : (e + 1) * C // 16]
+
         for e in range(E):
-            lst = offs_sb[:, e * C // 16 : (e + 1) * C // 16]
-            nc.vector.tensor_copy(xg[e][:], xw[:].bitcast(U32).indirect(lst))
-            nc.vector.tensor_copy(sg[e][:], xs[:].indirect(lst))
+            nc.vector.tensor_copy(xg[e][:], xw[:].bitcast(U32).indirect(slots(e)))
+            nc.vector.tensor_copy(sg[e][:], xs[:].indirect(slots(e)))
 
         y = [tile([P, S], F32, "y%d" % t) for t in range(LT)]
-        order = [(0, 0), (1, 0), (0, 1), (2, 0), (1, 1), (3, 0), (2, 1), (3, 1)] + [(e, t) for t in range(2, LT) for e in range(E)]
+        order = [(0, 0), (1, 0), (0, 1), (2, 0), (3, 0), (1, 1), (2, 1), (3, 1)] + [(e, t) for t in range(2, LT) for e in range(E)]
         for i, (e, t) in enumerate(order):
             acc = bank([P, C], i % 5, "yacc%d" % i)
             cols = slice(t * P, (t + 1) * P)
             nc.tensor.matmul_mx(
                 out=acc[:],
-                lhsT=ww[e // 2][:, e % 2, cols].bitcast(FP8X4),
+                lhsT=ww[:, e, cols].bitcast(FP8X4),
                 lhsT_scale=ws[4 * e : P, cols],
                 rhs=xg[e][:].bitcast(FP8X4),
                 rhs_scale=sg[e][:],
@@ -103,22 +104,24 @@ def tile_moe_mhm_none_kernel(
 
         cT = [tile([P, n, 2, P, 2], BF16, "cT%d" % i) for i, n in enumerate((2, 1, 1))]
 
-        def combine(piece, s0, ns, t, b):
+        def combine(piece, s0, ns, ts, b):
             zs = slice(s0 * P, (s0 + ns) * P)
-            part = [tile([P, ns * P], F32, "part%d_%d_%d" % (piece, t, r)) for r in range(2)]
-            for r in range(2):
-                lst = pos_sb[r][:, s0 * P // 16 : (s0 + ns) * P // 16]
-                nc.vector.tensor_tensor(part[r][:], y[t][:].indirect(lst), gate_sb[:, r, zs], MULT)
-            turned = bank([P, ns, P], b, "turned%d_%d" % (piece, t))
-            for s in range(ns):
+            turned = bank([P, ns, len(ts), P], b, "turned%d_%d" % (piece, ts[0]))
+            for i, t in enumerate(ts):
+                part = [tile([P, ns * P], F32, "part%d_%d_%d" % (piece, t, r)) for r in range(2)]
                 for r in range(2):
-                    nc.tensor.matmul(
-                        turned[:, s, :], part[r][:, s * P : (s + 1) * P], ident[:],
-                        start=(r == 0), stop=(r == 1), is_transpose=True,
-                    )
+                    lst = pos_sb[r][:, s0 * P // 16 : (s0 + ns) * P // 16]
+                    nc.vector.tensor_tensor(part[r][:], y[t][:].indirect(lst), gate_sb[:, r, zs], MULT)
+                for s in range(ns):
+                    for r in range(2):
+                        nc.tensor.matmul(
+                            turned[:, s, i, :], part[r][:, s * P : (s + 1) * P], ident[:],
+                            start=(r == 0), stop=(r == 1), is_transpose=True,
+                        )
+            rows = slice(32 * ts[0], 32 * (ts[-1] + 1))
             nc.scalar.copy(
-                cT[piece][:, :, :, 32 * t : 32 * (t + 1), :].rearrange("z s u q k -> z u s q k"),
-                turned[:].rearrange("z s (q u k) -> z u s q k", u=2, k=2),
+                cT[piece][:, :, :, rows, :].rearrange("z s u q k -> z u s q k"),
+                turned[:].rearrange("z s t (q u k) -> z u s (t q) k", u=2, k=2),
             )
 
         grouped = [tile([P, n * H], BF16, "grouped%d" % i) for i, n in enumerate((2, 1, 1))]
@@ -137,49 +140,37 @@ def tile_moe_mhm_none_kernel(
             )
 
         for t in range(LT):
-            combine(0, 0, 2, t, 5 + t % 2)
+            combine(0, 0, 2, [t], 5 + t % 2)
         turn_back(0, 7)
         turn_back(1, 0)
-        for t in range(LT):
-            combine(1, 2, 1, t, 2 + t % 2)
+        combine(1, 2, 1, [0, 1, 2], 6)
+        combine(1, 2, 1, [3], 0)
         turn_back(2, 1)
-        for t in range(LT):
-            combine(2, 3, 1, t, 2 + t % 2)
+        combine(2, 3, 1, [0, 1, 2], 0)
+        combine(2, 3, 1, [3], 1)
         turn_back(3, 7)
 
-        codes = [tile([P, n * P], U32, "codes%d" % i) for i, n in enumerate((2, 1, 1))]
-        planes = [tile([P, n * P], U8, "planes%d" % i) for i, n in enumerate((2, 1, 1))]
-        for g in range(3):
-            nc.vector.quantize_mx(out=codes[g][:].bitcast(FP8X4), scales=planes[g][:], in_=grouped[g][:])
-
-        def merge(acc, half, nh, o):
-            g, j = place[2 * o + half]
-            cols = slice(nh * P, (nh + 1) * P)
+        codes = [tile([P, T], U32, "codes%d" % o) for o in range(D)]
+        planes = [tile([P, T], U8, "planes%d" % o) for o in range(D)]
+        nc.vector.quantize_mx(out=codes[0][:].bitcast(FP8X4), scales=planes[0][:], in_=grouped[0][:])
+        for j in range(2):
             zc = slice(j * P, (j + 1) * P)
-            nc.tensor.matmul_mx(
-                out=acc,
-                lhsT=mw[:, o, cols].bitcast(FP8X4),
-                lhsT_scale=ms[4 * o : P, cols],
-                rhs=codes[g][:, zc].bitcast(FP8X4),
-                rhs_scale=planes[g][:, zc],
-                start=(o == 0),
-                stop=(o == D - 1),
-            )
+            nc.vector.quantize_mx(out=codes[1][:, zc].bitcast(FP8X4), scales=planes[1][:, zc], in_=grouped[1 + j][:])
 
-        out_v = out.rearrange("(nh p) t -> p nh t", p=P)
-        late = [bank([P, P], 5 + nh, "late%d" % nh) for nh in range(2)]
-        for nh in range(2):
-            merge(late[nh][:], 1, nh, 0)
-        early = bank([P, 2, P], 4, "early")
-        for nh in range(2):
-            for o in range(D):
-                merge(early[:, nh, :], 0, nh, o)
-        for nh in range(2):
-            merge(late[nh][:], 1, nh, 1)
-        res0 = tile([P, 2, P], F32, "res0")
-        res1 = tile([P, 2, P], F32, "res1")
-        nc.vector.tensor_copy(res1[:, 0, :], late[0][:])
-        nc.scalar.copy(res1[:, 1, :], late[1][:])
-        nc.sync.dma_start(out_v[:, :, P : 2 * P], res1[:])
-        nc.scalar.copy(res0[:], early[:])
-        nc.sync.dma_start(out_v[:, :, 0:P], res0[:])
+        merged = [bank([P, T], (1, 0)[nh], "merged%d" % nh) for nh in range(2)]
+        for o in range(D):
+            for nh in range(2):
+                cols = slice(nh * P, (nh + 1) * P)
+                nc.tensor.matmul_mx(
+                    out=merged[nh][:],
+                    lhsT=mw[:, o, cols].bitcast(FP8X4),
+                    lhsT_scale=ms[4 * o : P, cols],
+                    rhs=codes[o][:].bitcast(FP8X4),
+                    rhs_scale=planes[o][:],
+                    start=(o == 0),
+                    stop=(o == D - 1),
+                )
+        res = tile([P, 2, T], F32, "res")
+        nc.vector.tensor_copy(res[:, 0, :], merged[0][:])
+        nc.scalar.copy(res[:, 1, :], merged[1][:])
+        nc.sync.dma_start(out.rearrange("(nh p) t -> p nh t", p=P), res[:])

@@ -1,7 +1,6 @@
 from contextlib import ExitStack
 
 import concourse.mybir as mybir
-from concourse.masks import make_identity
 
 F32 = mybir.dt.float32
 BF16 = mybir.dt.bfloat16
@@ -11,6 +10,7 @@ U16 = mybir.dt.uint16
 U8 = mybir.dt.uint8
 FP8X4 = mybir.dt.float8_e4m3fn_x4
 MULT = mybir.AluOpType.mult
+ADD = mybir.AluOpType.add
 
 P = 128
 D, T, E, C, H, N = 2, 256, 4, 256, 512, 256
@@ -44,28 +44,26 @@ def tile_moe_mhm_none_kernel(
         mw = tile([P, D, N], I32, "mw")
         ms = tile([P, N], U8, "ms")
         gate_sb = tile([P, 2, Z], F32, "gate_sb")
-        ident = tile([P, P], F32, "ident")
 
-        nc.vector.memset(xs[:].bitcast(I32), 0)
         nc.vector.memset(ws[:].bitcast(I32), 0)
+        nc.vector.memset(xs[:].bitcast(I32), 0)
         nc.vector.memset(ms[:].bitcast(I32), 0)
-        make_identity(nc, ident[:])
-        nc.sync.dma_start(offs_sb[:], offs)
         nc.sync.dma_start(
             xw[:].rearrange("p (o t) -> p o t", o=D),
             x_words.rearrange("o p t d -> p o (t d)").bitcast(I32),
         )
+        nc.sync.dma_start(offs_sb[:], offs)
         nc.sync.dma_start(pos_sb[0][:], pos1)
-        for q in range(4):
-            nc.sync.dma_start(
-                xs[32 * q : 32 * q + 4, :].bitcast(I32).rearrange("r (o t) -> r o t", o=D),
-                x_scales[:, 4 * q : 4 * q + 4, :].bitcast(I32).rearrange("o r t -> r o t"),
-            )
-        nc.sync.dma_start(ww[:], w_words[:, 0].rearrange("e p l d -> p e (l d)").bitcast(I32))
         for q in range(4):
             nc.sync.dma_start(
                 ws[32 * q : 32 * q + 4 * E, :].bitcast(I32),
                 w_scales[:, 0, 4 * q : 4 * q + 4, :].bitcast(I32),
+            )
+        nc.sync.dma_start(ww[:], w_words[:, 0].rearrange("e p l d -> p e (l d)").bitcast(I32))
+        for q in range(4):
+            nc.sync.dma_start(
+                xs[32 * q : 32 * q + 4, :].bitcast(I32).rearrange("r (o t) -> r o t", o=D),
+                x_scales[:, 4 * q : 4 * q + 4, :].bitcast(I32).rearrange("o r t -> r o t"),
             )
         nc.sync.dma_start(pos_sb[1][:], pos2)
         nc.sync.dma_start(gate_sb[:], gate.rearrange("r p z -> p r z"))
@@ -84,93 +82,100 @@ def tile_moe_mhm_none_kernel(
 
         for e in range(E):
             nc.vector.tensor_copy(xg[e][:], xw[:].bitcast(U32).indirect(slots(e)))
+        wsp = tile([P, 4, P], U8, "wsp")
+        nc.vector.tensor_copy(wsp[:], ws[:].rearrange("p (m d) -> p d m", d=4))
+        w4 = ww[:].rearrange("p e (m d) -> p d e m", d=4)
+        wp0 = tile([P, E, P], I32, "wp0")
+        nc.vector.tensor_copy(wp0[:], w4[:, 0])
+        for e in range(E):
             nc.vector.tensor_copy(sg[e][:], xs[:].indirect(slots(e)))
+        wp123 = tile([P, 3, E, P], I32, "wp123", "xs")
+        nc.vector.tensor_copy(
+            wp123[:].rearrange("p d e m -> p (e m) d"), ww[:].rearrange("p e (m d) -> p (e m) d", d=4)[:, :, 1:4]
+        )
 
-        y = [tile([P, S], F32, "y%d" % t) for t in range(LT)]
-        order = [(0, 0), (1, 0), (0, 1), (2, 0), (3, 0), (1, 1), (2, 1), (3, 1)] + [(e, t) for t in range(2, LT) for e in range(E)]
-        for i, (e, t) in enumerate(order):
+        y = [tile([P, S], F32, "y%d" % d) for d in range(4)]
+        for i in range(4 * E):
+            d, e = divmod(i, E)
             acc = bank([P, C], i % 5, "yacc%d" % i)
-            cols = slice(t * P, (t + 1) * P)
             nc.tensor.matmul_mx(
                 out=acc[:],
-                lhsT=ww[:, e, cols].bitcast(FP8X4),
-                lhsT_scale=ws[4 * e : P, cols],
+                lhsT=(wp0[:, e, :] if d == 0 else wp123[:, d - 1, e, :]).bitcast(FP8X4),
+                lhsT_scale=wsp[4 * e : P, d, :],
                 rhs=xg[e][:].bitcast(FP8X4),
                 rhs_scale=sg[e][:],
                 start=True,
                 stop=True,
             )
-            nc.scalar.copy(y[t][:, e * C : (e + 1) * C], acc[:])
+            nc.scalar.copy(y[d][:, e * C : (e + 1) * C], acc[:])
 
-        cT = [tile([P, n, 2, P, 2], BF16, "cT%d" % i) for i, n in enumerate((2, 1, 1))]
+        part = [[tile([P, 4, T], F32, "part%d_%d" % (o, r)) for r in range(2)] for o in range(D)]
+        grouped = [tile([P, T, 4], BF16, "grouped%d" % o) for o in range(D)]
 
-        def combine(piece, s0, ns, ts, b):
-            zs = slice(s0 * P, (s0 + ns) * P)
-            turned = bank([P, ns, len(ts), P], b, "turned%d_%d" % (piece, ts[0]))
-            for i, t in enumerate(ts):
-                part = [tile([P, ns * P], F32, "part%d_%d_%d" % (piece, t, r)) for r in range(2)]
-                for r in range(2):
-                    lst = pos_sb[r][:, s0 * P // 16 : (s0 + ns) * P // 16]
-                    nc.vector.tensor_tensor(part[r][:], y[t][:].indirect(lst), gate_sb[:, r, zs], MULT)
-                for s in range(ns):
-                    for r in range(2):
-                        nc.tensor.matmul(
-                            turned[:, s, i, :], part[r][:, s * P : (s + 1) * P], ident[:],
-                            start=(r == 0), stop=(r == 1), is_transpose=True,
-                        )
-            rows = slice(32 * ts[0], 32 * (ts[-1] + 1))
-            nc.scalar.copy(
-                cT[piece][:, :, :, rows, :].rearrange("z s u q k -> z u s q k"),
-                turned[:].rearrange("z s t (q u k) -> z u s (t q) k", u=2, k=2),
-            )
+        def fetch(o, d, r):
+            lst = pos_sb[r][:, o * T // 16 : (o + 1) * T // 16]
+            nc.vector.tensor_tensor(part[o][r][:, d, :], y[d][:].indirect(lst), gate_sb[:, r, o * T : (o + 1) * T], MULT)
 
-        grouped = [tile([P, n * H], BF16, "grouped%d" % i) for i, n in enumerate((2, 1, 1))]
-        place = [(0, 0), (0, 1), (1, 0), (2, 0)]
-
-        def turn_back(s, b):
-            piece, i = place[s]
-            words = cT[piece][:, i].rearrange("z u p k -> z (u p k)").bitcast(F32)
-            back = bank([P, 2, P], b, "back%d" % s)
-            for u in range(2):
-                nc.tensor.transpose(back[:, u, :], words[:, u * P : (u + 1) * P], ident[:])
-            g, j = place[s]
-            nc.scalar.copy(
-                grouped[g][:, j * H : (j + 1) * H].bitcast(F32).rearrange("p (z u) -> p z u", u=2),
-                back[:].rearrange("p u z -> p z u"),
-            )
-
-        for t in range(LT):
-            combine(0, 0, 2, [t], 5 + t % 2)
-        turn_back(0, 7)
-        turn_back(1, 0)
-        combine(1, 2, 1, [0, 1, 2], 6)
-        combine(1, 2, 1, [3], 0)
-        turn_back(2, 1)
-        combine(2, 3, 1, [0, 1, 2], 0)
-        combine(2, 3, 1, [3], 1)
-        turn_back(3, 7)
+        summed = tile([P, 4, T], BF16, "summed")
+        steps = [(0, 0), (1, 0), (0, 1), (0, 2), (1, 1), (0, 3), (1, 2), (1, 3)]
+        for i, (o, d) in enumerate(steps):
+            fetch(o, d, 0)
+            if i > 0 and steps[i - 1][0] == 0:
+                done = steps[i - 1][1]
+                nc.vector.tensor_tensor(summed[:, done, :], part[0][0][:, done, :], part[0][1][:, done, :], ADD)
+            fetch(o, d, 1)
+        nc.scalar.copy(grouped[0][:], summed[:].rearrange("p d z -> p z d"))
 
         codes = [tile([P, T], U32, "codes%d" % o) for o in range(D)]
         planes = [tile([P, T], U8, "planes%d" % o) for o in range(D)]
-        nc.vector.quantize_mx(out=codes[0][:].bitcast(FP8X4), scales=planes[0][:], in_=grouped[0][:])
-        for j in range(2):
-            zc = slice(j * P, (j + 1) * P)
-            nc.vector.quantize_mx(out=codes[1][:, zc].bitcast(FP8X4), scales=planes[1][:, zc], in_=grouped[1 + j][:])
+        flat = [grouped[o][:].rearrange("p z d -> p (z d)") for o in range(D)]
 
-        merged = [bank([P, T], (1, 0)[nh], "merged%d" % nh) for nh in range(2)]
-        for o in range(D):
+        def quantise(o, half):
+            zc = slice(half * P, (half + 1) * P)
+            nc.vector.quantize_mx(
+                out=codes[o][:, zc].bitcast(FP8X4), scales=planes[o][:, zc], in_=flat[o][:, half * H : (half + 1) * H]
+            )
+
+        def add_second_head(half):
+            zc = slice(half * P, (half + 1) * P)
+            nc.vector.tensor_tensor(
+                grouped[1][:, zc, :],
+                part[1][0][:, :, zc].rearrange("p d z -> p z d"),
+                part[1][1][:, :, zc].rearrange("p d z -> p z d"),
+                ADD,
+            )
+
+        merged = [[bank([P, P], 2 * half + nh, "merged%d_%d" % (half, nh)) for nh in range(2)] for half in range(2)]
+
+        def merge(o, half):
+            zc = slice(half * P, (half + 1) * P)
             for nh in range(2):
                 cols = slice(nh * P, (nh + 1) * P)
                 nc.tensor.matmul_mx(
-                    out=merged[nh][:],
+                    out=merged[half][nh][:],
                     lhsT=mw[:, o, cols].bitcast(FP8X4),
                     lhsT_scale=ms[4 * o : P, cols],
-                    rhs=codes[o][:].bitcast(FP8X4),
-                    rhs_scale=planes[o][:],
+                    rhs=codes[o][:, zc].bitcast(FP8X4),
+                    rhs_scale=planes[o][:, zc],
                     start=(o == 0),
                     stop=(o == D - 1),
                 )
-        res = tile([P, 2, T], F32, "res")
-        nc.vector.tensor_copy(res[:, 0, :], merged[0][:])
-        nc.scalar.copy(res[:, 1, :], merged[1][:])
-        nc.sync.dma_start(out.rearrange("(nh p) t -> p nh t", p=P), res[:])
+
+        quantise(0, 0)
+        merge(0, 0)
+        add_second_head(0)
+        quantise(0, 1)
+        merge(0, 1)
+        quantise(1, 0)
+        merge(1, 0)
+        add_second_head(1)
+        quantise(1, 1)
+        merge(1, 1)
+        out_v = out.rearrange("(nh p) t -> p nh t", p=P)
+        res = [tile([P, 2, P], F32, "res%d" % half) for half in range(2)]
+        nc.scalar.copy(res[0][:, 0, :], merged[0][0][:])
+        nc.scalar.copy(res[0][:, 1, :], merged[0][1][:])
+        nc.sync.dma_start(out_v[:, :, 0:P], res[0][:])
+        nc.scalar.copy(res[1][:, 0, :], merged[1][0][:])
+        nc.vector.tensor_copy(res[1][:, 1, :], merged[1][1][:])
+        nc.sync.dma_start(out_v[:, :, P:T], res[1][:])

@@ -83,10 +83,10 @@ def tile_moe_mhm_none_kernel(
         for e in range(E):
             nc.vector.tensor_copy(xg[e][:], xw[:].bitcast(U32).indirect(slots(e)))
         wsp = tile([P, 4, P], U8, "wsp")
-        nc.vector.tensor_copy(wsp[:], ws[:].rearrange("p (m d) -> p d m", d=4))
+        nc.gpsimd.tensor_copy(wsp[:], ws[:].rearrange("p (m d) -> p d m", d=4))
         w4 = ww[:].rearrange("p e (m d) -> p d e m", d=4)
         wp0 = tile([P, E, P], I32, "wp0")
-        nc.vector.tensor_copy(wp0[:], w4[:, 0])
+        nc.gpsimd.tensor_copy(wp0[:], w4[:, 0])
         for e in range(E):
             nc.vector.tensor_copy(sg[e][:], xs[:].indirect(slots(e)))
         wp123 = tile([P, 3, E, P], I32, "wp123", "xs")
@@ -177,5 +177,6 @@ def tile_moe_mhm_none_kernel(
         nc.scalar.copy(res[0][:, 1, :], merged[0][1][:])
         nc.sync.dma_start(out_v[:, :, 0:P], res[0][:])
         nc.scalar.copy(res[1][:, 0, :], merged[1][0][:])
+        nc.sync.dma_start(out_v[:, 0, P:T], res[1][:, 0, :])
         nc.vector.tensor_copy(res[1][:, 1, :], merged[1][1][:])
-        nc.sync.dma_start(out_v[:, :, P:T], res[1][:])
+        nc.sync.dma_start(out_v[:, 1, P:T], res[1][:, 1, :])

@@ -1,6 +1,7 @@
 from contextlib import ExitStack
 
 import concourse.mybir as mybir
+from concourse.masks import make_identity
 
 F32 = mybir.dt.float32
 BF16 = mybir.dt.bfloat16
@@ -18,6 +19,8 @@ Z = D * T
 S = E * C
 LT = H // P
 ZT = Z // P
+XW = 704
+XS = Z
 FLOPS = 2 * H * H * S + 2 * D * H * N * T
 
 
@@ -37,34 +40,38 @@ def tile_moe_mhm_none_kernel(
 
         offs_sb = tile([P, S // 16], U16, "offs_sb")
         pos_sb = [tile([P, Z // 16], U16, "pos%d_sb" % r) for r in range(2)]
-        xw = tile([P, Z], I32, "xw")
-        xs = tile([P, Z], U8, "xs")
-        ww = tile([P, E, H], I32, "ww")
+        xw = tile([P, XW], I32, "xw")
+        xs = tile([P, XS], U8, "xs")
+        ww = tile([P, E * H], I32, "ww")
+        ww_half = [ww[:, 2 * g * H : 2 * (g + 1) * H] for g in range(2)]
         ws = tile([P, H], U8, "ws")
         mw = tile([P, D, N], I32, "mw")
         ms = tile([P, N], U8, "ms")
         gate_sb = tile([P, 2, Z], F32, "gate_sb")
 
-        nc.vector.memset(ws[:].bitcast(I32), 0)
         nc.vector.memset(xs[:].bitcast(I32), 0)
+        nc.gpsimd.memset(ws[:].bitcast(I32), 0)
+        nc.vector.memset(xw[:, Z:XW], 0)
         nc.vector.memset(ms[:].bitcast(I32), 0)
         nc.sync.dma_start(
-            xw[:].rearrange("p (o t) -> p o t", o=D),
+            xw[:, 0:Z].rearrange("p (o t) -> p o t", o=D),
             x_words.rearrange("o p t d -> p o (t d)").bitcast(I32),
         )
         nc.sync.dma_start(offs_sb[:], offs)
         nc.sync.dma_start(pos_sb[0][:], pos1)
         for q in range(4):
             nc.sync.dma_start(
+                xs[32 * q : 32 * q + 4, 0:Z].bitcast(I32).rearrange("r (o t) -> r o t", o=D),
+                x_scales[:, 4 * q : 4 * q + 4, :].bitcast(I32).rearrange("o r t -> r o t"),
+            )
+        w_rows = w_words[:, 0].rearrange("e p l d -> p e (l d)").bitcast(I32)
+        nc.sync.dma_start(ww_half[0].rearrange("p (e l) -> p e l", e=2), w_rows[:, 0:2, :])
+        for q in range(4):
+            nc.sync.dma_start(
                 ws[32 * q : 32 * q + 4 * E, :].bitcast(I32),
                 w_scales[:, 0, 4 * q : 4 * q + 4, :].bitcast(I32),
             )
-        nc.sync.dma_start(ww[:], w_words[:, 0].rearrange("e p l d -> p e (l d)").bitcast(I32))
-        for q in range(4):
-            nc.sync.dma_start(
-                xs[32 * q : 32 * q + 4, :].bitcast(I32).rearrange("r (o t) -> r o t", o=D),
-                x_scales[:, 4 * q : 4 * q + 4, :].bitcast(I32).rearrange("o r t -> r o t"),
-            )
+        nc.sync.dma_start(ww_half[1].rearrange("p (e l) -> p e l", e=2), w_rows[:, 2:4, :])
         nc.sync.dma_start(pos_sb[1][:], pos2)
         nc.sync.dma_start(gate_sb[:], gate.rearrange("r p z -> p r z"))
         nc.sync.dma_start(mw[:], wm_words.rearrange("o p n d -> p o (n d)").bitcast(I32))
@@ -74,24 +81,36 @@ def tile_moe_mhm_none_kernel(
                 wm_scales[:, 4 * q : 4 * q + 4, :].bitcast(I32),
             )
 
-        xg = [tile([P, C], U32, "xg%d" % e) for e in range(E)]
-        sg = [tile([P, C], U8, "sg%d" % e) for e in range(E)]
+        ident = tile([P, P], F32, "ident")
+        make_identity(nc, ident[:])
 
-        def slots(e):
-            return offs_sb[:, e * C // 16 : (e + 1) * C // 16]
+        xg = tile([P, S], U32, "xg")
+        sg = tile([P, S], U8, "sg")
 
+        def gather_words(s0, s1):
+            nc.vector.tensor_copy(xg[:, s0:s1], xw[:].bitcast(U32).indirect(offs_sb[:, s0 // 16 : s1 // 16]))
+
+        def gather_scales(s0, s1):
+            nc.vector.tensor_copy(sg[:, s0:s1], xs[:].indirect(offs_sb[:, s0 // 16 : s1 // 16]))
+
+        gather_words(0, 2 * C)
+        gather_words(2 * C, S)
         for e in range(E):
-            nc.vector.tensor_copy(xg[e][:], xw[:].bitcast(U32).indirect(slots(e)))
+            gather_scales(e * C, (e + 1) * C)
+        wp0 = [tile([P, 2 * P], I32, "wp0_%d" % g) for g in range(2)]
         wsp = tile([P, 4, P], U8, "wsp")
-        nc.gpsimd.tensor_copy(wsp[:], ws[:].rearrange("p (m d) -> p d m", d=4))
-        w4 = ww[:].rearrange("p e (m d) -> p d e m", d=4)
-        wp0 = tile([P, E, P], I32, "wp0")
-        nc.gpsimd.tensor_copy(wp0[:], w4[:, 0])
-        for e in range(E):
-            nc.vector.tensor_copy(sg[e][:], xs[:].indirect(slots(e)))
-        wp123 = tile([P, 3, E, P], I32, "wp123", "xs")
+        ws4 = ws[:].rearrange("p (m d) -> p d m", d=4)
+
+        def first_lane(g):
+            nc.gpsimd.tensor_copy(wp0[g][:], ww_half[g].rearrange("p (c d) -> p d c", d=4)[:, 0, :])
+
+        first_lane(0)
+        nc.gpsimd.tensor_copy(wsp[:, 0, :], ws4[:, 0, :])
+        first_lane(1)
+        nc.gpsimd.tensor_copy(wsp[:, 1:4, :], ws4[:, 1:4, :])
+        wp123 = tile([P, 3, E * P], I32, "wp123", "xs")
         nc.vector.tensor_copy(
-            wp123[:].rearrange("p d e m -> p (e m) d"), ww[:].rearrange("p e (m d) -> p (e m) d", d=4)[:, :, 1:4]
+            wp123[:].rearrange("p d c -> p c d"), ww[:].rearrange("p (c d) -> p c d", d=4)[:, :, 1:4]
         )
 
         y = [tile([P, S], F32, "y%d" % d) for d in range(4)]
@@ -100,77 +119,96 @@ def tile_moe_mhm_none_kernel(
             acc = bank([P, C], i % 5, "yacc%d" % i)
             nc.tensor.matmul_mx(
                 out=acc[:],
-                lhsT=(wp0[:, e, :] if d == 0 else wp123[:, d - 1, e, :]).bitcast(FP8X4),
+                lhsT=(wp0[e // 2][:, (e % 2) * P : (e % 2 + 1) * P] if d == 0 else wp123[:, d - 1, e * P : (e + 1) * P]).bitcast(FP8X4),
                 lhsT_scale=wsp[4 * e : P, d, :],
-                rhs=xg[e][:].bitcast(FP8X4),
-                rhs_scale=sg[e][:],
+                rhs=xg[:, e * C : (e + 1) * C].bitcast(FP8X4),
+                rhs_scale=sg[:, e * C : (e + 1) * C],
                 start=True,
                 stop=True,
             )
             nc.scalar.copy(y[d][:, e * C : (e + 1) * C], acc[:])
 
-        part = [[tile([P, 4, T], F32, "part%d_%d" % (o, r)) for r in range(2)] for o in range(D)]
-        grouped = [tile([P, T, 4], BF16, "grouped%d" % o) for o in range(D)]
+        NB = 3
+        W = NB * P
+        part = [[tile([P, W], F32, "part%d_%d" % (d, r)) for r in range(2)] for d in range(4)]
+        turned = [bank([P, 4, P], 5 + b, "turned%d" % b) for b in range(NB)]
+        pairs = [[tile([P, P, 2], BF16, "pairs%d_%d" % (b, u)) for u in range(2)] for b in range(NB)]
+        grouped = tile([P, NB * H], BF16, "grouped")
 
-        def fetch(o, d, r):
-            lst = pos_sb[r][:, o * T // 16 : (o + 1) * T // 16]
-            nc.vector.tensor_tensor(part[o][r][:, d, :], y[d][:].indirect(lst), gate_sb[:, r, o * T : (o + 1) * T], MULT)
+        def fetch(dst, d, r, z0, z1):
+            nc.vector.tensor_tensor(dst, y[d][:].indirect(pos_sb[r][:, z0 // 16 : z1 // 16]), gate_sb[:, r, z0:z1], MULT)
 
-        summed = tile([P, 4, T], BF16, "summed")
-        steps = [(0, 0), (1, 0), (0, 1), (0, 2), (1, 1), (0, 3), (1, 2), (1, 3)]
-        for i, (o, d) in enumerate(steps):
-            fetch(o, d, 0)
-            if i > 0 and steps[i - 1][0] == 0:
-                done = steps[i - 1][1]
-                nc.vector.tensor_tensor(summed[:, done, :], part[0][0][:, done, :], part[0][1][:, done, :], ADD)
-            fetch(o, d, 1)
-        nc.scalar.copy(grouped[0][:], summed[:].rearrange("p d z -> p z d"))
+        def fetch_and_turn(d, b0, b1):
+            for r in range(2):
+                fetch(part[d][r][:, b0 * P : b1 * P], d, r, b0 * P, b1 * P)
+                for b in range(b0, b1):
+                    nc.tensor.matmul(
+                        turned[b][:, d, :],
+                        lhsT=part[d][r][:, b * P : (b + 1) * P],
+                        rhs=ident[:],
+                        is_transpose=True,
+                        start=(r == 0),
+                        stop=(r == 1),
+                    )
 
-        codes = [tile([P, T], U32, "codes%d" % o) for o in range(D)]
-        planes = [tile([P, T], U8, "planes%d" % o) for o in range(D)]
-        flat = [grouped[o][:].rearrange("p z d -> p (z d)") for o in range(D)]
+        def turn_back(b, u):
+            nc.scalar.copy(pairs[b][u][:], turned[b][:, 2 * u : 2 * u + 2, :].rearrange("z e p -> z p e"))
+            nc.tensor.transpose(turned[b][:, u, :], pairs[b][u][:].rearrange("z p e -> z (p e)").bitcast(F32), ident[:])
 
-        def quantise(o, half):
-            zc = slice(half * P, (half + 1) * P)
-            nc.vector.quantize_mx(
-                out=codes[o][:, zc].bitcast(FP8X4), scales=planes[o][:, zc], in_=flat[o][:, half * H : (half + 1) * H]
+        def regroup(b):
+            nc.scalar.copy(
+                grouped[:, b * H : (b + 1) * H].bitcast(F32).rearrange("p (z u) -> p z u", u=2), turned[b][:, 0:2, :].rearrange("p u z -> p z u")
             )
 
-        def add_second_head(half):
-            zc = slice(half * P, (half + 1) * P)
-            nc.vector.tensor_tensor(
-                grouped[1][:, zc, :],
-                part[1][0][:, :, zc].rearrange("p d z -> p z d"),
-                part[1][1][:, :, zc].rearrange("p d z -> p z d"),
-                ADD,
-            )
+        codes = tile([P, Z], U32, "codes")
+        planes = tile([P, Z], U8, "planes")
+
+        def quantise(b0, b1, values):
+            zc = slice(b0 * P, b1 * P)
+            nc.vector.quantize_mx(out=codes[:, zc].bitcast(FP8X4), scales=planes[:, zc], in_=values)
 
         merged = [[bank([P, P], 2 * half + nh, "merged%d_%d" % (half, nh)) for nh in range(2)] for half in range(2)]
 
-        def merge(o, half):
-            zc = slice(half * P, (half + 1) * P)
+        def merge(b):
+            o, half = divmod(b, 2)
             for nh in range(2):
                 cols = slice(nh * P, (nh + 1) * P)
                 nc.tensor.matmul_mx(
                     out=merged[half][nh][:],
                     lhsT=mw[:, o, cols].bitcast(FP8X4),
                     lhsT_scale=ms[4 * o : P, cols],
-                    rhs=codes[o][:, zc].bitcast(FP8X4),
-                    rhs_scale=planes[o][:, zc],
+                    rhs=codes[:, b * P : (b + 1) * P].bitcast(FP8X4),
+                    rhs_scale=planes[:, b * P : (b + 1) * P],
                     start=(o == 0),
                     stop=(o == D - 1),
                 )
 
-        quantise(0, 0)
-        merge(0, 0)
-        add_second_head(0)
-        quantise(0, 1)
-        merge(0, 1)
-        quantise(1, 0)
-        merge(1, 0)
-        add_second_head(1)
-        quantise(1, 1)
-        merge(1, 1)
+        for d in range(4):
+            fetch_and_turn(d, 0, NB)
+            if d % 2 == 1:
+                for b in range(NB):
+                    turn_back(b, d // 2)
+        for b in range(NB):
+            regroup(b)
+
+        last = [tile([P, 4, P], F32, "last%d" % r, "part1_%d" % r) for r in range(2)]
+        for d in range(4):
+            for r in range(2):
+                fetch(last[r][:, d, :], d, r, W, Z)
+        quantise(0, 2, grouped[:, 0 : 2 * H])
+        merge(0)
+        merge(1)
+        quantise(2, 3, grouped[:, 2 * H : 3 * H])
+        merge(2)
+        grouped3 = tile([P, H], BF16, "grouped3", "grouped")
+        nc.vector.tensor_tensor(
+            grouped3[:].rearrange("p (c i d) -> p c d i", i=4, d=4),
+            last[0][:].rearrange("p d (c i) -> p c d i", i=4),
+            last[1][:].rearrange("p d (c i) -> p c d i", i=4),
+            ADD,
+        )
+        quantise(3, 4, grouped3[:])
+        merge(3)
         out_v = out.rearrange("(nh p) t -> p nh t", p=P)
         res = [tile([P, 2, P], F32, "res%d" % half) for half in range(2)]
         nc.scalar.copy(res[0][:, 0, :], merged[0][0][:])

@@ -43,7 +43,8 @@ def tile_moe_mhm_none_kernel(
         xw = tile([P, XW], I32, "xw")
         xs = tile([P, XS], U8, "xs")
         ww = tile([P, E * H], I32, "ww")
-        ww_half = [ww[:, 2 * g * H : 2 * (g + 1) * H] for g in range(2)]
+        groups = ((0, E - 1), (E - 1, E))
+        ww_part = [ww[:, e0 * H : e1 * H] for e0, e1 in groups]
         ws = tile([P, H], U8, "ws")
         mw = tile([P, D, N], I32, "mw")
         ms = tile([P, N], U8, "ms")
@@ -65,13 +66,13 @@ def tile_moe_mhm_none_kernel(
                 x_scales[:, 4 * q : 4 * q + 4, :].bitcast(I32).rearrange("o r t -> r o t"),
             )
         w_rows = w_words[:, 0].rearrange("e p l d -> p e (l d)").bitcast(I32)
-        nc.sync.dma_start(ww_half[0].rearrange("p (e l) -> p e l", e=2), w_rows[:, 0:2, :])
+        nc.sync.dma_start(ww_part[0].rearrange("p (e l) -> p e l", l=H), w_rows[:, 0 : E - 1, :])
         for q in range(4):
             nc.sync.dma_start(
                 ws[32 * q : 32 * q + 4 * E, :].bitcast(I32),
                 w_scales[:, 0, 4 * q : 4 * q + 4, :].bitcast(I32),
             )
-        nc.sync.dma_start(ww_half[1].rearrange("p (e l) -> p e l", e=2), w_rows[:, 2:4, :])
+        nc.sync.dma_start(ww_part[1], w_rows[:, E - 1, :])
         nc.sync.dma_start(pos_sb[1][:], pos2)
         nc.sync.dma_start(gate_sb[:], gate.rearrange("r p z -> p r z"))
         nc.sync.dma_start(mw[:], wm_words.rearrange("o p n d -> p o (n d)").bitcast(I32))
@@ -95,38 +96,54 @@ def tile_moe_mhm_none_kernel(
 
         gather_words(0, 2 * C)
         gather_words(2 * C, S)
-        for e in range(E):
-            gather_scales(e * C, (e + 1) * C)
-        wp0 = [tile([P, 2 * P], I32, "wp0_%d" % g) for g in range(2)]
+        pieces = [(0, C), (C, 2 * C), (2 * C, 3 * C), (3 * C, 3 * C + P), (3 * C + P, S)]
+        for s0, s1 in pieces:
+            gather_scales(s0, s1)
+        wp0 = tile([P, E * P], I32, "wp0")
         wsp = tile([P, 4, P], U8, "wsp")
         ws4 = ws[:].rearrange("p (m d) -> p d m", d=4)
 
         def first_lane(g):
-            nc.gpsimd.tensor_copy(wp0[g][:], ww_half[g].rearrange("p (c d) -> p d c", d=4)[:, 0, :])
+            nc.gpsimd.tensor_copy(wp0[:, groups[g][0] * P : groups[g][1] * P], ww_part[g].rearrange("p (c d) -> p d c", d=4)[:, 0, :])
 
         first_lane(0)
         nc.gpsimd.tensor_copy(wsp[:, 0, :], ws4[:, 0, :])
         first_lane(1)
         nc.gpsimd.tensor_copy(wsp[:, 1:4, :], ws4[:, 1:4, :])
         wp123 = tile([P, 3, E * P], I32, "wp123", "xs")
-        nc.vector.tensor_copy(
-            wp123[:].rearrange("p d c -> p c d"), ww[:].rearrange("p (c d) -> p c d", d=4)[:, :, 1:4]
-        )
+        for c0 in (0, 2 * P):
+            nc.vector.tensor_copy(
+                wp123[:, :, c0 : c0 + 2 * P].rearrange("p d c -> p c d"),
+                ww[:].rearrange("p (c d) -> p c d", d=4)[:, c0 : c0 + 2 * P, 1:4],
+            )
 
-        y = [tile([P, S], F32, "y%d" % d) for d in range(4)]
-        for i in range(4 * E):
-            d, e = divmod(i, E)
-            acc = bank([P, C], i % 5, "yacc%d" % i)
+        for i in range(2):
+            idle = bank([P, H], 5 + i, "idle%d" % i)
             nc.tensor.matmul_mx(
-                out=acc[:],
-                lhsT=(wp0[e // 2][:, (e % 2) * P : (e % 2 + 1) * P] if d == 0 else wp123[:, d - 1, e * P : (e + 1) * P]).bitcast(FP8X4),
-                lhsT_scale=wsp[4 * e : P, d, :],
-                rhs=xg[:, e * C : (e + 1) * C].bitcast(FP8X4),
-                rhs_scale=sg[:, e * C : (e + 1) * C],
+                out=idle[:],
+                lhsT=ww[:, 0:P].bitcast(FP8X4),
+                lhsT_scale=ws[:, 0:P],
+                rhs=ww[:, 0:H].bitcast(FP8X4),
+                rhs_scale=ws[:],
                 start=True,
                 stop=True,
             )
-            nc.scalar.copy(y[d][:, e * C : (e + 1) * C], acc[:])
+
+        y = [tile([P, S], F32, "y%d" % d) for d in range(4)]
+        steps = [(0, s0, s1) for s0, s1 in pieces] + [(d, e * C, (e + 1) * C) for d in range(1, 4) for e in range(E)]
+        for i, (d, s0, s1) in enumerate(steps):
+            cols = slice(s0 // C * P, (s0 // C + 1) * P)
+            acc = bank([P, s1 - s0], i % 5, "yacc%d" % i)
+            nc.tensor.matmul_mx(
+                out=acc[:],
+                lhsT=(wp0[:, cols] if d == 0 else wp123[:, d - 1, cols]).bitcast(FP8X4),
+                lhsT_scale=wsp[4 * (s0 // C) : P, d, :],
+                rhs=xg[:, s0:s1].bitcast(FP8X4),
+                rhs_scale=sg[:, s0:s1],
+                start=True,
+                stop=True,
+            )
+            nc.scalar.copy(y[d][:, s0:s1], acc[:])
 
         NB = 3
         W = NB * P
@@ -183,13 +200,17 @@ def tile_moe_mhm_none_kernel(
                     stop=(o == D - 1),
                 )
 
-        for d in range(4):
-            fetch_and_turn(d, 0, NB)
-            if d % 2 == 1:
-                for b in range(NB):
-                    turn_back(b, d // 2)
+        fetch_and_turn(0, 0, NB)
+        fetch_and_turn(1, 0, NB)
         for b in range(NB):
-            regroup(b)
+            turn_back(b, 0)
+        fetch_and_turn(2, 0, NB)
+        for b0, b1 in ((0, NB - 1), (NB - 1, NB)):
+            fetch_and_turn(3, b0, b1)
+            for b in range(b0, b1):
+                turn_back(b, 1)
+            for b in range(b0, b1):
+                regroup(b)
 
         last = [tile([P, 4, P], F32, "last%d" % r, "part1_%d" % r) for r in range(2)]
         for d in range(4):
@@ -201,13 +222,19 @@ def tile_moe_mhm_none_kernel(
         quantise(2, 3, grouped[:, 2 * H : 3 * H])
         merge(2)
         grouped3 = tile([P, H], BF16, "grouped3", "grouped")
-        nc.vector.tensor_tensor(
-            grouped3[:].rearrange("p (c i d) -> p c d i", i=4, d=4),
-            last[0][:].rearrange("p d (c i) -> p c d i", i=4),
-            last[1][:].rearrange("p d (c i) -> p c d i", i=4),
-            ADD,
-        )
-        quantise(3, 4, grouped3[:])
+        for z0 in (0, P // 2):
+            zc = slice(z0, z0 + P // 2)
+            nc.vector.tensor_tensor(
+                grouped3[:, 4 * z0 : 4 * z0 + H // 2].rearrange("p (c i d) -> p c d i", i=4, d=4),
+                last[0][:, :, zc].rearrange("p d (c i) -> p c d i", i=4),
+                last[1][:, :, zc].rearrange("p d (c i) -> p c d i", i=4),
+                ADD,
+            )
+        for z0 in (0, P // 2):
+            zc = slice(W + z0, W + z0 + P // 2)
+            nc.vector.quantize_mx(
+                out=codes[:, zc].bitcast(FP8X4), scales=planes[:, zc], in_=grouped3[:, 4 * z0 : 4 * z0 + H // 2]
+            )
         merge(3)
         out_v = out.rearrange("(nh p) t -> p nh t", p=P)
         res = [tile([P, 2, P], F32, "res%d" % half) for half in range(2)]
@@ -215,6 +242,6 @@ def tile_moe_mhm_none_kernel(
         nc.scalar.copy(res[0][:, 1, :], merged[0][1][:])
         nc.sync.dma_start(out_v[:, :, 0:P], res[0][:])
         nc.scalar.copy(res[1][:, 0, :], merged[1][0][:])
-        nc.sync.dma_start(out_v[:, 0, P:T], res[1][:, 0, :])
+        nc.scalar.dma_start(out_v[:, 0, P:T], res[1][:, 0, :])
         nc.vector.tensor_copy(res[1][:, 1, :], merged[1][1][:])
         nc.sync.dma_start(out_v[:, 1, P:T], res[1][:, 1, :])

@@ -17,10 +17,11 @@ P = 128
 D, T, E, C, H, N = 2, 256, 4, 256, 512, 256
 Z = D * T
 S = E * C
-LT = H // P
-ZT = Z // P
-XW = 704
-XS = Z
+LANES = 4
+WORD_WINDOW = 704
+TURNED = 3
+W = TURNED * P
+Y_BANKS = 5
 FLOPS = 2 * H * H * S + 2 * D * H * N * T
 
 
@@ -35,16 +36,16 @@ def tile_moe_mhm_none_kernel(
         def tile(shape, dtype, name, tag=None):
             return sb.tile(shape, dtype, name=name, tag=tag or name, align_bytes=64)
 
-        def bank(shape, b, name):
-            return ps.tile(shape, F32, name=name, tag="bank%d" % b)
+        def bank(shape, number, name):
+            return ps.tile(shape, F32, name=name, tag="bank%d" % number)
 
         offs_sb = tile([P, S // 16], U16, "offs_sb")
         pos_sb = [tile([P, Z // 16], U16, "pos%d_sb" % r) for r in range(2)]
-        xw = tile([P, XW], I32, "xw")
-        xs = tile([P, XS], U8, "xs")
+        xw = tile([P, WORD_WINDOW], I32, "xw")
+        xs = tile([P, Z], U8, "xs")
         ww = tile([P, E * H], I32, "ww")
-        groups = ((0, E - 1), (E - 1, E))
-        ww_part = [ww[:, e0 * H : e1 * H] for e0, e1 in groups]
+        w_loads = ((0, E - 1), (E - 1, E))
+        ww_part = [ww[:, e0 * H : e1 * H] for e0, e1 in w_loads]
         ws = tile([P, H], U8, "ws")
         mw = tile([P, D, N], I32, "mw")
         ms = tile([P, N], U8, "ms")
@@ -52,8 +53,9 @@ def tile_moe_mhm_none_kernel(
 
         nc.vector.memset(xs[:].bitcast(I32), 0)
         nc.gpsimd.memset(ws[:].bitcast(I32), 0)
-        nc.vector.memset(xw[:, Z:XW], 0)
+        nc.vector.memset(xw[:, Z:WORD_WINDOW], 0)
         nc.vector.memset(ms[:].bitcast(I32), 0)
+
         nc.sync.dma_start(
             xw[:, 0:Z].rearrange("p (o t) -> p o t", o=D),
             x_words.rearrange("o p t d -> p o (t d)").bitcast(I32),
@@ -87,57 +89,43 @@ def tile_moe_mhm_none_kernel(
 
         xg = tile([P, S], U32, "xg")
         sg = tile([P, S], U8, "sg")
-
-        def gather_words(s0, s1):
+        for s0 in (0, S // 2):
+            s1 = s0 + S // 2
             nc.vector.tensor_copy(xg[:, s0:s1], xw[:].bitcast(U32).indirect(offs_sb[:, s0 // 16 : s1 // 16]))
-
-        def gather_scales(s0, s1):
+        pieces = [(e * C, (e + 1) * C) for e in range(E - 1)] + [(S - C, S - C // 2), (S - C // 2, S)]
+        for s0, s1 in pieces:
             nc.vector.tensor_copy(sg[:, s0:s1], xs[:].indirect(offs_sb[:, s0 // 16 : s1 // 16]))
 
-        gather_words(0, 2 * C)
-        gather_words(2 * C, S)
-        pieces = [(0, C), (C, 2 * C), (2 * C, 3 * C), (3 * C, 3 * C + P), (3 * C + P, S)]
-        for s0, s1 in pieces:
-            gather_scales(s0, s1)
         wp0 = tile([P, E * P], I32, "wp0")
-        wsp = tile([P, 4, P], U8, "wsp")
-        ws4 = ws[:].rearrange("p (m d) -> p d m", d=4)
+        wsp = tile([P, LANES, P], U8, "wsp")
+        ws_lanes = ws[:].rearrange("p (m d) -> p d m", d=LANES)
 
-        def first_lane(g):
-            nc.gpsimd.tensor_copy(wp0[:, groups[g][0] * P : groups[g][1] * P], ww_part[g].rearrange("p (c d) -> p d c", d=4)[:, 0, :])
+        def sort_lane_0(load):
+            e0, e1 = w_loads[load]
+            nc.gpsimd.tensor_copy(wp0[:, e0 * P : e1 * P], ww_part[load].rearrange("p (c d) -> p d c", d=LANES)[:, 0, :])
 
-        first_lane(0)
-        nc.gpsimd.tensor_copy(wsp[:, 0, :], ws4[:, 0, :])
-        first_lane(1)
-        nc.gpsimd.tensor_copy(wsp[:, 1:4, :], ws4[:, 1:4, :])
-        wp123 = tile([P, 3, E * P], I32, "wp123", "xs")
+        sort_lane_0(0)
+        nc.gpsimd.tensor_copy(wsp[:, 0, :], ws_lanes[:, 0, :])
+        sort_lane_0(1)
+        nc.gpsimd.tensor_copy(wsp[:, 1:LANES, :], ws_lanes[:, 1:LANES, :])
+        wp123 = tile([P, LANES - 1, E * P], I32, "wp123", "xs")
         for c0 in (0, 2 * P):
             nc.vector.tensor_copy(
                 wp123[:, :, c0 : c0 + 2 * P].rearrange("p d c -> p c d"),
-                ww[:].rearrange("p (c d) -> p c d", d=4)[:, c0 : c0 + 2 * P, 1:4],
+                ww[:].rearrange("p (c d) -> p c d", d=LANES)[:, c0 : c0 + 2 * P, 1:LANES],
             )
 
-        for i in range(2):
-            idle = bank([P, H], 5 + i, "idle%d" % i)
-            nc.tensor.matmul_mx(
-                out=idle[:],
-                lhsT=ww[:, 0:P].bitcast(FP8X4),
-                lhsT_scale=ws[:, 0:P],
-                rhs=ww[:, 0:H].bitcast(FP8X4),
-                rhs_scale=ws[:],
-                start=True,
-                stop=True,
-            )
-
-        y = [tile([P, S], F32, "y%d" % d) for d in range(4)]
-        steps = [(0, s0, s1) for s0, s1 in pieces] + [(d, e * C, (e + 1) * C) for d in range(1, 4) for e in range(E)]
+        y = [tile([P, S], F32, "y%d" % d) for d in range(LANES)]
+        steps = [(0, s0, s1) for s0, s1 in pieces]
+        steps.extend((d, e * C, (e + 1) * C) for d in range(1, LANES) for e in range(E))
         for i, (d, s0, s1) in enumerate(steps):
-            cols = slice(s0 // C * P, (s0 // C + 1) * P)
-            acc = bank([P, s1 - s0], i % 5, "yacc%d" % i)
+            e = s0 // C
+            cols = slice(e * P, (e + 1) * P)
+            acc = bank([P, s1 - s0], i % Y_BANKS, "yacc%d" % i)
             nc.tensor.matmul_mx(
                 out=acc[:],
                 lhsT=(wp0[:, cols] if d == 0 else wp123[:, d - 1, cols]).bitcast(FP8X4),
-                lhsT_scale=wsp[4 * (s0 // C) : P, d, :],
+                lhsT_scale=wsp[4 * e : P, d, :],
                 rhs=xg[:, s0:s1].bitcast(FP8X4),
                 rhs_scale=sg[:, s0:s1],
                 start=True,
@@ -145,103 +133,104 @@ def tile_moe_mhm_none_kernel(
             )
             nc.scalar.copy(y[d][:, s0:s1], acc[:])
 
-        NB = 3
-        W = NB * P
-        part = [[tile([P, W], F32, "part%d_%d" % (d, r)) for r in range(2)] for d in range(4)]
-        turned = [bank([P, 4, P], 5 + b, "turned%d" % b) for b in range(NB)]
-        pairs = [[tile([P, P, 2], BF16, "pairs%d_%d" % (b, u)) for u in range(2)] for b in range(NB)]
-        grouped = tile([P, NB * H], BF16, "grouped")
+        last_step = len(steps) - 1
+        turned_banks = (Y_BANKS, (last_step - E) % Y_BANKS, last_step % Y_BANKS)
+        part = [[tile([P, W], F32, "part%d_%d" % (d, r)) for r in range(2)] for d in range(LANES)]
+        turned = [bank([P, LANES, P], turned_banks[g], "turned%d" % g) for g in range(TURNED)]
+        pairs = [[tile([P, P, 2], BF16, "pairs%d_%d" % (g, u)) for u in range(2)] for g in range(TURNED)]
+        grouped01 = tile([P, 2 * H], BF16, "grouped01")
+        grouped2 = tile([P, H], BF16, "grouped2")
+        grouped = [grouped01[:, 0:H], grouped01[:, H : 2 * H], grouped2[:]]
 
         def fetch(dst, d, r, z0, z1):
             nc.vector.tensor_tensor(dst, y[d][:].indirect(pos_sb[r][:, z0 // 16 : z1 // 16]), gate_sb[:, r, z0:z1], MULT)
 
-        def fetch_and_turn(d, b0, b1):
+        def fetch_and_turn(d, g0, g1):
             for r in range(2):
-                fetch(part[d][r][:, b0 * P : b1 * P], d, r, b0 * P, b1 * P)
-                for b in range(b0, b1):
+                fetch(part[d][r][:, g0 * P : g1 * P], d, r, g0 * P, g1 * P)
+                for g in range(g0, g1):
                     nc.tensor.matmul(
-                        turned[b][:, d, :],
-                        lhsT=part[d][r][:, b * P : (b + 1) * P],
+                        turned[g][:, d, :],
+                        lhsT=part[d][r][:, g * P : (g + 1) * P],
                         rhs=ident[:],
                         is_transpose=True,
                         start=(r == 0),
                         stop=(r == 1),
                     )
 
-        def turn_back(b, u):
-            nc.scalar.copy(pairs[b][u][:], turned[b][:, 2 * u : 2 * u + 2, :].rearrange("z e p -> z p e"))
-            nc.tensor.transpose(turned[b][:, u, :], pairs[b][u][:].rearrange("z p e -> z (p e)").bitcast(F32), ident[:])
+        def turn_back(g, u):
+            nc.scalar.copy(pairs[g][u][:], turned[g][:, 2 * u : 2 * u + 2, :].rearrange("z e p -> z p e"))
+            nc.tensor.transpose(turned[g][:, u, :], pairs[g][u][:].rearrange("z p e -> z (p e)").bitcast(F32), ident[:])
 
-        def regroup(b):
+        def regroup(g):
             nc.scalar.copy(
-                grouped[:, b * H : (b + 1) * H].bitcast(F32).rearrange("p (z u) -> p z u", u=2), turned[b][:, 0:2, :].rearrange("p u z -> p z u")
+                grouped[g].bitcast(F32).rearrange("p (z u) -> p z u", u=2), turned[g][:, 0:2, :].rearrange("p u z -> p z u")
             )
 
-        codes = tile([P, Z], U32, "codes")
+        codes012 = tile([P, W], U32, "codes012")
+        codes3 = tile([P, P], U32, "codes3", "grouped2")
+        codes = [codes012[:, g * P : (g + 1) * P] for g in range(TURNED)] + [codes3[:]]
         planes = tile([P, Z], U8, "planes")
 
-        def quantise(b0, b1, values):
-            zc = slice(b0 * P, b1 * P)
-            nc.vector.quantize_mx(out=codes[:, zc].bitcast(FP8X4), scales=planes[:, zc], in_=values)
+        def quantise(dst, g0, g1, values):
+            nc.vector.quantize_mx(out=dst.bitcast(FP8X4), scales=planes[:, g0 * P : g1 * P], in_=values)
 
-        merged = [[bank([P, P], 2 * half + nh, "merged%d_%d" % (half, nh)) for nh in range(2)] for half in range(2)]
+        merge_banks = [b for b in range(1, 8) if b not in turned_banks]
+        merged = [
+            [bank([P, P], merge_banks[2 * half + nh], "merged%d_%d" % (half, nh)) for nh in range(2)] for half in range(2)
+        ]
 
-        def merge(b):
-            o, half = divmod(b, 2)
+        def merge(g):
+            o, half = divmod(g, 2)
             for nh in range(2):
                 cols = slice(nh * P, (nh + 1) * P)
                 nc.tensor.matmul_mx(
                     out=merged[half][nh][:],
                     lhsT=mw[:, o, cols].bitcast(FP8X4),
                     lhsT_scale=ms[4 * o : P, cols],
-                    rhs=codes[:, b * P : (b + 1) * P].bitcast(FP8X4),
-                    rhs_scale=planes[:, b * P : (b + 1) * P],
+                    rhs=codes[g].bitcast(FP8X4),
+                    rhs_scale=planes[:, g * P : (g + 1) * P],
                     start=(o == 0),
                     stop=(o == D - 1),
                 )
 
-        fetch_and_turn(0, 0, NB)
-        fetch_and_turn(1, 0, NB)
-        for b in range(NB):
-            turn_back(b, 0)
-        fetch_and_turn(2, 0, NB)
-        for b0, b1 in ((0, NB - 1), (NB - 1, NB)):
-            fetch_and_turn(3, b0, b1)
-            for b in range(b0, b1):
-                turn_back(b, 1)
-            for b in range(b0, b1):
-                regroup(b)
+        fetch_and_turn(0, 0, TURNED)
+        fetch_and_turn(1, 0, TURNED)
+        for g in range(TURNED):
+            turn_back(g, 0)
+        fetch_and_turn(2, 0, TURNED)
+        for g0, g1 in ((0, TURNED - 1), (TURNED - 1, TURNED)):
+            fetch_and_turn(3, g0, g1)
+            for g in range(g0, g1):
+                turn_back(g, 1)
+            for g in range(g0, g1):
+                regroup(g)
 
-        last = [tile([P, 4, P], F32, "last%d" % r, "part1_%d" % r) for r in range(2)]
-        for d in range(4):
+        last = [tile([P, LANES, P], F32, "last%d" % r, "part1_%d" % r) for r in range(2)]
+        for d in range(LANES):
             for r in range(2):
                 fetch(last[r][:, d, :], d, r, W, Z)
-        quantise(0, 2, grouped[:, 0 : 2 * H])
+        quantise(codes012[:, 0 : 2 * P], 0, 2, grouped01[:])
         merge(0)
         merge(1)
-        quantise(2, 3, grouped[:, 2 * H : 3 * H])
+        grouped3 = tile([P, H], BF16, "grouped3", "grouped01")
+        nc.vector.tensor_tensor(
+            grouped3[:].rearrange("p (c i d) -> p c d i", i=4, d=LANES),
+            last[0][:].rearrange("p d (c i) -> p c d i", i=4),
+            last[1][:].rearrange("p d (c i) -> p c d i", i=4),
+            ADD,
+        )
+        quantise(codes[2], 2, 3, grouped2[:])
+        quantise(codes[3], 3, 4, grouped3[:])
         merge(2)
-        grouped3 = tile([P, H], BF16, "grouped3", "grouped")
-        for z0 in (0, P // 2):
-            zc = slice(z0, z0 + P // 2)
-            nc.vector.tensor_tensor(
-                grouped3[:, 4 * z0 : 4 * z0 + H // 2].rearrange("p (c i d) -> p c d i", i=4, d=4),
-                last[0][:, :, zc].rearrange("p d (c i) -> p c d i", i=4),
-                last[1][:, :, zc].rearrange("p d (c i) -> p c d i", i=4),
-                ADD,
-            )
-        for z0 in (0, P // 2):
-            zc = slice(W + z0, W + z0 + P // 2)
-            nc.vector.quantize_mx(
-                out=codes[:, zc].bitcast(FP8X4), scales=planes[:, zc], in_=grouped3[:, 4 * z0 : 4 * z0 + H // 2]
-            )
         merge(3)
+
         out_v = out.rearrange("(nh p) t -> p nh t", p=P)
         res = [tile([P, 2, P], F32, "res%d" % half) for half in range(2)]
         nc.scalar.copy(res[0][:, 0, :], merged[0][0][:])
         nc.scalar.copy(res[0][:, 1, :], merged[0][1][:])
         nc.sync.dma_start(out_v[:, :, 0:P], res[0][:])
         nc.scalar.copy(res[1][:, 0, :], merged[1][0][:])
-        nc.scalar.dma_start(out_v[:, 0, P:T], res[1][:, 0, :])
+        nc.sync.dma_start(out_v[:, 0, P:T], res[1][:, 0, :])
         nc.vector.tensor_copy(res[1][:, 1, :], merged[1][1][:])
         nc.sync.dma_start(out_v[:, 1, P:T], res[1][:, 1, :])

@@ -18,7 +18,8 @@ D, T, E, C, H, N = 2, 256, 4, 256, 512, 256
 Z = D * T
 S = E * C
 LANES = 4
-WORD_WINDOW = 704
+WORD_WINDOW = 1376
+BYTE_WINDOW = 704
 TURNED = 3
 W = TURNED * P
 Y_BANKS = 5
@@ -42,7 +43,7 @@ def tile_moe_mhm_none_kernel(
         offs_sb = tile([P, S // 16], U16, "offs_sb")
         pos_sb = [tile([P, Z // 16], U16, "pos%d_sb" % r) for r in range(2)]
         xw = tile([P, WORD_WINDOW], I32, "xw")
-        xs = tile([P, Z], U8, "xs")
+        xs = tile([P, BYTE_WINDOW], U8, "xs")
         ww = tile([P, E * H], I32, "ww")
         w_loads = ((0, E - 1), (E - 1, E))
         ww_part = [ww[:, e0 * H : e1 * H] for e0, e1 in w_loads]
@@ -53,8 +54,8 @@ def tile_moe_mhm_none_kernel(
 
         nc.vector.memset(xs[:].bitcast(I32), 0)
         nc.gpsimd.memset(ws[:].bitcast(I32), 0)
-        nc.vector.memset(xw[:, Z:WORD_WINDOW], 0)
         nc.vector.memset(ms[:].bitcast(I32), 0)
+        nc.vector.memset(xw[:, Z:WORD_WINDOW], 0)
 
         nc.sync.dma_start(
             xw[:, 0:Z].rearrange("p (o t) -> p o t", o=D),
@@ -89,11 +90,9 @@ def tile_moe_mhm_none_kernel(
 
         xg = tile([P, S], U32, "xg")
         sg = tile([P, S], U8, "sg")
-        for s0 in (0, S // 2):
-            s1 = s0 + S // 2
-            nc.vector.tensor_copy(xg[:, s0:s1], xw[:].bitcast(U32).indirect(offs_sb[:, s0 // 16 : s1 // 16]))
+        nc.vector.tensor_copy(xg[:], xw[:].bitcast(U32).indirect(offs_sb[:]))
         pieces = [(e * C, (e + 1) * C) for e in range(E - 1)] + [(S - C, S - C // 2), (S - C // 2, S)]
-        for s0, s1 in pieces:
+        for s0, s1 in [(0, 2 * C)] + pieces[2:]:
             nc.vector.tensor_copy(sg[:, s0:s1], xs[:].indirect(offs_sb[:, s0 // 16 : s1 // 16]))
 
         wp0 = tile([P, E * P], I32, "wp0")
@@ -135,7 +134,9 @@ def tile_moe_mhm_none_kernel(
 
         last_step = len(steps) - 1
         turned_banks = (Y_BANKS, (last_step - E) % Y_BANKS, last_step % Y_BANKS)
-        part = [[tile([P, W], F32, "part%d_%d" % (d, r)) for r in range(2)] for d in range(LANES)]
+        fetched = [tile([P, (LANES * TURNED + 1) * P], F32, "fetched%d" % r) for r in range(2)]
+        first = [0] + [(d * TURNED + 1) * P for d in range(1, LANES)]
+        part = [[fetched[r][:, first[d] : first[d] + (Z if d == 0 else W)] for r in range(2)] for d in range(LANES)]
         turned = [bank([P, LANES, P], turned_banks[g], "turned%d" % g) for g in range(TURNED)]
         pairs = [[tile([P, P, 2], BF16, "pairs%d_%d" % (g, u)) for u in range(2)] for g in range(TURNED)]
         grouped01 = tile([P, 2 * H], BF16, "grouped01")
@@ -145,9 +146,9 @@ def tile_moe_mhm_none_kernel(
         def fetch(dst, d, r, z0, z1):
             nc.vector.tensor_tensor(dst, y[d][:].indirect(pos_sb[r][:, z0 // 16 : z1 // 16]), gate_sb[:, r, z0:z1], MULT)
 
-        def fetch_and_turn(d, g0, g1):
+        def fetch_and_turn(d, g0, g1, more=0):
             for r in range(2):
-                fetch(part[d][r][:, g0 * P : g1 * P], d, r, g0 * P, g1 * P)
+                fetch(part[d][r][:, g0 * P : (g1 + more) * P], d, r, g0 * P, (g1 + more) * P)
                 for g in range(g0, g1):
                     nc.tensor.matmul(
                         turned[g][:, d, :],
@@ -168,12 +169,12 @@ def tile_moe_mhm_none_kernel(
             )
 
         codes012 = tile([P, W], U32, "codes012")
-        codes3 = tile([P, P], U32, "codes3", "grouped2")
+        codes3 = tile([P, P], U32, "codes3")
         codes = [codes012[:, g * P : (g + 1) * P] for g in range(TURNED)] + [codes3[:]]
         planes = tile([P, Z], U8, "planes")
 
-        def quantise(dst, g0, g1, values):
-            nc.vector.quantize_mx(out=dst.bitcast(FP8X4), scales=planes[:, g0 * P : g1 * P], in_=values)
+        def quantise(dst, scales, values):
+            nc.vector.quantize_mx(out=dst.bitcast(FP8X4), scales=scales, in_=values)
 
         merge_banks = [b for b in range(1, 8) if b not in turned_banks]
         merged = [
@@ -194,7 +195,7 @@ def tile_moe_mhm_none_kernel(
                     stop=(o == D - 1),
                 )
 
-        fetch_and_turn(0, 0, TURNED)
+        fetch_and_turn(0, 0, TURNED, 1)
         fetch_and_turn(1, 0, TURNED)
         for g in range(TURNED):
             turn_back(g, 0)
@@ -206,23 +207,27 @@ def tile_moe_mhm_none_kernel(
             for g in range(g0, g1):
                 regroup(g)
 
-        last = [tile([P, LANES, P], F32, "last%d" % r, "part1_%d" % r) for r in range(2)]
-        for d in range(LANES):
+        last = [fetched[r][:].rearrange("p (b z) -> p b z", z=P)[:, TURNED :: TURNED, :] for r in range(2)]
+        for d in range(1, LANES):
             for r in range(2):
                 fetch(last[r][:, d, :], d, r, W, Z)
-        quantise(codes012[:, 0 : 2 * P], 0, 2, grouped01[:])
+        quantise(codes012[:, 0 : 2 * P], planes[:, 0 : 2 * P], grouped01[:])
         merge(0)
         merge(1)
-        grouped3 = tile([P, H], BF16, "grouped3", "grouped01")
-        nc.vector.tensor_tensor(
-            grouped3[:].rearrange("p (c i d) -> p c d i", i=4, d=LANES),
-            last[0][:].rearrange("p d (c i) -> p c d i", i=4),
-            last[1][:].rearrange("p d (c i) -> p c d i", i=4),
-            ADD,
-        )
-        quantise(codes[2], 2, 3, grouped2[:])
-        quantise(codes[3], 3, 4, grouped3[:])
+        quantise(codes[2], planes[:, 2 * P : W], grouped2[:])
         merge(2)
+        halves = [tile([P, H // 2], BF16, "grouped3_%d" % k, tag) for k, tag in enumerate(("grouped01", "grouped2"))]
+        for k in range(2):
+            cols = slice(k * P // 2, (k + 1) * P // 2)
+            nc.vector.tensor_tensor(
+                halves[k][:].rearrange("p (c i d) -> p c d i", i=4, d=LANES),
+                last[0][:, :, cols].rearrange("p d (c i) -> p c d i", i=4),
+                last[1][:, :, cols].rearrange("p d (c i) -> p c d i", i=4),
+                ADD,
+            )
+        for k in range(2):
+            z0, z1 = k * P // 2, (k + 1) * P // 2
+            quantise(codes3[:, z0:z1], planes[:, W + z0 : W + z1], halves[k][:])
         merge(3)
 
         out_v = out.rearrange("(nh p) t -> p nh t", p=P)

@@ -12,17 +12,18 @@ U8 = mybir.dt.uint8
 FP8X4 = mybir.dt.float8_e4m3fn_x4
 MULT = mybir.AluOpType.mult
 ADD = mybir.AluOpType.add
+COPY = mybir.ActivationFunctionType.Copy
 
 P = 128
 D, T, E, C, H, N = 2, 256, 4, 256, 512, 256
 Z = D * T
 S = E * C
 LANES = 4
-WORD_WINDOW = 1376
+WORD_WINDOW = 704
 BYTE_WINDOW = 704
-TURNED = 3
+TURNED = 2
 W = TURNED * P
-Y_BANKS = 5
+ZV = Z - P
 FLOPS = 2 * H * H * S + 2 * D * H * N * T
 
 
@@ -44,13 +45,12 @@ def tile_moe_mhm_none_kernel(
         pos_sb = [tile([P, Z // 16], U16, "pos%d_sb" % r) for r in range(2)]
         xw = tile([P, WORD_WINDOW], I32, "xw")
         xs = tile([P, BYTE_WINDOW], U8, "xs")
-        ww = tile([P, E * H], I32, "ww")
-        w_loads = ((0, E - 1), (E - 1, E))
-        ww_part = [ww[:, e0 * H : e1 * H] for e0, e1 in w_loads]
+        ww = [tile([P, 2 * H], I32, "ww%d" % k) for k in range(2)]
         ws = tile([P, H], U8, "ws")
         mw = tile([P, D, N], I32, "mw")
         ms = tile([P, N], U8, "ms")
-        gate_sb = tile([P, 2, Z], F32, "gate_sb")
+        gate_sb = tile([P, 2, ZV], F32, "gate_sb")
+        gate_col = tile([P, 2], F32, "gate_col")
 
         nc.vector.memset(xs[:].bitcast(I32), 0)
         nc.gpsimd.memset(ws[:].bitcast(I32), 0)
@@ -69,15 +69,16 @@ def tile_moe_mhm_none_kernel(
                 x_scales[:, 4 * q : 4 * q + 4, :].bitcast(I32).rearrange("o r t -> r o t"),
             )
         w_rows = w_words[:, 0].rearrange("e p l d -> p e (l d)").bitcast(I32)
-        nc.sync.dma_start(ww_part[0].rearrange("p (e l) -> p e l", l=H), w_rows[:, 0 : E - 1, :])
+        nc.sync.dma_start(ww[0][:].rearrange("p (e l) -> p e l", l=H), w_rows[:, 0:2, :])
         for q in range(4):
             nc.sync.dma_start(
                 ws[32 * q : 32 * q + 4 * E, :].bitcast(I32),
                 w_scales[:, 0, 4 * q : 4 * q + 4, :].bitcast(I32),
             )
-        nc.sync.dma_start(ww_part[1], w_rows[:, E - 1, :])
+        nc.sync.dma_start(ww[1][:].rearrange("p (e l) -> p e l", l=H), w_rows[:, 2:E, :])
         nc.sync.dma_start(pos_sb[1][:], pos2)
-        nc.sync.dma_start(gate_sb[:], gate.rearrange("r p z -> p r z"))
+        nc.sync.dma_start(gate_sb[:], gate[:, :, P:Z].rearrange("r p z -> p r z"))
+        nc.sync.dma_start(gate_col[:], gate[:, 0, 0:P].rearrange("r z -> z r"), allow_slow_non_contiguous=True)
         nc.sync.dma_start(mw[:], wm_words.rearrange("o p n d -> p o (n d)").bitcast(I32))
         for q in range(4):
             nc.sync.dma_start(
@@ -88,63 +89,78 @@ def tile_moe_mhm_none_kernel(
         ident = tile([P, P], F32, "ident")
         make_identity(nc, ident[:])
 
-        xg = tile([P, S], U32, "xg")
+        xg = [tile([P, 2 * C], U32, "xg0"), tile([P, 2 * C], U32, "xg1", "xs")]
         sg = tile([P, S], U8, "sg")
-        nc.vector.tensor_copy(xg[:], xw[:].bitcast(U32).indirect(offs_sb[:]))
-        pieces = [(e * C, (e + 1) * C) for e in range(E - 1)] + [(S - C, S - C // 2), (S - C // 2, S)]
-        for s0, s1 in [(0, 2 * C)] + pieces[2:]:
+
+        def words(s0, s1):
+            k = s0 // (2 * C)
+            return xg[k][:, s0 - 2 * C * k : s1 - 2 * C * k]
+
+        def gather_words(s0, s1):
+            nc.vector.tensor_copy(words(s0, s1), xw[:].bitcast(U32).indirect(offs_sb[:, s0 // 16 : s1 // 16]))
+
+        def gather_bytes(s0, s1):
             nc.vector.tensor_copy(sg[:, s0:s1], xs[:].indirect(offs_sb[:, s0 // 16 : s1 // 16]))
 
-        wp0 = tile([P, E * P], I32, "wp0")
+        pieces = [(2 * C, 3 * C), (3 * C, S - C // 2), (S - C // 2, S)]
+        gather_words(0, 2 * C)
+        gather_bytes(0, 2 * C)
+        gather_bytes(2 * C, S)
+        for s0, s1 in pieces:
+            gather_words(s0, s1)
+
+        wp01 = tile([P, LANES, 2 * P], U32, "wp01")
+        wp23 = [tile([P, 2 * P], I32, "wp23_%d" % d) for d in range(LANES)]
         wsp = tile([P, LANES, P], U8, "wsp")
         ws_lanes = ws[:].rearrange("p (m d) -> p d m", d=LANES)
-
-        def sort_lane_0(load):
-            e0, e1 = w_loads[load]
-            nc.gpsimd.tensor_copy(wp0[:, e0 * P : e1 * P], ww_part[load].rearrange("p (c d) -> p d c", d=LANES)[:, 0, :])
-
-        sort_lane_0(0)
+        nc.scalar.copy(wp01[:].rearrange("p d c -> p c d"), ww[0][:].bitcast(U32).rearrange("p (c d) -> p c d", d=LANES))
         nc.gpsimd.tensor_copy(wsp[:, 0, :], ws_lanes[:, 0, :])
-        sort_lane_0(1)
         nc.gpsimd.tensor_copy(wsp[:, 1:LANES, :], ws_lanes[:, 1:LANES, :])
-        wp123 = tile([P, LANES - 1, E * P], I32, "wp123", "xs")
-        for c0 in (0, 2 * P):
-            nc.vector.tensor_copy(
-                wp123[:, :, c0 : c0 + 2 * P].rearrange("p d c -> p c d"),
-                ww[:].rearrange("p (c d) -> p c d", d=LANES)[:, c0 : c0 + 2 * P, 1:LANES],
-            )
+        for d in range(LANES):
+            nc.gpsimd.tensor_copy(wp23[d][:], ww[1][:].rearrange("p (c d) -> p d c", d=LANES)[:, d, :])
 
         y = [tile([P, S], F32, "y%d" % d) for d in range(LANES)]
-        steps = [(0, s0, s1) for s0, s1 in pieces]
-        steps.extend((d, e * C, (e + 1) * C) for d in range(1, LANES) for e in range(E))
-        for i, (d, s0, s1) in enumerate(steps):
-            e = s0 // C
-            cols = slice(e * P, (e + 1) * P)
-            acc = bank([P, s1 - s0], i % Y_BANKS, "yacc%d" % i)
-            nc.tensor.matmul_mx(
-                out=acc[:],
-                lhsT=(wp0[:, cols] if d == 0 else wp123[:, d - 1, cols]).bitcast(FP8X4),
-                lhsT_scale=wsp[4 * e : P, d, :],
-                rhs=xg[:, s0:s1].bitcast(FP8X4),
-                rhs_scale=sg[:, s0:s1],
-                start=True,
-                stop=True,
-            )
-            nc.scalar.copy(y[d][:, s0:s1], acc[:])
 
-        last_step = len(steps) - 1
-        turned_banks = (Y_BANKS, (last_step - E) % Y_BANKS, last_step % Y_BANKS)
+        def product(d, s0, s1, number, copy_out):
+            acc = bank([P, s1 - s0], number, "yacc%d_%d" % (d, s0))
+            for t0 in range(s0, s1, C):
+                t1 = min(t0 + C, s1)
+                e = t0 // C
+                cols = slice(e % 2 * P, (e % 2 + 1) * P)
+                nc.tensor.matmul_mx(
+                    out=acc[:, t0 - s0 : t1 - s0],
+                    lhsT=(wp01[:, d, cols] if e < 2 else wp23[d][:, cols]).bitcast(FP8X4),
+                    lhsT_scale=wsp[4 * e : P, d, :],
+                    rhs=words(t0, t1).bitcast(FP8X4),
+                    rhs_scale=sg[:, t0:t1],
+                    start=True,
+                    stop=True,
+                )
+            copy_out(y[d][:, s0:s1], acc[:])
+
+        for d in range(LANES):
+            product(d, 0, 2 * C, d, nc.vector.tensor_copy if d == LANES - 1 else nc.scalar.copy)
+        for i, (s0, s1) in enumerate(pieces):
+            product(0, s0, s1, 4 + i, nc.scalar.copy)
+        for d, number in ((1, 7), (2, 0), (3, 1)):
+            product(d, 2 * C, S, number, nc.scalar.copy)
+
+        plain_banks = (6, 2)
+        turned_banks = (4, 5)
+        merge_banks = (0, 1, 3, 7)
         fetched = [tile([P, (LANES * TURNED + 1) * P], F32, "fetched%d" % r) for r in range(2)]
         first = [0] + [(d * TURNED + 1) * P for d in range(1, LANES)]
-        part = [[fetched[r][:, first[d] : first[d] + (Z if d == 0 else W)] for r in range(2)] for d in range(LANES)]
+        part = [[fetched[r][:, first[d] : first[d] + (ZV if d == 0 else W)] for r in range(2)] for d in range(LANES)]
         turned = [bank([P, LANES, P], turned_banks[g], "turned%d" % g) for g in range(TURNED)]
-        pairs = [[tile([P, P, 2], BF16, "pairs%d_%d" % (g, u)) for u in range(2)] for g in range(TURNED)]
-        grouped01 = tile([P, 2 * H], BF16, "grouped01")
-        grouped2 = tile([P, H], BF16, "grouped2")
-        grouped = [grouped01[:, 0:H], grouped01[:, H : 2 * H], grouped2[:]]
+        pairs = [[tile([P, P, 2], BF16, "pairs%d_%d" % (g, u)) for u in range(2)] for g in range(TURNED + 1)]
+        grouped0 = tile([P, H], BF16, "grouped0")
+        grouped12 = tile([P, 2 * H], BF16, "grouped12")
+        grouped = [grouped0[:], grouped12[:, 0:H], grouped12[:, H : 2 * H]]
 
         def fetch(dst, d, r, z0, z1):
-            nc.vector.tensor_tensor(dst, y[d][:].indirect(pos_sb[r][:, z0 // 16 : z1 // 16]), gate_sb[:, r, z0:z1], MULT)
+            nc.vector.tensor_tensor(
+                dst, y[d][:].indirect(pos_sb[r][:, (P + z0) // 16 : (P + z1) // 16]), gate_sb[:, r, z0:z1], MULT
+            )
 
         def fetch_and_turn(d, g0, g1, more=0):
             for r in range(2):
@@ -159,24 +175,45 @@ def tile_moe_mhm_none_kernel(
                         stop=(r == 1),
                     )
 
-        def turn_back(g, u):
-            nc.scalar.copy(pairs[g][u][:], turned[g][:, 2 * u : 2 * u + 2, :].rearrange("z e p -> z p e"))
-            nc.tensor.transpose(turned[g][:, u, :], pairs[g][u][:].rearrange("z p e -> z (p e)").bitcast(F32), ident[:])
+        def words_back(dst, g, u):
+            nc.tensor.transpose(dst[:, u, :], pairs[g][u][:].rearrange("z p e -> z (p e)").bitcast(F32), ident[:])
 
-        def regroup(g):
+        def turn_back(g, u):
+            nc.scalar.copy(pairs[g + 1][u][:], turned[g][:, 2 * u : 2 * u + 2, :].rearrange("z e p -> z p e"))
+            words_back(turned[g], g + 1, u)
+
+        def regroup(g, src):
             nc.scalar.copy(
-                grouped[g].bitcast(F32).rearrange("p (z u) -> p z u", u=2), turned[g][:, 0:2, :].rearrange("p u z -> p z u")
+                grouped[g].bitcast(F32).rearrange("p (z u) -> p z u", u=2), src[:, 0:2, :].rearrange("p u z -> p z u")
             )
 
-        codes012 = tile([P, W], U32, "codes012")
+        plain = [bank([P, 2, 2, P], plain_banks[u], "plain%d" % u) for u in range(2)]
+        picked = tile([P, LANES, 2, P], F32, "picked")
+        gated0 = tile([P, 2 * P], F32, "gated0")
+        gated = [v.rearrange("z (p e) -> z p e", e=2) for v in (gated0[:], part[2][0])]
+
+        def pick(u):
+            for e in range(2):
+                d = 2 * u + e
+                for r in range(2):
+                    nc.scalar.activation(picked[:, d, r, :], y[d][:].indirect(pos_sb[r][:, 0 : P // 16]), COPY)
+                    nc.tensor.transpose(plain[u][:, r, e, :], picked[:, d, r, :], ident[:])
+            nc.scalar.activation(gated[u], plain[u][:, 0].rearrange("z e p -> z p e"), COPY, scale=gate_col[:, 0:1])
+
+        def combine(u):
+            nc.vector.scalar_tensor_tensor(
+                pairs[0][u][:], plain[u][:, 1].rearrange("z e p -> z p e"), gate_col[:, 1:2], gated[u], MULT, ADD
+            )
+            words_back(plain[0][:, 0], 0, u)
+
+        codes012 = tile([P, 3 * P], U32, "codes012")
         codes3 = tile([P, P], U32, "codes3")
-        codes = [codes012[:, g * P : (g + 1) * P] for g in range(TURNED)] + [codes3[:]]
+        codes = [codes012[:, g * P : (g + 1) * P] for g in range(3)] + [codes3[:]]
         planes = tile([P, Z], U8, "planes")
 
         def quantise(dst, scales, values):
             nc.vector.quantize_mx(out=dst.bitcast(FP8X4), scales=scales, in_=values)
 
-        merge_banks = [b for b in range(1, 8) if b not in turned_banks]
         merged = [
             [bank([P, P], merge_banks[2 * half + nh], "merged%d_%d" % (half, nh)) for nh in range(2)] for half in range(2)
         ]
@@ -191,32 +228,37 @@ def tile_moe_mhm_none_kernel(
                     lhsT_scale=ms[4 * o : P, cols],
                     rhs=codes[g].bitcast(FP8X4),
                     rhs_scale=planes[:, g * P : (g + 1) * P],
-                    start=(o == 0),
-                    stop=(o == D - 1),
+                    start=(g in (1, 2)),
+                    stop=(g in (0, 3)),
                 )
 
         fetch_and_turn(0, 0, TURNED, 1)
         fetch_and_turn(1, 0, TURNED)
+        pick(0)
         for g in range(TURNED):
             turn_back(g, 0)
         fetch_and_turn(2, 0, TURNED)
-        for g0, g1 in ((0, TURNED - 1), (TURNED - 1, TURNED)):
-            fetch_and_turn(3, g0, g1)
-            for g in range(g0, g1):
-                turn_back(g, 1)
-            for g in range(g0, g1):
-                regroup(g)
+        pick(1)
+        fetch_and_turn(3, 0, TURNED)
+        combine(0)
+        for g in range(TURNED):
+            turn_back(g, 1)
+        for g in range(TURNED):
+            regroup(g + 1, turned[g])
 
         last = [fetched[r][:].rearrange("p (b z) -> p b z", z=P)[:, TURNED :: TURNED, :] for r in range(2)]
         for d in range(1, LANES):
             for r in range(2):
-                fetch(last[r][:, d, :], d, r, W, Z)
-        quantise(codes012[:, 0 : 2 * P], planes[:, 0 : 2 * P], grouped01[:])
-        merge(0)
+                fetch(last[r][:, d, :], d, r, W, ZV)
+            if d == 1:
+                combine(1)
+        regroup(0, plain[0][:, 0])
+        quantise(codes012[:, P : 3 * P], planes[:, P : 3 * P], grouped12[:])
         merge(1)
-        quantise(codes[2], planes[:, 2 * P : W], grouped2[:])
         merge(2)
-        halves = [tile([P, H // 2], BF16, "grouped3_%d" % k, tag) for k, tag in enumerate(("grouped01", "grouped2"))]
+        quantise(codes[0], planes[:, 0:P], grouped0[:])
+        merge(0)
+        halves = [tile([P, H // 2], BF16, "grouped3_%d" % k, tag) for k, tag in enumerate(("grouped12", "grouped0"))]
         for k in range(2):
             cols = slice(k * P // 2, (k + 1) * P // 2)
             nc.vector.tensor_tensor(
@@ -227,7 +269,7 @@ def tile_moe_mhm_none_kernel(
             )
         for k in range(2):
             z0, z1 = k * P // 2, (k + 1) * P // 2
-            quantise(codes3[:, z0:z1], planes[:, W + z0 : W + z1], halves[k][:])
+            quantise(codes3[:, z0:z1], planes[:, 3 * P + z0 : 3 * P + z1], halves[k][:])
         merge(3)
 
         out_v = out.rearrange("(nh p) t -> p nh t", p=P)

@@ -89,7 +89,7 @@ def tile_moe_mhm_none_kernel(
         ident = tile([P, P], F32, "ident")
         make_identity(nc, ident[:])
 
-        xg = [tile([P, 2 * C], U32, "xg0"), tile([P, 2 * C], U32, "xg1", "xs")]
+        xg = [tile([P, 2 * C], U32, "xg0"), tile([P, 2 * C], U32, "xg1", "ww0")]
         sg = tile([P, S], U8, "sg")
 
         def words(s0, s1):
@@ -121,7 +121,7 @@ def tile_moe_mhm_none_kernel(
 
         y = [tile([P, S], F32, "y%d" % d) for d in range(LANES)]
 
-        def product(d, s0, s1, number, copy_out):
+        def multiply(d, s0, s1, number):
             acc = bank([P, s1 - s0], number, "yacc%d_%d" % (d, s0))
             for t0 in range(s0, s1, C):
                 t1 = min(t0 + C, s1)
@@ -136,26 +136,36 @@ def tile_moe_mhm_none_kernel(
                     start=True,
                     stop=True,
                 )
-            copy_out(y[d][:, s0:s1], acc[:])
+            return acc
 
-        for d in range(LANES):
-            product(d, 0, 2 * C, d, nc.vector.tensor_copy if d == LANES - 1 else nc.scalar.copy)
+        def product(d, s0, s1, number, copy_out):
+            copy_out(y[d][:, s0:s1], multiply(d, s0, s1, number)[:])
+
+        for d in range(2):
+            product(d, 0, 2 * C, d, nc.scalar.copy)
+        product(2, 0, C, 6, nc.scalar.copy)
+        lane2 = multiply(2, C, 2 * C, 2)
         for i, (s0, s1) in enumerate(pieces):
-            product(0, s0, s1, 4 + i, nc.scalar.copy)
-        for d, number in ((1, 7), (2, 0), (3, 1)):
-            product(d, 2 * C, S, number, nc.scalar.copy)
+            product(0, s0, s1, 3 + i, nc.scalar.copy if i else nc.vector.tensor_copy)
+        nc.vector.tensor_copy(y[2][:, C : 2 * C], lane2[:])
 
-        plain_banks = (6, 2)
-        turned_banks = (4, 5)
-        merge_banks = (0, 1, 3, 7)
-        fetched = [tile([P, (LANES * TURNED + 1) * P], F32, "fetched%d" % r) for r in range(2)]
-        first = [0] + [(d * TURNED + 1) * P for d in range(1, LANES)]
-        part = [[fetched[r][:, first[d] : first[d] + (ZV if d == 0 else W)] for r in range(2)] for d in range(LANES)]
-        turned = [bank([P, LANES, P], turned_banks[g], "turned%d" % g) for g in range(TURNED)]
-        pairs = [[tile([P, P, 2], BF16, "pairs%d_%d" % (g, u)) for u in range(2)] for g in range(TURNED + 1)]
+        merge_banks = (2, 3, 4, 6)
+        fetched = [tile([P, 7 * P], F32, "fetched%d" % r) for r in range(2)]
+        middle = [tile([P, 2, W], F32, "middle%d" % r) for r in range(2)]
+        part = [
+            [fetched[r][:, 0:ZV] for r in range(2)],
+            [middle[r][:, 0, :] for r in range(2)],
+            [middle[r][:, 1, :] for r in range(2)],
+            [fetched[0][:, 3 * P : 5 * P], fetched[1][:, 5 * P : 7 * P]],
+        ]
+        plain = [bank([P, 2, 2, P], u, "plain%d" % u) for u in range(2)]
+        early = bank([P, TURNED, 2, P], 6, "early")
+        late = [bank([P, 2, 2, P], (7, 5)[g], "late%d" % g) for g in range(TURNED)]
+        pairs0 = [tile([P, P, 2], BF16, "pairs0_%d" % u) for u in range(2)]
+        early_pairs = tile([P, TURNED, P, 2], BF16, "early_pairs")
+        late_pairs = [tile([P, P, 2], BF16, "late_pairs%d" % g) for g in range(TURNED)]
         grouped0 = tile([P, H], BF16, "grouped0")
         grouped12 = tile([P, 2 * H], BF16, "grouped12")
-        grouped = [grouped0[:], grouped12[:, 0:H], grouped12[:, H : 2 * H]]
 
         def fetch(dst, d, r, z0, z1):
             nc.vector.tensor_tensor(
@@ -167,44 +177,43 @@ def tile_moe_mhm_none_kernel(
                 fetch(part[d][r][:, g0 * P : (g1 + more) * P], d, r, g0 * P, (g1 + more) * P)
                 for g in range(g0, g1):
                     nc.tensor.matmul(
-                        turned[g][:, d, :],
+                        early[:, g, d, :] if d < 2 else late[g][:, 0, d - 2, :],
                         lhsT=part[d][r][:, g * P : (g + 1) * P],
                         rhs=ident[:],
                         is_transpose=True,
-                        start=(r == 0),
-                        stop=(r == 1),
+                        start=(r == 0 and (g == 0 or d >= 2)),
+                        stop=(r == 1 and (g == TURNED - 1 or d >= 2)),
                     )
 
-        def words_back(dst, g, u):
-            nc.tensor.transpose(dst[:, u, :], pairs[g][u][:].rearrange("z p e -> z (p e)").bitcast(F32), ident[:])
+        def words_back(dst, pairs):
+            nc.tensor.transpose(dst, pairs.rearrange("z p e -> z (p e)").bitcast(F32), ident[:])
 
-        def turn_back(g, u):
-            nc.scalar.copy(pairs[g + 1][u][:], turned[g][:, 2 * u : 2 * u + 2, :].rearrange("z e p -> z p e"))
-            words_back(turned[g], g + 1, u)
+        def turn_back(g):
+            nc.scalar.copy(late_pairs[g][:], late[g][:, 0].rearrange("z e p -> z p e"))
+            words_back(late[g][:, 1, 0, :], early_pairs[:, g])
+            words_back(late[g][:, 1, 1, :], late_pairs[g][:])
 
-        def regroup(g, src):
-            nc.scalar.copy(
-                grouped[g].bitcast(F32).rearrange("p (z u) -> p z u", u=2), src[:, 0:2, :].rearrange("p u z -> p z u")
-            )
+        def regroup(dst, src):
+            nc.scalar.copy(dst.bitcast(F32).rearrange("p (z u) -> p z u", u=2), src.rearrange("p u z -> p z u"))
 
-        plain = [bank([P, 2, 2, P], plain_banks[u], "plain%d" % u) for u in range(2)]
         picked = tile([P, LANES, 2, P], F32, "picked")
-        gated0 = tile([P, 2 * P], F32, "gated0")
-        gated = [v.rearrange("z (p e) -> z p e", e=2) for v in (gated0[:], part[2][0])]
+        gated = [
+            v.rearrange("z (p e) -> z p e", e=2) for v in (fetched[0][:, 5 * P : 7 * P], fetched[1][:, 3 * P : 5 * P])
+        ]
 
-        def pick(u):
-            for e in range(2):
-                d = 2 * u + e
-                for r in range(2):
-                    nc.scalar.activation(picked[:, d, r, :], y[d][:].indirect(pos_sb[r][:, 0 : P // 16]), COPY)
-                    nc.tensor.transpose(plain[u][:, r, e, :], picked[:, d, r, :], ident[:])
+        def pick(d):
+            u, e = divmod(d, 2)
+            for r in range(2):
+                nc.scalar.activation(picked[:, d, r, :], y[d][:].indirect(pos_sb[r][:, 0 : P // 16]), COPY)
+                nc.tensor.transpose(plain[u][:, r, e, :], picked[:, d, r, :], ident[:])
+
+        def scale(u):
             nc.scalar.activation(gated[u], plain[u][:, 0].rearrange("z e p -> z p e"), COPY, scale=gate_col[:, 0:1])
 
         def combine(u):
             nc.vector.scalar_tensor_tensor(
-                pairs[0][u][:], plain[u][:, 1].rearrange("z e p -> z p e"), gate_col[:, 1:2], gated[u], MULT, ADD
+                pairs0[u][:], plain[u][:, 1].rearrange("z e p -> z p e"), gate_col[:, 1:2], gated[u], MULT, ADD
             )
-            words_back(plain[0][:, 0], 0, u)
 
         codes012 = tile([P, 3 * P], U32, "codes012")
         codes3 = tile([P, P], U32, "codes3")
@@ -232,27 +241,35 @@ def tile_moe_mhm_none_kernel(
                     stop=(g in (0, 3)),
                 )
 
+        product(1, 2 * C, S, 3, nc.scalar.copy)
+        pick(0)
+        product(2, 2 * C, S, 4, nc.scalar.copy)
+        product(3, 0, 2 * C, 5, nc.scalar.copy)
+        product(3, 2 * C, S, 2, nc.scalar.copy)
+        for d in range(1, LANES):
+            pick(d)
         fetch_and_turn(0, 0, TURNED, 1)
         fetch_and_turn(1, 0, TURNED)
-        pick(0)
-        for g in range(TURNED):
-            turn_back(g, 0)
+        scale(0)
+        nc.scalar.copy(early_pairs[:], early[:].rearrange("z g e p -> z g p e"))
+        scale(1)
         fetch_and_turn(2, 0, TURNED)
-        pick(1)
-        fetch_and_turn(3, 0, TURNED)
+        for g in range(TURNED):
+            fetch_and_turn(3, g, g + 1)
+            turn_back(g)
+        last = [fetched[r][:, 2 * P : 6 * P].rearrange("p (d z) -> p d z", z=P) for r in range(2)]
+        for d, r in ((1, 0), (2, 0), (3, 1)):
+            fetch(last[r][:, d, :], d, r, W, ZV)
         combine(0)
+        fetch(last[0][:, 3, :], 3, 0, W, ZV)
+        combine(1)
+        for d in (1, 2):
+            fetch(last[1][:, d, :], d, 1, W, ZV)
+        for u in range(2):
+            words_back(plain[1][:, 0, u, :], pairs0[u][:])
         for g in range(TURNED):
-            turn_back(g, 1)
-        for g in range(TURNED):
-            regroup(g + 1, turned[g])
-
-        last = [fetched[r][:].rearrange("p (b z) -> p b z", z=P)[:, TURNED :: TURNED, :] for r in range(2)]
-        for d in range(1, LANES):
-            for r in range(2):
-                fetch(last[r][:, d, :], d, r, W, ZV)
-            if d == 1:
-                combine(1)
-        regroup(0, plain[0][:, 0])
+            regroup(grouped12[:, g * H : (g + 1) * H], late[g][:, 1])
+        regroup(grouped0[:], plain[1][:, 0])
         quantise(codes012[:, P : 3 * P], planes[:, P : 3 * P], grouped12[:])
         merge(1)
         merge(2)

@@ -89,7 +89,7 @@ def tile_moe_mhm_none_kernel(
         ident = tile([P, P], F32, "ident")
         make_identity(nc, ident[:])
 
-        xg = [tile([P, 2 * C], U32, "xg0"), tile([P, 2 * C], U32, "xg1", "ww0")]
+        xg = [tile([P, 2 * C], U32, "xg0"), tile([P, 2 * C], U32, "xg1", "xs")]
         sg = tile([P, S], U8, "sg")
 
         def words(s0, s1):

@@ -149,40 +149,68 @@ def tile_moe_mhm_none_kernel(
             product(0, s0, s1, 3 + i, nc.scalar.copy if i else nc.vector.tensor_copy)
         nc.vector.tensor_copy(y[2][:, C : 2 * C], lane2[:])
 
-        merge_banks = (2, 3, 4, 6)
+        def empty(copy, d, s0, s1, acc):
+            copy(y[d][:, s0:s1], acc[:])
+
+        rest = [multiply(*a) for a in ((1, 2 * C, S, 3), (2, 2 * C, S, 4), (3, 0, 2 * C, 5), (3, 2 * C, S, 2))]
+
         fetched = [tile([P, 7 * P], F32, "fetched%d" % r) for r in range(2)]
-        middle = [tile([P, 2, W], F32, "middle%d" % r) for r in range(2)]
+        second = [tile([P, W], F32, "second%d" % r) for r in range(2)]
         part = [
             [fetched[r][:, 0:ZV] for r in range(2)],
-            [middle[r][:, 0, :] for r in range(2)],
-            [middle[r][:, 1, :] for r in range(2)],
-            [fetched[0][:, 3 * P : 5 * P], fetched[1][:, 5 * P : 7 * P]],
+            [second[r][:] for r in range(2)],
+            [fetched[r][:, 5 * P : 7 * P] for r in range(2)],
+            [fetched[r][:, 3 * P : 5 * P] for r in range(2)],
         ]
-        plain = [bank([P, 2, 2, P], u, "plain%d" % u) for u in range(2)]
         early = bank([P, TURNED, 2, P], 6, "early")
+        plain = [bank([P, 2, 2, P], u, "plain%d" % u) for u in range(2)]
         late = [bank([P, 2, 2, P], (7, 5)[g], "late%d" % g) for g in range(TURNED)]
-        pairs0 = [tile([P, P, 2], BF16, "pairs0_%d" % u) for u in range(2)]
         early_pairs = tile([P, TURNED, P, 2], BF16, "early_pairs")
         late_pairs = [tile([P, P, 2], BF16, "late_pairs%d" % g) for g in range(TURNED)]
         grouped0 = tile([P, H], BF16, "grouped0")
         grouped12 = tile([P, 2 * H], BF16, "grouped12")
+        picked = tile([P, LANES, 2, P], F32, "picked")
+        scaled = tile([P, 2, 2, 2, P], F32, "scaled")
 
         def fetch(dst, d, r, z0, z1):
             nc.vector.tensor_tensor(
                 dst, y[d][:].indirect(pos_sb[r][:, (P + z0) // 16 : (P + z1) // 16]), gate_sb[:, r, z0:z1], MULT
             )
 
+        def turn(d, r, g):
+            nc.tensor.matmul(
+                early[:, g, d, :] if d < 2 else late[g][:, 0, d - 2, :],
+                lhsT=part[d][r][:, g * P : (g + 1) * P],
+                rhs=ident[:],
+                is_transpose=True,
+                start=(d % 2 == 0 and r == 0 and (g == 0 or d >= 2)),
+                stop=(d % 2 == 1 and r == 1 and (g == TURNED - 1 or d >= 2)),
+            )
+
         def fetch_and_turn(d, g0, g1, more=0):
             for r in range(2):
                 fetch(part[d][r][:, g0 * P : (g1 + more) * P], d, r, g0 * P, (g1 + more) * P)
                 for g in range(g0, g1):
+                    turn(d, r, g)
+
+        def pick(d):
+            u, e = divmod(d, 2)
+            for r in range(2):
+                nc.scalar.activation(picked[:, d, r, :], y[d][:].indirect(pos_sb[r][:, 0 : P // 16]), COPY)
+                nc.tensor.transpose(plain[u][:, r, e, :], picked[:, d, r, :], ident[:])
+
+        def scale(u, back):
+            for r in range(2):
+                nc.scalar.activation(scaled[:, u, r], plain[u][:, r], COPY, scale=gate_col[:, r : r + 1])
+            for e in range(2):
+                for r in range(2):
                     nc.tensor.matmul(
-                        early[:, g, d, :] if d < 2 else late[g][:, 0, d - 2, :],
-                        lhsT=part[d][r][:, g * P : (g + 1) * P],
+                        back[:, 2 * u + e, :],
+                        lhsT=scaled[:, u, r, e, :],
                         rhs=ident[:],
                         is_transpose=True,
-                        start=(r == 0 and (g == 0 or d >= 2)),
-                        stop=(r == 1 and (g == TURNED - 1 or d >= 2)),
+                        start=(r == 0),
+                        stop=(r == 1),
                     )
 
         def words_back(dst, pairs):
@@ -193,39 +221,47 @@ def tile_moe_mhm_none_kernel(
             words_back(late[g][:, 1, 0, :], early_pairs[:, g])
             words_back(late[g][:, 1, 1, :], late_pairs[g][:])
 
-        def regroup(dst, src):
-            nc.scalar.copy(dst.bitcast(F32).rearrange("p (z u) -> p z u", u=2), src.rearrange("p u z -> p z u"))
-
-        picked = tile([P, LANES, 2, P], F32, "picked")
-        gated = [
-            v.rearrange("z (p e) -> z p e", e=2) for v in (fetched[0][:, 5 * P : 7 * P], fetched[1][:, 3 * P : 5 * P])
-        ]
-
-        def pick(d):
-            u, e = divmod(d, 2)
-            for r in range(2):
-                nc.scalar.activation(picked[:, d, r, :], y[d][:].indirect(pos_sb[r][:, 0 : P // 16]), COPY)
-                nc.tensor.transpose(plain[u][:, r, e, :], picked[:, d, r, :], ident[:])
-
-        def scale(u):
-            nc.scalar.activation(gated[u], plain[u][:, 0].rearrange("z e p -> z p e"), COPY, scale=gate_col[:, 0:1])
-
-        def combine(u):
-            nc.vector.scalar_tensor_tensor(
-                pairs0[u][:], plain[u][:, 1].rearrange("z e p -> z p e"), gate_col[:, 1:2], gated[u], MULT, ADD
+        def regroup(g):
+            nc.scalar.copy(
+                grouped12[:, g * H : (g + 1) * H].bitcast(F32).rearrange("p (z u) -> p z u", u=2),
+                late[g][:, 1].rearrange("p u z -> p z u"),
             )
 
-        codes012 = tile([P, 3 * P], U32, "codes012")
-        codes3 = tile([P, P], U32, "codes3")
-        codes = [codes012[:, g * P : (g + 1) * P] for g in range(3)] + [codes3[:]]
+        empty(nc.scalar.copy, 1, 2 * C, S, rest[0])
+        fetch_and_turn(0, 0, TURNED, 1)
+        pick(0)
+        empty(nc.scalar.copy, 2, 2 * C, S, rest[1])
+        pick(1)
+        fetch_and_turn(1, 0, TURNED)
+        empty(nc.scalar.copy, 3, 0, 2 * C, rest[2])
+        empty(nc.scalar.copy, 3, 2 * C, S, rest[3])
+        back = bank([P, LANES, P], 3, "back")
+        fetch_and_turn(2, 0, TURNED)
+        pick(2)
+        scale(0, back)
+        pick(3)
+        for g in range(TURNED):
+            fetch_and_turn(3, g, g + 1)
+        nc.scalar.copy(early_pairs[:], early[:].rearrange("z g e p -> z g p e"))
+        scale(1, back)
+        for g in range(TURNED):
+            turn_back(g)
+        for g in range(TURNED):
+            regroup(g)
+        nc.scalar.copy(grouped0[:].rearrange("p (z d) -> p z d", d=LANES), back[:].rearrange("p d z -> p z d"))
+
+        last = [fetched[r][:, 2 * P : 6 * P].rearrange("p (d z) -> p d z", z=P) for r in range(2)]
+        for d in (3, 1, 2):
+            for r in range(2):
+                fetch(last[r][:, d, :], d, r, W, ZV)
+
+        codes = tile([P, Z], U32, "codes")
         planes = tile([P, Z], U8, "planes")
 
-        def quantise(dst, scales, values):
-            nc.vector.quantize_mx(out=dst.bitcast(FP8X4), scales=scales, in_=values)
+        def quantise(z0, z1, values):
+            nc.vector.quantize_mx(out=codes[:, z0:z1].bitcast(FP8X4), scales=planes[:, z0:z1], in_=values)
 
-        merged = [
-            [bank([P, P], merge_banks[2 * half + nh], "merged%d_%d" % (half, nh)) for nh in range(2)] for half in range(2)
-        ]
+        merged = [[bank([P, P], b, "merged%d" % b) for b in pair] for pair in ((2, 4), (6, 0))]
 
         def merge(g):
             o, half = divmod(g, 2)
@@ -235,47 +271,13 @@ def tile_moe_mhm_none_kernel(
                     out=merged[half][nh][:],
                     lhsT=mw[:, o, cols].bitcast(FP8X4),
                     lhsT_scale=ms[4 * o : P, cols],
-                    rhs=codes[g].bitcast(FP8X4),
+                    rhs=codes[:, g * P : (g + 1) * P].bitcast(FP8X4),
                     rhs_scale=planes[:, g * P : (g + 1) * P],
-                    start=(g in (1, 2)),
-                    stop=(g in (0, 3)),
+                    start=(o == 1),
+                    stop=(o == 0),
                 )
 
-        product(1, 2 * C, S, 3, nc.scalar.copy)
-        pick(0)
-        product(2, 2 * C, S, 4, nc.scalar.copy)
-        product(3, 0, 2 * C, 5, nc.scalar.copy)
-        product(3, 2 * C, S, 2, nc.scalar.copy)
-        for d in range(1, LANES):
-            pick(d)
-        fetch_and_turn(0, 0, TURNED, 1)
-        fetch_and_turn(1, 0, TURNED)
-        scale(0)
-        nc.scalar.copy(early_pairs[:], early[:].rearrange("z g e p -> z g p e"))
-        scale(1)
-        fetch_and_turn(2, 0, TURNED)
-        for g in range(TURNED):
-            fetch_and_turn(3, g, g + 1)
-            turn_back(g)
-        last = [fetched[r][:, 2 * P : 6 * P].rearrange("p (d z) -> p d z", z=P) for r in range(2)]
-        for d, r in ((1, 0), (2, 0), (3, 1)):
-            fetch(last[r][:, d, :], d, r, W, ZV)
-        combine(0)
-        fetch(last[0][:, 3, :], 3, 0, W, ZV)
-        combine(1)
-        for d in (1, 2):
-            fetch(last[1][:, d, :], d, 1, W, ZV)
-        for u in range(2):
-            words_back(plain[1][:, 0, u, :], pairs0[u][:])
-        for g in range(TURNED):
-            regroup(grouped12[:, g * H : (g + 1) * H], late[g][:, 1])
-        regroup(grouped0[:], plain[1][:, 0])
-        quantise(codes012[:, P : 3 * P], planes[:, P : 3 * P], grouped12[:])
-        merge(1)
-        merge(2)
-        quantise(codes[0], planes[:, 0:P], grouped0[:])
-        merge(0)
-        halves = [tile([P, H // 2], BF16, "grouped3_%d" % k, tag) for k, tag in enumerate(("grouped12", "grouped0"))]
+        halves = [tile([P, H // 2], BF16, "grouped3_%d" % k) for k in range(2)]
         for k in range(2):
             cols = slice(k * P // 2, (k + 1) * P // 2)
             nc.vector.tensor_tensor(
@@ -285,16 +287,20 @@ def tile_moe_mhm_none_kernel(
                 ADD,
             )
         for k in range(2):
-            z0, z1 = k * P // 2, (k + 1) * P // 2
-            quantise(codes3[:, z0:z1], planes[:, 3 * P + z0 : 3 * P + z1], halves[k][:])
+            quantise(3 * P + k * P // 2, 3 * P + (k + 1) * P // 2, halves[k][:])
         merge(3)
+        quantise(P, 3 * P, grouped12[:])
+        merge(1)
+        merge(2)
+        quantise(0, P, grouped0[:])
+        merge(0)
 
         out_v = out.rearrange("(nh p) t -> p nh t", p=P)
         res = [tile([P, 2, P], F32, "res%d" % half) for half in range(2)]
-        nc.scalar.copy(res[0][:, 0, :], merged[0][0][:])
-        nc.scalar.copy(res[0][:, 1, :], merged[0][1][:])
-        nc.sync.dma_start(out_v[:, :, 0:P], res[0][:])
         nc.scalar.copy(res[1][:, 0, :], merged[1][0][:])
-        nc.sync.dma_start(out_v[:, 0, P:T], res[1][:, 0, :])
-        nc.vector.tensor_copy(res[1][:, 1, :], merged[1][1][:])
-        nc.sync.dma_start(out_v[:, 1, P:T], res[1][:, 1, :])
+        nc.scalar.copy(res[1][:, 1, :], merged[1][1][:])
+        nc.sync.dma_start(out_v[:, :, P:T], res[1][:])
+        nc.scalar.copy(res[0][:, 0, :], merged[0][0][:])
+        nc.sync.dma_start(out_v[:, 0, 0:P], res[0][:, 0, :])
+        nc.vector.tensor_copy(res[0][:, 1, :], merged[0][1][:])
+        nc.sync.dma_start(out_v[:, 1, 0:P], res[0][:, 1, :])

@@ -164,12 +164,18 @@ def tile_moe_mhm_none_kernel(
         ]
         early = bank([P, TURNED, 2, P], 6, "early")
         plain = [bank([P, 2, 2, P], u, "plain%d" % u) for u in range(2)]
-        late = [bank([P, 2, 2, P], (7, 5)[g], "late%d" % g) for g in range(TURNED)]
+        late = [bank([P, 2, P], (7, 5)[g], "late%d" % g) for g in range(TURNED)]
         early_pairs = tile([P, TURNED, P, 2], BF16, "early_pairs")
         late_pairs = [tile([P, P, 2], BF16, "late_pairs%d" % g) for g in range(TURNED)]
         grouped0 = tile([P, H], BF16, "grouped0")
         grouped12 = tile([P, 2 * H], BF16, "grouped12")
-        picked = tile([P, LANES, 2, P], F32, "picked")
+        own = tile([P, 5, P], F32, "own")
+        picked = [
+            [own[:, 0, :], own[:, 1, :]],
+            [own[:, 2, :], own[:, 3, :]],
+            [fetched[1][:, 3 * P : 4 * P], fetched[0][:, 4 * P : 5 * P]],
+            [fetched[1][:, 4 * P : 5 * P], own[:, 4, :]],
+        ]
         scaled = tile([P, 2, 2, 2, P], F32, "scaled")
 
         def fetch(dst, d, r, z0, z1):
@@ -179,7 +185,7 @@ def tile_moe_mhm_none_kernel(
 
         def turn(d, r, g):
             nc.tensor.matmul(
-                early[:, g, d, :] if d < 2 else late[g][:, 0, d - 2, :],
+                early[:, g, d, :] if d < 2 else late[g][:, d - 2, :],
                 lhsT=part[d][r][:, g * P : (g + 1) * P],
                 rhs=ident[:],
                 is_transpose=True,
@@ -196,8 +202,8 @@ def tile_moe_mhm_none_kernel(
         def pick(d):
             u, e = divmod(d, 2)
             for r in range(2):
-                nc.scalar.activation(picked[:, d, r, :], y[d][:].indirect(pos_sb[r][:, 0 : P // 16]), COPY)
-                nc.tensor.transpose(plain[u][:, r, e, :], picked[:, d, r, :], ident[:])
+                nc.scalar.activation(picked[d][r], y[d][:].indirect(pos_sb[r][:, 0 : P // 16]), COPY)
+                nc.tensor.transpose(plain[u][:, r, e, :], picked[d][r], ident[:])
 
         def scale(u, back):
             for r in range(2):
@@ -216,15 +222,10 @@ def tile_moe_mhm_none_kernel(
         def words_back(dst, pairs):
             nc.tensor.transpose(dst, pairs.rearrange("z p e -> z (p e)").bitcast(F32), ident[:])
 
-        def turn_back(g):
-            nc.scalar.copy(late_pairs[g][:], late[g][:, 0].rearrange("z e p -> z p e"))
-            words_back(late[g][:, 1, 0, :], early_pairs[:, g])
-            words_back(late[g][:, 1, 1, :], late_pairs[g][:])
-
         def regroup(g):
             nc.scalar.copy(
                 grouped12[:, g * H : (g + 1) * H].bitcast(F32).rearrange("p (z u) -> p z u", u=2),
-                late[g][:, 1].rearrange("p u z -> p z u"),
+                packed[g][:].rearrange("p u z -> p z u"),
             )
 
         empty(nc.scalar.copy, 1, 2 * C, S, rest[0])
@@ -238,17 +239,21 @@ def tile_moe_mhm_none_kernel(
         back = bank([P, LANES, P], 3, "back")
         fetch_and_turn(2, 0, TURNED)
         pick(2)
-        scale(0, back)
         pick(3)
+        scale(0, back)
         for g in range(TURNED):
             fetch_and_turn(3, g, g + 1)
         nc.scalar.copy(early_pairs[:], early[:].rearrange("z g e p -> z g p e"))
+        packed = [bank([P, 2, P], (6, 0)[g], "packed%d" % g) for g in range(TURNED)]
+        for g in range(TURNED):
+            words_back(packed[g][:, 0, :], early_pairs[:, g])
         scale(1, back)
         for g in range(TURNED):
-            turn_back(g)
+            nc.scalar.copy(late_pairs[g][:], late[g][:].rearrange("z e p -> z p e"))
+            words_back(packed[g][:, 1, :], late_pairs[g][:])
+        nc.scalar.copy(grouped0[:].rearrange("p (z d) -> p z d", d=LANES), back[:].rearrange("p d z -> p z d"))
         for g in range(TURNED):
             regroup(g)
-        nc.scalar.copy(grouped0[:].rearrange("p (z d) -> p z d", d=LANES), back[:].rearrange("p d z -> p z d"))
 
         last = [fetched[r][:, 2 * P : 6 * P].rearrange("p (d z) -> p d z", z=P) for r in range(2)]
         for d in (3, 1, 2):
@@ -261,20 +266,20 @@ def tile_moe_mhm_none_kernel(
         def quantise(z0, z1, values):
             nc.vector.quantize_mx(out=codes[:, z0:z1].bitcast(FP8X4), scales=planes[:, z0:z1], in_=values)
 
-        merged = [[bank([P, P], b, "merged%d" % b) for b in pair] for pair in ((2, 4), (6, 0))]
+        merged = [[bank([P, P], b, "merged%d" % b)[:] for b in pair] for pair in ((2, 4), (5, 3))]
 
         def merge(g):
             o, half = divmod(g, 2)
             for nh in range(2):
                 cols = slice(nh * P, (nh + 1) * P)
                 nc.tensor.matmul_mx(
-                    out=merged[half][nh][:],
+                    out=merged[half][nh],
                     lhsT=mw[:, o, cols].bitcast(FP8X4),
                     lhsT_scale=ms[4 * o : P, cols],
                     rhs=codes[:, g * P : (g + 1) * P].bitcast(FP8X4),
                     rhs_scale=planes[:, g * P : (g + 1) * P],
-                    start=(o == 1),
-                    stop=(o == 0),
+                    start=(g in (0, 3)),
+                    stop=(g in (1, 2)),
                 )
 
         halves = [tile([P, H // 2], BF16, "grouped3_%d" % k) for k in range(2)]
@@ -289,18 +294,18 @@ def tile_moe_mhm_none_kernel(
         for k in range(2):
             quantise(3 * P + k * P // 2, 3 * P + (k + 1) * P // 2, halves[k][:])
         merge(3)
-        quantise(P, 3 * P, grouped12[:])
-        merge(1)
-        merge(2)
         quantise(0, P, grouped0[:])
         merge(0)
+        for g in (1, 2):
+            quantise(g * P, (g + 1) * P, grouped12[:, (g - 1) * H : g * H])
+            merge(g)
 
         out_v = out.rearrange("(nh p) t -> p nh t", p=P)
         res = [tile([P, 2, P], F32, "res%d" % half) for half in range(2)]
-        nc.scalar.copy(res[1][:, 0, :], merged[1][0][:])
-        nc.scalar.copy(res[1][:, 1, :], merged[1][1][:])
+        nc.scalar.copy(res[1][:, 0, :], merged[1][0])
+        nc.vector.tensor_copy(res[1][:, 1, :], merged[1][1])
         nc.sync.dma_start(out_v[:, :, P:T], res[1][:])
-        nc.scalar.copy(res[0][:, 0, :], merged[0][0][:])
+        nc.scalar.copy(res[0][:, 0, :], merged[0][0])
         nc.sync.dma_start(out_v[:, 0, 0:P], res[0][:, 0, :])
-        nc.vector.tensor_copy(res[0][:, 1, :], merged[0][1][:])
+        nc.vector.tensor_copy(res[0][:, 1, :], merged[0][1])
         nc.sync.dma_start(out_v[:, 1, 0:P], res[0][:, 1, :])

@@ -109,13 +109,14 @@ def tile_moe_mhm_none_kernel(
         for s0, s1 in pieces:
             gather_words(s0, s1)
 
-        wp01 = tile([P, LANES, 2 * P], U32, "wp01")
+        wp01 = [tile([P, 2, 2 * P], U32, "wp01_%d" % u) for u in range(2)]
         wp23 = [tile([P, 2 * P], I32, "wp23_%d" % d) for d in range(LANES)]
         wsp = tile([P, LANES, P], U8, "wsp")
         ws_lanes = ws[:].rearrange("p (m d) -> p d m", d=LANES)
-        nc.scalar.copy(wp01[:].rearrange("p d c -> p c d"), ww[0][:].bitcast(U32).rearrange("p (c d) -> p c d", d=LANES))
-        nc.gpsimd.tensor_copy(wsp[:, 0, :], ws_lanes[:, 0, :])
-        nc.gpsimd.tensor_copy(wsp[:, 1:LANES, :], ws_lanes[:, 1:LANES, :])
+        ww_lanes = ww[0][:].bitcast(U32).rearrange("p (c d) -> p c d", d=LANES)
+        for u in range(2):
+            nc.scalar.copy(wp01[u][:].rearrange("p d c -> p c d"), ww_lanes[:, :, 2 * u : 2 * u + 2])
+            nc.gpsimd.tensor_copy(wsp[:, 2 * u : 2 * u + 2, :], ws_lanes[:, 2 * u : 2 * u + 2, :])
         for d in range(LANES):
             nc.gpsimd.tensor_copy(wp23[d][:], ww[1][:].rearrange("p (c d) -> p d c", d=LANES)[:, d, :])
 
@@ -129,7 +130,7 @@ def tile_moe_mhm_none_kernel(
                 cols = slice(e % 2 * P, (e % 2 + 1) * P)
                 nc.tensor.matmul_mx(
                     out=acc[:, t0 - s0 : t1 - s0],
-                    lhsT=(wp01[:, d, cols] if e < 2 else wp23[d][:, cols]).bitcast(FP8X4),
+                    lhsT=(wp01[d // 2][:, d % 2, cols] if e < 2 else wp23[d][:, cols]).bitcast(FP8X4),
                     lhsT_scale=wsp[4 * e : P, d, :],
                     rhs=words(t0, t1).bitcast(FP8X4),
                     rhs_scale=sg[:, t0:t1],

@@ -170,12 +170,12 @@ def tile_moe_mhm_none_kernel(
         late_pairs = [tile([P, P, 2], BF16, "late_pairs%d" % g) for g in range(TURNED)]
         grouped0 = tile([P, H], BF16, "grouped0")
         grouped12 = tile([P, 2 * H], BF16, "grouped12")
-        own = tile([P, 5, P], F32, "own")
+        own = tile([P, 8, P], F32, "own")
         picked = [
             [own[:, 0, :], own[:, 1, :]],
             [own[:, 2, :], own[:, 3, :]],
-            [fetched[1][:, 3 * P : 4 * P], fetched[0][:, 4 * P : 5 * P]],
-            [fetched[1][:, 4 * P : 5 * P], own[:, 4, :]],
+            [own[:, 4, :], own[:, 5, :]],
+            [own[:, 6, :], own[:, 7, :]],
         ]
         scaled = tile([P, 2, 2, 2, P], F32, "scaled")
 

@@ -21,9 +21,8 @@ S = E * C
 LANES = 4
 WORD_WINDOW = 704
 BYTE_WINDOW = 704
-TURNED = 2
-W = TURNED * P
-ZV = Z - P
+MIXED = 3
+W = MIXED * P
 FLOPS = 2 * H * H * S + 2 * D * H * N * T
 
 
@@ -49,8 +48,9 @@ def tile_moe_mhm_none_kernel(
         ws = tile([P, H], U8, "ws")
         mw = tile([P, D, N], I32, "mw")
         ms = tile([P, N], U8, "ms")
-        gate_sb = tile([P, 2, ZV], F32, "gate_sb")
-        gate_col = tile([P, 2], F32, "gate_col")
+        gate2 = tile([P, Z], F32, "gate2")
+        gate1 = tile([P, P], F32, "gate1")
+        gate_col = tile([P, MIXED], F32, "gate_col")
 
         nc.vector.memset(xs[:].bitcast(I32), 0)
         nc.gpsimd.memset(ws[:].bitcast(I32), 0)
@@ -77,8 +77,9 @@ def tile_moe_mhm_none_kernel(
             )
         nc.sync.dma_start(ww[1][:].rearrange("p (e l) -> p e l", l=H), w_rows[:, 2:E, :])
         nc.sync.dma_start(pos_sb[1][:], pos2)
-        nc.sync.dma_start(gate_sb[:], gate[:, :, P:Z].rearrange("r p z -> p r z"))
-        nc.sync.dma_start(gate_col[:], gate[:, 0, 0:P].rearrange("r z -> z r"), allow_slow_non_contiguous=True)
+        nc.sync.dma_start(gate2[:], gate[1])
+        nc.sync.dma_start(gate1[:], gate[0, :, W:Z])
+        nc.sync.dma_start(gate_col[:], gate[0, 0, 0:W].rearrange("(g z) -> z g", z=P), allow_slow_non_contiguous=True)
         nc.sync.dma_start(mw[:], wm_words.rearrange("o p n d -> p o (n d)").bitcast(I32))
         for q in range(4):
             nc.sync.dma_start(
@@ -155,119 +156,54 @@ def tile_moe_mhm_none_kernel(
 
         rest = [multiply(*a) for a in ((1, 2 * C, S, 3), (2, 2 * C, S, 4), (3, 0, 2 * C, 5), (3, 2 * C, S, 2))]
 
-        fetched = [tile([P, 7 * P], F32, "fetched%d" % r) for r in range(2)]
-        second = [tile([P, W], F32, "second%d" % r) for r in range(2)]
-        part = [
-            [fetched[r][:, 0:ZV] for r in range(2)],
-            [second[r][:] for r in range(2)],
-            [fetched[r][:, 5 * P : 7 * P] for r in range(2)],
-            [fetched[r][:, 3 * P : 5 * P] for r in range(2)],
-        ]
-        early = bank([P, TURNED, 2, P], 6, "early")
-        plain = [bank([P, 2, 2, P], u, "plain%d" % u) for u in range(2)]
-        late = [bank([P, 2, P], (7, 5)[g], "late%d" % g) for g in range(TURNED)]
-        early_pairs = tile([P, TURNED, P, 2], BF16, "early_pairs")
-        late_pairs = [tile([P, P, 2], BF16, "late_pairs%d" % g) for g in range(TURNED)]
-        grouped0 = tile([P, H], BF16, "grouped0")
-        grouped12 = tile([P, 2 * H], BF16, "grouped12")
-        own = tile([P, 8, P], F32, "own")
-        picked = [
-            [own[:, 0, :], own[:, 1, :]],
-            [own[:, 2, :], own[:, 3, :]],
-            [own[:, 4, :], own[:, 5, :]],
-            [own[:, 6, :], own[:, 7, :]],
-        ]
-        scaled = tile([P, 2, 2, 2, P], F32, "scaled")
+        first = [tile([P, W], F32, "first%d" % d) for d in range(LANES)]
+        first3 = tile([P, LANES, P], F32, "first_last")
+        second = tile([P, LANES, Z], F32, "second")
+        scaled = [[tile([P, 2, P], F32, "scaled%d_%d" % (u, g)) for g in range(MIXED)] for u in range(2)]
+        order = (1, 0, 2)
+        turned = []
+        for u in range(2):
+            pair = bank([P, 2, 2, P], (0, 6)[u], "turned%d" % u)
+            turned.append({1: pair[:, 0], 0: pair[:, 1], 2: bank([P, 2, P], (1, 7)[u], "turned%d_2" % u)[:]})
+        back = {g: bank([P, LANES, P], number, "back%d" % g) for g, number in zip(order, (3, 4, 5))}
 
-        def fetch(dst, d, r, z0, z1):
-            nc.vector.tensor_tensor(
-                dst, y[d][:].indirect(pos_sb[r][:, (P + z0) // 16 : (P + z1) // 16]), gate_sb[:, r, z0:z1], MULT
-            )
+        def fetch_second(d):
+            nc.vector.tensor_tensor(second[:, d, :], y[d][:].indirect(pos_sb[1][:]), gate2[:], MULT)
 
-        def turn(d, r, g):
-            nc.tensor.matmul(
-                early[:, g, d, :] if d < 2 else late[g][:, d - 2, :],
-                lhsT=part[d][r][:, g * P : (g + 1) * P],
-                rhs=ident[:],
-                is_transpose=True,
-                start=(d % 2 == 0 and r == 0 and (g == 0 or d >= 2)),
-                stop=(d % 2 == 1 and r == 1 and (g == TURNED - 1 or d >= 2)),
-            )
+        def fetch_first3(d):
+            nc.vector.tensor_tensor(first3[:, d, :], y[d][:].indirect(pos_sb[0][:, W // 16 : Z // 16]), gate1[:], MULT)
 
-        def fetch_and_turn(d, g0, g1, more=0):
-            for r in range(2):
-                fetch(part[d][r][:, g0 * P : (g1 + more) * P], d, r, g0 * P, (g1 + more) * P)
-                for g in range(g0, g1):
-                    turn(d, r, g)
-
-        def pick(d):
+        def pick(d, groups=order):
             u, e = divmod(d, 2)
-            for r in range(2):
-                nc.scalar.activation(picked[d][r], y[d][:].indirect(pos_sb[r][:, 0 : P // 16]), COPY)
-                nc.tensor.transpose(plain[u][:, r, e, :], picked[d][r], ident[:])
+            z0, z1 = min(groups) * P, (max(groups) + 1) * P
+            nc.scalar.activation(first[d][:, z0:z1], y[d][:].indirect(pos_sb[0][:, z0 // 16 : z1 // 16]), COPY)
+            for g in groups:
+                nc.tensor.transpose(turned[u][g][:, e, :], first[d][:, g * P : (g + 1) * P], ident[:])
 
-        def scale(u, back):
-            for r in range(2):
-                nc.scalar.activation(scaled[:, u, r], plain[u][:, r], COPY, scale=gate_col[:, r : r + 1])
+        def scale(u, g, on_vector=False):
+            if on_vector:
+                nc.vector.tensor_scalar(scaled[u][g][:], turned[u][g], gate_col[:, g : g + 1], None, MULT)
+            else:
+                nc.scalar.activation(scaled[u][g][:], turned[u][g], COPY, scale=gate_col[:, g : g + 1])
             for e in range(2):
-                for r in range(2):
-                    nc.tensor.matmul(
-                        back[:, 2 * u + e, :],
-                        lhsT=scaled[:, u, r, e, :],
-                        rhs=ident[:],
-                        is_transpose=True,
-                        start=(r == 0),
-                        stop=(r == 1),
-                    )
-
-        def words_back(dst, pairs):
-            nc.tensor.transpose(dst, pairs.rearrange("z p e -> z (p e)").bitcast(F32), ident[:])
-
-        def regroup(g):
-            nc.scalar.copy(
-                grouped12[:, g * H : (g + 1) * H].bitcast(F32).rearrange("p (z u) -> p z u", u=2),
-                packed[g][:].rearrange("p u z -> p z u"),
-            )
-
-        empty(nc.scalar.copy, 1, 2 * C, S, rest[0])
-        fetch_and_turn(0, 0, TURNED, 1)
-        pick(0)
-        empty(nc.scalar.copy, 2, 2 * C, S, rest[1])
-        pick(1)
-        fetch_and_turn(1, 0, TURNED)
-        empty(nc.scalar.copy, 3, 0, 2 * C, rest[2])
-        empty(nc.scalar.copy, 3, 2 * C, S, rest[3])
-        back = bank([P, LANES, P], 3, "back")
-        fetch_and_turn(2, 0, TURNED)
-        pick(2)
-        pick(3)
-        scale(0, back)
-        for g in range(TURNED):
-            fetch_and_turn(3, g, g + 1)
-        nc.scalar.copy(early_pairs[:], early[:].rearrange("z g e p -> z g p e"))
-        packed = [bank([P, 2, P], (6, 0)[g], "packed%d" % g) for g in range(TURNED)]
-        for g in range(TURNED):
-            words_back(packed[g][:, 0, :], early_pairs[:, g])
-        scale(1, back)
-        for g in range(TURNED):
-            nc.scalar.copy(late_pairs[g][:], late[g][:].rearrange("z e p -> z p e"))
-            words_back(packed[g][:, 1, :], late_pairs[g][:])
-        nc.scalar.copy(grouped0[:].rearrange("p (z d) -> p z d", d=LANES), back[:].rearrange("p d z -> p z d"))
-        for g in range(TURNED):
-            regroup(g)
-
-        last = [fetched[r][:, 2 * P : 6 * P].rearrange("p (d z) -> p d z", z=P) for r in range(2)]
-        for d in (3, 1, 2):
-            for r in range(2):
-                fetch(last[r][:, d, :], d, r, W, ZV)
+                nc.tensor.transpose(back[g][:, 2 * u + e, :], scaled[u][g][:, e, :], ident[:])
 
         codes = tile([P, Z], U32, "codes")
         planes = tile([P, Z], U8, "planes")
 
+        def add(values, a, b):
+            nc.vector.tensor_tensor(
+                values.rearrange("p (c i d) -> p c d i", i=4, d=LANES),
+                a.rearrange("p d (c i) -> p c d i", i=4),
+                b.rearrange("p d (c i) -> p c d i", i=4),
+                ADD,
+            )
+
         def quantise(z0, z1, values):
             nc.vector.quantize_mx(out=codes[:, z0:z1].bitcast(FP8X4), scales=planes[:, z0:z1], in_=values)
 
-        merged = [[bank([P, P], b, "merged%d" % b)[:] for b in pair] for pair in ((2, 4), (5, 3))]
+        shared = bank([P, 2, P], 2, "merged1")
+        merged = [[bank([P, P], b, "merged0_%d" % b)[:] for b in (0, 1)], [shared[:, 0], shared[:, 1]]]
 
         def merge(g):
             o, half = divmod(g, 2)
@@ -279,32 +215,48 @@ def tile_moe_mhm_none_kernel(
                     lhsT_scale=ms[4 * o : P, cols],
                     rhs=codes[:, g * P : (g + 1) * P].bitcast(FP8X4),
                     rhs_scale=planes[:, g * P : (g + 1) * P],
-                    start=(g in (0, 3)),
-                    stop=(g in (1, 2)),
+                    start=(g == 0 or (g, nh) == (3, 0)),
+                    stop=(g == 2 or (g, nh) == (1, 1)),
                 )
 
-        halves = [tile([P, H // 2], BF16, "grouped3_%d" % k) for k in range(2)]
-        for k in range(2):
-            cols = slice(k * P // 2, (k + 1) * P // 2)
-            nc.vector.tensor_tensor(
-                halves[k][:].rearrange("p (c i d) -> p c d i", i=4, d=LANES),
-                last[0][:, :, cols].rearrange("p d (c i) -> p c d i", i=4),
-                last[1][:, :, cols].rearrange("p d (c i) -> p c d i", i=4),
-                ADD,
-            )
-        for k in range(2):
-            quantise(3 * P + k * P // 2, 3 * P + (k + 1) * P // 2, halves[k][:])
-        merge(3)
-        quantise(0, P, grouped0[:])
-        merge(0)
-        for g in (1, 2):
-            quantise(g * P, (g + 1) * P, grouped12[:, (g - 1) * H : g * H])
-            merge(g)
+        empty(nc.scalar.copy, 1, 2 * C, S, rest[0])
+        fetch_second(0)
+        pick(0)
+        empty(nc.scalar.copy, 2, 2 * C, S, rest[1])
+        fetch_second(1)
+        pick(1)
+        empty(nc.scalar.copy, 3, 0, 2 * C, rest[2])
+        empty(nc.scalar.copy, 3, 2 * C, S, rest[3])
+        fetch_second(2)
+        fetch_first3(0)
+        fetch_first3(1)
+        pick(2)
+        pick(3)
+        fetch_second(3)
+        fetch_first3(3)
+        plain = tile([P, P], F32, "plain")
+        nc.scalar.activation(plain[:], y[2][:].indirect(pos_sb[0][:, W // 16 : Z // 16]), COPY)
+        nc.vector.tensor_tensor(first3[:, 2, :], plain[:], gate1[:], MULT)
+        grouped = [tile([P, H], BF16, "grouped%d" % g) for g in range(4)]
+        add(grouped[3][:], first3[:], second[:, :, W:Z])
+        scale(0, 1)
+        scale(0, 0)
+        scale(1, 1)
+        scale(1, 0)
+        scale(0, 2)
+        scale(1, 2)
+        waiting = 3
+        for g in order:
+            add(grouped[g][:], back[g][:], second[:, :, g * P : (g + 1) * P])
+            quantise(waiting * P, (waiting + 1) * P, grouped[waiting][:])
+            merge(waiting)
+            waiting = g
+        quantise(waiting * P, (waiting + 1) * P, grouped[waiting][:])
+        merge(waiting)
 
         out_v = out.rearrange("(nh p) t -> p nh t", p=P)
         res = [tile([P, 2, P], F32, "res%d" % half) for half in range(2)]
-        nc.scalar.copy(res[1][:, 0, :], merged[1][0])
-        nc.vector.tensor_copy(res[1][:, 1, :], merged[1][1])
+        nc.scalar.copy(res[1][:], shared[:])
         nc.sync.dma_start(out_v[:, :, P:T], res[1][:])
         nc.scalar.copy(res[0][:, 0, :], merged[0][0])
         nc.sync.dma_start(out_v[:, 0, 0:P], res[0][:, 0, :])

@@ -21,8 +21,7 @@ S = E * C
 LANES = 4
 WORD_WINDOW = 704
 BYTE_WINDOW = 704
-MIXED = 3
-W = MIXED * P
+W = 2 * P
 FLOPS = 2 * H * H * S + 2 * D * H * N * T
 
 
@@ -48,9 +47,10 @@ def tile_moe_mhm_none_kernel(
         ws = tile([P, H], U8, "ws")
         mw = tile([P, D, N], I32, "mw")
         ms = tile([P, N], U8, "ms")
-        gate2 = tile([P, Z], F32, "gate2")
-        gate1 = tile([P, P], F32, "gate1")
-        gate_col = tile([P, MIXED], F32, "gate_col")
+        gate1 = tile([P, Z - W], F32, "gate1")
+        gate2 = tile([P, Z - P], F32, "gate2")
+        gate1_col = tile([P, 2], F32, "gate1_col")
+        gate2_col = tile([P, 1], F32, "gate2_col")
 
         nc.vector.memset(xs[:].bitcast(I32), 0)
         nc.gpsimd.memset(ws[:].bitcast(I32), 0)
@@ -77,9 +77,10 @@ def tile_moe_mhm_none_kernel(
             )
         nc.sync.dma_start(ww[1][:].rearrange("p (e l) -> p e l", l=H), w_rows[:, 2:E, :])
         nc.sync.dma_start(pos_sb[1][:], pos2)
-        nc.sync.dma_start(gate2[:], gate[1])
+        nc.sync.dma_start(gate2[:], gate[1, :, P:Z])
         nc.sync.dma_start(gate1[:], gate[0, :, W:Z])
-        nc.sync.dma_start(gate_col[:], gate[0, 0, 0:W].rearrange("(g z) -> z g", z=P), allow_slow_non_contiguous=True)
+        nc.sync.dma_start(gate1_col[:], gate[0, 0, 0:W].rearrange("(g z) -> z g", z=P), allow_slow_non_contiguous=True)
+        nc.sync.dma_start(gate2_col[:], gate[1, 0:1, 0:P].rearrange("a z -> z a"), allow_slow_non_contiguous=True)
         nc.sync.dma_start(mw[:], wm_words.rearrange("o p n d -> p o (n d)").bitcast(I32))
         for q in range(4):
             nc.sync.dma_start(
@@ -156,37 +157,52 @@ def tile_moe_mhm_none_kernel(
 
         rest = [multiply(*a) for a in ((1, 2 * C, S, 3), (2, 2 * C, S, 4), (3, 0, 2 * C, 5), (3, 2 * C, S, 2))]
 
-        first = [tile([P, W], F32, "first%d" % d) for d in range(LANES)]
-        first3 = tile([P, LANES, P], F32, "first_last")
-        second = tile([P, LANES, Z], F32, "second")
-        scaled = [[tile([P, 2, P], F32, "scaled%d_%d" % (u, g)) for g in range(MIXED)] for u in range(2)]
-        order = (1, 0, 2)
-        turned = []
-        for u in range(2):
-            pair = bank([P, 2, 2, P], (0, 6)[u], "turned%d" % u)
-            turned.append({1: pair[:, 0], 0: pair[:, 1], 2: bank([P, 2, P], (1, 7)[u], "turned%d_2" % u)[:]})
-        back = {g: bank([P, LANES, P], number, "back%d" % g) for g, number in zip(order, (3, 4, 5))}
+        first = tile([P, LANES, Z - W], F32, "first")
+        second = tile([P, LANES, Z - P], F32, "second")
+        plain1 = [tile([P, W], F32, "plain1_%d" % d) for d in range(LANES)]
+        plain2 = [tile([P, P], F32, "plain2_%d" % d) for d in range(LANES)]
+        scaled0 = [tile([P, 2, 2, P], F32, "scaled0_%d" % u) for u in range(2)]
+        scaled1 = [tile([P, 2, P], F32, "scaled1_%d" % u) for u in range(2)]
+        turned0 = [bank([P, 2, 2, P], u, "turned0_%d" % u) for u in range(2)]
+        turned1 = [bank([P, 2, P], 6 + u, "turned1_%d" % u) for u in range(2)]
+        back0 = [bank([P, 2, P], (3, 5)[u], "back0_%d" % u) for u in range(2)]
+        back1 = bank([P, LANES, P], 4, "back1")
 
-        def fetch_second(d):
-            nc.vector.tensor_tensor(second[:, d, :], y[d][:].indirect(pos_sb[1][:]), gate2[:], MULT)
+        def fetch(d):
+            nc.vector.tensor_tensor(second[:, d, :], y[d][:].indirect(pos_sb[1][:, P // 16 : Z // 16]), gate2[:], MULT)
+            nc.vector.tensor_tensor(first[:, d, :], y[d][:].indirect(pos_sb[0][:, W // 16 : Z // 16]), gate1[:], MULT)
 
-        def fetch_first3(d):
-            nc.vector.tensor_tensor(first3[:, d, :], y[d][:].indirect(pos_sb[0][:, W // 16 : Z // 16]), gate1[:], MULT)
-
-        def pick(d, groups=order):
+        def pick1(d):
             u, e = divmod(d, 2)
-            z0, z1 = min(groups) * P, (max(groups) + 1) * P
-            nc.scalar.activation(first[d][:, z0:z1], y[d][:].indirect(pos_sb[0][:, z0 // 16 : z1 // 16]), COPY)
-            for g in groups:
-                nc.tensor.transpose(turned[u][g][:, e, :], first[d][:, g * P : (g + 1) * P], ident[:])
+            nc.scalar.activation(plain1[d][:], y[d][:].indirect(pos_sb[0][:, 0 : W // 16]), COPY)
+            nc.tensor.transpose(turned1[u][:, e, :], plain1[d][:, P:W], ident[:])
+            nc.tensor.transpose(turned0[u][:, 0, e, :], plain1[d][:, 0:P], ident[:])
 
-        def scale(u, g, on_vector=False):
-            if on_vector:
-                nc.vector.tensor_scalar(scaled[u][g][:], turned[u][g], gate_col[:, g : g + 1], None, MULT)
+        def pick2(d):
+            u, e = divmod(d, 2)
+            nc.scalar.activation(plain2[d][:], y[d][:].indirect(pos_sb[1][:, 0 : P // 16]), COPY)
+            nc.tensor.transpose(turned0[u][:, 1, e, :], plain2[d][:], ident[:])
+
+        def scale0(u):
+            for r, col in enumerate((gate1_col[:, 0:1], gate2_col[:])):
+                nc.scalar.activation(scaled0[u][:, r], turned0[u][:, r], COPY, scale=col)
+                for e in range(2):
+                    nc.tensor.matmul(
+                        back0[u][:, e, :],
+                        lhsT=scaled0[u][:, r, e, :],
+                        rhs=ident[:],
+                        is_transpose=True,
+                        start=(r, e) == (0, 0),
+                        stop=(r, e) == (1, 1),
+                    )
+
+        def scale1(u):
+            if u == 0:
+                nc.scalar.activation(scaled1[u][:], turned1[u][:], COPY, scale=gate1_col[:, 1:2])
             else:
-                nc.scalar.activation(scaled[u][g][:], turned[u][g], COPY, scale=gate_col[:, g : g + 1])
+                nc.vector.tensor_scalar(scaled1[u][:], turned1[u][:], gate1_col[:, 1:2], None, MULT)
             for e in range(2):
-                nc.tensor.transpose(back[g][:, 2 * u + e, :], scaled[u][g][:, e, :], ident[:])
+                nc.tensor.transpose(back1[:, 2 * u + e, :], scaled1[u][:, e, :], ident[:])
 
         codes = tile([P, Z], U32, "codes")
         planes = tile([P, Z], U8, "planes")
@@ -202,8 +218,8 @@ def tile_moe_mhm_none_kernel(
         def quantise(z0, z1, values):
             nc.vector.quantize_mx(out=codes[:, z0:z1].bitcast(FP8X4), scales=planes[:, z0:z1], in_=values)
 
-        shared = bank([P, 2, P], 2, "merged1")
-        merged = [[bank([P, P], b, "merged0_%d" % b)[:] for b in (0, 1)], [shared[:, 0], shared[:, 1]]]
+        shared = bank([P, 2, P], 1, "merged1")
+        merged = [[bank([P, P], b, "merged0_%d" % b)[:] for b in (6, 7)], [shared[:, 0], shared[:, 1]]]
 
         def merge(g):
             o, half = divmod(g, 2)
@@ -215,44 +231,42 @@ def tile_moe_mhm_none_kernel(
                     lhsT_scale=ms[4 * o : P, cols],
                     rhs=codes[:, g * P : (g + 1) * P].bitcast(FP8X4),
                     rhs_scale=planes[:, g * P : (g + 1) * P],
-                    start=(g == 0 or (g, nh) == (3, 0)),
-                    stop=(g == 2 or (g, nh) == (1, 1)),
+                    start=(g == 2 or (g, nh) == (3, 0)),
+                    stop=(g == 0 or (g, nh) == (1, 1)),
                 )
 
         empty(nc.scalar.copy, 1, 2 * C, S, rest[0])
-        fetch_second(0)
-        pick(0)
+        fetch(0)
+        pick1(0)
+        pick2(0)
         empty(nc.scalar.copy, 2, 2 * C, S, rest[1])
-        fetch_second(1)
-        pick(1)
+        fetch(1)
+        pick1(1)
+        pick2(1)
         empty(nc.scalar.copy, 3, 0, 2 * C, rest[2])
         empty(nc.scalar.copy, 3, 2 * C, S, rest[3])
-        fetch_second(2)
-        fetch_first3(0)
-        fetch_first3(1)
-        pick(2)
-        pick(3)
-        fetch_second(3)
-        fetch_first3(3)
-        plain = tile([P, P], F32, "plain")
-        nc.scalar.activation(plain[:], y[2][:].indirect(pos_sb[0][:, W // 16 : Z // 16]), COPY)
-        nc.vector.tensor_tensor(first3[:, 2, :], plain[:], gate1[:], MULT)
+        fetch(2)
+        fetch(3)
+        pick1(2)
+        pick1(3)
+        scale1(0)
+        pick2(2)
+        pick2(3)
+        scale0(0)
+        scale0(1)
         grouped = [tile([P, H], BF16, "grouped%d" % g) for g in range(4)]
-        add(grouped[3][:], first3[:], second[:, :, W:Z])
-        scale(0, 1)
-        scale(0, 0)
-        scale(1, 1)
-        scale(1, 0)
-        scale(0, 2)
-        scale(1, 2)
-        waiting = 3
-        for g in order:
-            add(grouped[g][:], back[g][:], second[:, :, g * P : (g + 1) * P])
-            quantise(waiting * P, (waiting + 1) * P, grouped[waiting][:])
-            merge(waiting)
-            waiting = g
-        quantise(waiting * P, (waiting + 1) * P, grouped[waiting][:])
-        merge(waiting)
+        for u in range(2):
+            nc.scalar.copy(
+                grouped[0][:].rearrange("p (z u e) -> p z u e", u=2, e=2)[:, :, u, :],
+                back0[u][:].rearrange("p e z -> p z e"),
+            )
+        scale1(1)
+        add(grouped[3][:], first[:, :, P:W], second[:, :, W : W + P])
+        add(grouped[1][:], back1[:], second[:, :, 0:P])
+        add(grouped[2][:], first[:, :, 0:P], second[:, :, P:W])
+        for g in (3, 1, 2, 0):
+            quantise(g * P, (g + 1) * P, grouped[g][:])
+            merge(g)
 
         out_v = out.rearrange("(nh p) t -> p nh t", p=P)
         res = [tile([P, 2, P], F32, "res%d" % half) for half in range(2)]

@@ -197,10 +197,7 @@ def tile_moe_mhm_none_kernel(
                     )
 
         def scale1(u):
-            if u == 0:
-                nc.scalar.activation(scaled1[u][:], turned1[u][:], COPY, scale=gate1_col[:, 1:2])
-            else:
-                nc.vector.tensor_scalar(scaled1[u][:], turned1[u][:], gate1_col[:, 1:2], None, MULT)
+            nc.vector.tensor_scalar(scaled1[u][:], turned1[u][:], gate1_col[:, 1:2], None, MULT)
             for e in range(2):
                 nc.tensor.transpose(back1[:, 2 * u + e, :], scaled1[u][:, e, :], ident[:])
 

@@ -47,10 +47,8 @@ def tile_moe_mhm_none_kernel(
         ws = tile([P, H], U8, "ws")
         mw = tile([P, D, N], I32, "mw")
         ms = tile([P, N], U8, "ms")
-        gate1 = tile([P, Z - W], F32, "gate1")
-        gate2 = tile([P, Z - P], F32, "gate2")
-        gate1_col = tile([P, 2], F32, "gate1_col")
-        gate2_col = tile([P, 1], F32, "gate2_col")
+        gate_sb = tile([P, 2, Z - P], F32, "gate_sb")
+        gate_col = tile([P, 2], F32, "gate_col")
 
         nc.vector.memset(xs[:].bitcast(I32), 0)
         nc.gpsimd.memset(ws[:].bitcast(I32), 0)
@@ -77,10 +75,8 @@ def tile_moe_mhm_none_kernel(
             )
         nc.sync.dma_start(ww[1][:].rearrange("p (e l) -> p e l", l=H), w_rows[:, 2:E, :])
         nc.sync.dma_start(pos_sb[1][:], pos2)
-        nc.sync.dma_start(gate2[:], gate[1, :, P:Z])
-        nc.sync.dma_start(gate1[:], gate[0, :, W:Z])
-        nc.sync.dma_start(gate1_col[:], gate[0, 0, 0:W].rearrange("(g z) -> z g", z=P), allow_slow_non_contiguous=True)
-        nc.sync.dma_start(gate2_col[:], gate[1, 0:1, 0:P].rearrange("a z -> z a"), allow_slow_non_contiguous=True)
+        nc.sync.dma_start(gate_sb[:], gate[:, :, P:Z].rearrange("r p z -> p r z"))
+        nc.sync.dma_start(gate_col[:], gate[:, 0, 0:P].rearrange("r z -> z r"), allow_slow_non_contiguous=True)
         nc.sync.dma_start(mw[:], wm_words.rearrange("o p n d -> p o (n d)").bitcast(I32))
         for q in range(4):
             nc.sync.dma_start(
@@ -157,26 +153,24 @@ def tile_moe_mhm_none_kernel(
 
         rest = [multiply(*a) for a in ((1, 2 * C, S, 3), (2, 2 * C, S, 4), (3, 0, 2 * C, 5), (3, 2 * C, S, 2))]
 
-        first = tile([P, LANES, Z - W], F32, "first")
+        first = tile([P, LANES, Z - P], F32, "first")
         second = tile([P, LANES, Z - P], F32, "second")
-        plain1 = [tile([P, W], F32, "plain1_%d" % d) for d in range(LANES)]
+        plain1 = tile([P, LANES, W], F32, "plain1")
         plain2 = [tile([P, P], F32, "plain2_%d" % d) for d in range(LANES)]
         scaled0 = [tile([P, 2, 2, P], F32, "scaled0_%d" % u) for u in range(2)]
-        scaled1 = [tile([P, 2, P], F32, "scaled1_%d" % u) for u in range(2)]
         turned0 = [bank([P, 2, 2, P], u, "turned0_%d" % u) for u in range(2)]
-        turned1 = [bank([P, 2, P], 6 + u, "turned1_%d" % u) for u in range(2)]
         back0 = [bank([P, 2, P], (3, 5)[u], "back0_%d" % u) for u in range(2)]
-        back1 = bank([P, LANES, P], 4, "back1")
 
         def fetch(d):
-            nc.vector.tensor_tensor(second[:, d, :], y[d][:].indirect(pos_sb[1][:, P // 16 : Z // 16]), gate2[:], MULT)
-            nc.vector.tensor_tensor(first[:, d, :], y[d][:].indirect(pos_sb[0][:, W // 16 : Z // 16]), gate1[:], MULT)
+            nc.vector.tensor_tensor(second[:, d, :], y[d][:].indirect(pos_sb[1][:, P // 16 : Z // 16]), gate_sb[:, 1, :], MULT)
+            nc.vector.tensor_tensor(
+                first[:, d, W - P :], y[d][:].indirect(pos_sb[0][:, W // 16 : Z // 16]), gate_sb[:, 0, W - P :], MULT
+            )
 
         def pick1(d):
             u, e = divmod(d, 2)
-            nc.scalar.activation(plain1[d][:], y[d][:].indirect(pos_sb[0][:, 0 : W // 16]), COPY)
-            nc.tensor.transpose(turned1[u][:, e, :], plain1[d][:, P:W], ident[:])
-            nc.tensor.transpose(turned0[u][:, 0, e, :], plain1[d][:, 0:P], ident[:])
+            nc.scalar.activation(plain1[:, d, :], y[d][:].indirect(pos_sb[0][:, 0 : W // 16]), COPY)
+            nc.tensor.transpose(turned0[u][:, 0, e, :], plain1[:, d, 0:P], ident[:])
 
         def pick2(d):
             u, e = divmod(d, 2)
@@ -184,8 +178,8 @@ def tile_moe_mhm_none_kernel(
             nc.tensor.transpose(turned0[u][:, 1, e, :], plain2[d][:], ident[:])
 
         def scale0(u):
-            for r, col in enumerate((gate1_col[:, 0:1], gate2_col[:])):
-                nc.scalar.activation(scaled0[u][:, r], turned0[u][:, r], COPY, scale=col)
+            for r in range(2):
+                nc.scalar.activation(scaled0[u][:, r], turned0[u][:, r], COPY, scale=gate_col[:, r : r + 1])
                 for e in range(2):
                     nc.tensor.matmul(
                         back0[u][:, e, :],
@@ -195,11 +189,6 @@ def tile_moe_mhm_none_kernel(
                         start=(r, e) == (0, 0),
                         stop=(r, e) == (1, 1),
                     )
-
-        def scale1(u):
-            nc.vector.tensor_scalar(scaled1[u][:], turned1[u][:], gate1_col[:, 1:2], None, MULT)
-            for e in range(2):
-                nc.tensor.transpose(back1[:, 2 * u + e, :], scaled1[u][:, e, :], ident[:])
 
         codes = tile([P, Z], U32, "codes")
         planes = tile([P, Z], U8, "planes")
@@ -246,7 +235,6 @@ def tile_moe_mhm_none_kernel(
         fetch(3)
         pick1(2)
         pick1(3)
-        scale1(0)
         pick2(2)
         pick2(3)
         scale0(0)
@@ -257,10 +245,15 @@ def tile_moe_mhm_none_kernel(
                 grouped[0][:].rearrange("p (z u e) -> p z u e", u=2, e=2)[:, :, u, :],
                 back0[u][:].rearrange("p e z -> p z e"),
             )
-        scale1(1)
-        add(grouped[3][:], first[:, :, P:W], second[:, :, W : W + P])
-        add(grouped[1][:], back1[:], second[:, :, 0:P])
-        add(grouped[2][:], first[:, :, 0:P], second[:, :, P:W])
+        nc.vector.tensor_tensor(
+            first[:, :, 0 : W - P],
+            plain1[:, :, P:W],
+            gate_sb[:, 0:1, 0 : W - P].to_broadcast([P, LANES, W - P]),
+            MULT,
+        )
+        for g in (3, 1, 2):
+            cols = slice((g - 1) * P, g * P)
+            add(grouped[g][:], first[:, :, cols], second[:, :, cols])
         for g in (3, 1, 2, 0):
             quantise(g * P, (g + 1) * P, grouped[g][:])
             merge(g)

@@ -22,6 +22,7 @@ LANES = 4
 WORD_WINDOW = 704
 BYTE_WINDOW = 704
 W = 2 * P
+HEAD = 32
 FLOPS = 2 * H * H * S + 2 * D * H * N * T
 
 
@@ -43,7 +44,9 @@ def tile_moe_mhm_none_kernel(
         pos_sb = [tile([P, Z // 16], U16, "pos%d_sb" % r) for r in range(2)]
         xw = tile([P, WORD_WINDOW], I32, "xw")
         xs = tile([P, BYTE_WINDOW], U8, "xs")
-        ww = [tile([P, 2 * H], I32, "ww%d" % k) for k in range(2)]
+        ww_head = tile([P, 2, HEAD], I32, "ww_head")
+        ww_rest = tile([P, 2, H - HEAD], I32, "ww_rest")
+        ww23 = tile([P, 2 * H], I32, "ww23")
         ws = tile([P, H], U8, "ws")
         mw = tile([P, D, N], I32, "mw")
         ms = tile([P, N], U8, "ms")
@@ -60,20 +63,21 @@ def tile_moe_mhm_none_kernel(
             x_words.rearrange("o p t d -> p o (t d)").bitcast(I32),
         )
         nc.sync.dma_start(offs_sb[:], offs)
-        nc.sync.dma_start(pos_sb[0][:], pos1)
+        w_rows = w_words[:, 0].rearrange("e p l d -> p e (l d)").bitcast(I32)
+        nc.sync.dma_start(ww_head[:], w_rows[:, 0:2, 0:HEAD])
         for q in range(4):
             nc.sync.dma_start(
                 xs[32 * q : 32 * q + 4, 0:Z].bitcast(I32).rearrange("r (o t) -> r o t", o=D),
                 x_scales[:, 4 * q : 4 * q + 4, :].bitcast(I32).rearrange("o r t -> r o t"),
             )
-        w_rows = w_words[:, 0].rearrange("e p l d -> p e (l d)").bitcast(I32)
-        nc.sync.dma_start(ww[0][:].rearrange("p (e l) -> p e l", l=H), w_rows[:, 0:2, :])
+        nc.sync.dma_start(ww_rest[:], w_rows[:, 0:2, HEAD:H])
         for q in range(4):
             nc.sync.dma_start(
                 ws[32 * q : 32 * q + 4 * E, :].bitcast(I32),
                 w_scales[:, 0, 4 * q : 4 * q + 4, :].bitcast(I32),
             )
-        nc.sync.dma_start(ww[1][:].rearrange("p (e l) -> p e l", l=H), w_rows[:, 2:E, :])
+        nc.sync.dma_start(ww23[:].rearrange("p (e l) -> p e l", l=H), w_rows[:, 2:E, :])
+        nc.sync.dma_start(pos_sb[0][:], pos1)
         nc.sync.dma_start(pos_sb[1][:], pos2)
         nc.sync.dma_start(gate_sb[:], gate[:, :, P:Z].rearrange("r p z -> p r z"))
         nc.sync.dma_start(gate_col[:], gate[:, 0, 0:P].rearrange("r z -> z r"), allow_slow_non_contiguous=True)
@@ -87,7 +91,26 @@ def tile_moe_mhm_none_kernel(
         ident = tile([P, P], F32, "ident")
         make_identity(nc, ident[:])
 
-        xg = [tile([P, 2 * C], U32, "xg0"), tile([P, 2 * C], U32, "xg1", "xs")]
+        wp01 = [tile([P, 2, 2 * P], U32, "wp01_%d" % u) for u in range(2)]
+        wp23 = [tile([P, 2 * P], I32, "wp23_%d" % d) for d in range(LANES)]
+        wsp = tile([P, LANES, P], U8, "wsp")
+        ws_lanes = ws[:].rearrange("p (m d) -> p d m", d=LANES)
+        for d in range(LANES):
+            nc.gpsimd.tensor_copy(
+                wp01[d // 2][:, d % 2, :].rearrange("p (e c) -> p e c", e=2)[:, :, 0 : HEAD // LANES],
+                ww_head[:].bitcast(U32).rearrange("p e (c d) -> p e c d", d=LANES)[:, :, :, d],
+            )
+        for u in range(2):
+            nc.scalar.copy(
+                wp01[u][:].rearrange("p d (e c) -> p e c d", e=2)[:, :, HEAD // LANES :, :],
+                ww_rest[:].bitcast(U32).rearrange("p e (c d) -> p e c d", d=LANES)[:, :, :, 2 * u : 2 * u + 2],
+            )
+        for u in range(2):
+            nc.gpsimd.tensor_copy(wsp[:, 2 * u : 2 * u + 2, :], ws_lanes[:, 2 * u : 2 * u + 2, :])
+        for d in range(LANES):
+            nc.gpsimd.tensor_copy(wp23[d][:], ww23[:].rearrange("p (c d) -> p d c", d=LANES)[:, d, :])
+
+        xg = [tile([P, 2 * C], U32, "xg0"), tile([P, 2 * C], U32, "xg1", "ww_head")]
         sg = tile([P, S], U8, "sg")
 
         def words(s0, s1):
@@ -107,22 +130,11 @@ def tile_moe_mhm_none_kernel(
         for s0, s1 in pieces:
             gather_words(s0, s1)
 
-        wp01 = [tile([P, 2, 2 * P], U32, "wp01_%d" % u) for u in range(2)]
-        wp23 = [tile([P, 2 * P], I32, "wp23_%d" % d) for d in range(LANES)]
-        wsp = tile([P, LANES, P], U8, "wsp")
-        ws_lanes = ws[:].rearrange("p (m d) -> p d m", d=LANES)
-        ww_lanes = ww[0][:].bitcast(U32).rearrange("p (c d) -> p c d", d=LANES)
-        for u in range(2):
-            nc.scalar.copy(wp01[u][:].rearrange("p d c -> p c d"), ww_lanes[:, :, 2 * u : 2 * u + 2])
-            nc.gpsimd.tensor_copy(wsp[:, 2 * u : 2 * u + 2, :], ws_lanes[:, 2 * u : 2 * u + 2, :])
-        for d in range(LANES):
-            nc.gpsimd.tensor_copy(wp23[d][:], ww[1][:].rearrange("p (c d) -> p d c", d=LANES)[:, d, :])
-
         y = [tile([P, S], F32, "y%d" % d) for d in range(LANES)]
 
         def multiply(d, s0, s1, number):
             acc = bank([P, s1 - s0], number, "yacc%d_%d" % (d, s0))
-            for t0 in range(s0, s1, C):
+            for t0 in range(s0, s1, C)[:: -1 if number == 7 else 1]:
                 t1 = min(t0 + C, s1)
                 e = t0 // C
                 cols = slice(e % 2 * P, (e % 2 + 1) * P)
@@ -151,7 +163,7 @@ def tile_moe_mhm_none_kernel(
         def empty(copy, d, s0, s1, acc):
             copy(y[d][:, s0:s1], acc[:])
 
-        rest = [multiply(*a) for a in ((1, 2 * C, S, 3), (2, 2 * C, S, 4), (3, 0, 2 * C, 5), (3, 2 * C, S, 2))]
+        rest = [multiply(*a) for a in ((1, 2 * C, S, 7), (2, 2 * C, S, 4), (3, 0, 2 * C, 5), (3, 2 * C, S, 2))]
 
         first = tile([P, LANES, Z - P], F32, "first")
         second = tile([P, LANES, Z - P], F32, "second")
@@ -263,6 +275,5 @@ def tile_moe_mhm_none_kernel(
         nc.scalar.copy(res[1][:], shared[:])
         nc.sync.dma_start(out_v[:, :, P:T], res[1][:])
         nc.scalar.copy(res[0][:, 0, :], merged[0][0])
-        nc.sync.dma_start(out_v[:, 0, 0:P], res[0][:, 0, :])
         nc.vector.tensor_copy(res[0][:, 1, :], merged[0][1])
-        nc.sync.dma_start(out_v[:, 1, 0:P], res[0][:, 1, :])
+        nc.sync.dma_start(out_v[:, :, 0:P], res[0][:])

@@ -32,6 +32,7 @@ def tile_moe_mhm_none_kernel(
     nc = tc.nc
     with ExitStack() as ctx:
         sb = ctx.enter_context(tc.tile_pool(name="sb", bufs=1))
+        slots = ctx.enter_context(tc.tile_pool(name="slots", bufs=1))
         ps = ctx.enter_context(tc.psum_pool(name="ps", bufs=1))
 
         def tile(shape, dtype, name, tag=None):
@@ -46,7 +47,8 @@ def tile_moe_mhm_none_kernel(
         xs = tile([P, BYTE_WINDOW], U8, "xs")
         ww_head = tile([P, 2, HEAD], I32, "ww_head")
         ww_rest = tile([P, 2, H - HEAD], I32, "ww_rest")
-        ww23 = tile([P, 2 * H], I32, "ww23")
+        ww2 = slots.tile([P, S + C], I32, name="ww2", align_bytes=64, offset=4 * S - 2 * C)
+        ww3 = tile([P, H], I32, "ww3")
         ws = tile([P, H], U8, "ws")
         mw = tile([P, D, N], I32, "mw")
         ms = tile([P, N], U8, "ms")
@@ -76,23 +78,27 @@ def tile_moe_mhm_none_kernel(
                 ws[32 * q : 32 * q + 4 * E, :].bitcast(I32),
                 w_scales[:, 0, 4 * q : 4 * q + 4, :].bitcast(I32),
             )
-        nc.sync.dma_start(ww23[:].rearrange("p (e l) -> p e l", l=H), w_rows[:, 2:E, :])
+        nc.sync.dma_start(ww2[:, 0:H], w_rows[:, 2, :])
+        nc.sync.dma_start(ww3[:], w_rows[:, 3, :])
         nc.sync.dma_start(pos_sb[0][:], pos1)
         nc.sync.dma_start(pos_sb[1][:], pos2)
-        nc.sync.dma_start(gate_sb[:], gate[:, :, P:Z].rearrange("r p z -> p r z"))
+        for r in (1, 0):
+            nc.sync.dma_start(gate_sb[:, r, :], gate[r, :, P:Z])
         nc.sync.dma_start(gate_col[:], gate[:, 0, 0:P].rearrange("r z -> z r"), allow_slow_non_contiguous=True)
-        nc.sync.dma_start(mw[:], wm_words.rearrange("o p n d -> p o (n d)").bitcast(I32))
-        for q in range(4):
-            nc.sync.dma_start(
-                ms[32 * q : 32 * q + 4 * D, :].bitcast(I32),
-                wm_scales[:, 4 * q : 4 * q + 4, :].bitcast(I32),
-            )
+        for o in range(D):
+            nc.sync.dma_start(mw[:, o, :], wm_words[o].rearrange("p n d -> p (n d)").bitcast(I32))
+            for q in range(4):
+                nc.sync.dma_start(
+                    ms[32 * q + 4 * o : 32 * q + 4 * o + 4, :].bitcast(I32),
+                    wm_scales[o, 4 * q : 4 * q + 4, :].bitcast(I32),
+                )
 
         ident = tile([P, P], F32, "ident")
         make_identity(nc, ident[:])
 
         wp01 = [tile([P, 2, 2 * P], U32, "wp01_%d" % u) for u in range(2)]
-        wp23 = [tile([P, 2 * P], I32, "wp23_%d" % d) for d in range(LANES)]
+        wp2 = tile([P, LANES, P], U32, "wp2")
+        wp3 = tile([P, LANES, P], I32, "wp3")
         wsp = tile([P, LANES, P], U8, "wsp")
         ws_lanes = ws[:].rearrange("p (m d) -> p d m", d=LANES)
         for d in range(LANES):
@@ -105,10 +111,14 @@ def tile_moe_mhm_none_kernel(
                 wp01[u][:].rearrange("p d (e c) -> p e c d", e=2)[:, :, HEAD // LANES :, :],
                 ww_rest[:].bitcast(U32).rearrange("p e (c d) -> p e c d", d=LANES)[:, :, :, 2 * u : 2 * u + 2],
             )
-        for u in range(2):
-            nc.gpsimd.tensor_copy(wsp[:, 2 * u : 2 * u + 2, :], ws_lanes[:, 2 * u : 2 * u + 2, :])
-        for d in range(LANES):
-            nc.gpsimd.tensor_copy(wp23[d][:], ww23[:].rearrange("p (c d) -> p d c", d=LANES)[:, d, :])
+        nc.scalar.copy(
+            wp2[:].rearrange("p d c -> p c d"), ww2[:, 0:H].bitcast(U32).rearrange("p (c d) -> p c d", d=LANES)
+        )
+        steps = ((0, 1), (1, 2), (2, LANES))
+        for d0, d1 in steps:
+            nc.gpsimd.tensor_copy(wsp[:, d0:d1, :], ws_lanes[:, d0:d1, :])
+        for d0, d1 in steps:
+            nc.gpsimd.tensor_copy(wp3[:, d0:d1, :], ww3[:].rearrange("p (c d) -> p d c", d=LANES)[:, d0:d1, :])
 
         xg = [tile([P, 2 * C], U32, "xg0"), tile([P, 2 * C], U32, "xg1", "ww_head")]
         sg = tile([P, S], U8, "sg")
@@ -130,7 +140,7 @@ def tile_moe_mhm_none_kernel(
         for s0, s1 in pieces:
             gather_words(s0, s1)
 
-        y = [tile([P, S], F32, "y%d" % d) for d in range(LANES)]
+        y = [slots.tile([P, S], F32, name="y%d" % d, align_bytes=64, offset=4 * S * d) for d in range(LANES)]
 
         def multiply(d, s0, s1, number):
             acc = bank([P, s1 - s0], number, "yacc%d_%d" % (d, s0))
@@ -140,7 +150,7 @@ def tile_moe_mhm_none_kernel(
                 cols = slice(e % 2 * P, (e % 2 + 1) * P)
                 nc.tensor.matmul_mx(
                     out=acc[:, t0 - s0 : t1 - s0],
-                    lhsT=(wp01[d // 2][:, d % 2, cols] if e < 2 else wp23[d][:, cols]).bitcast(FP8X4),
+                    lhsT=(wp01[d // 2][:, d % 2, cols] if e < 2 else (wp2, wp3)[e - 2][:, d, :]).bitcast(FP8X4),
                     lhsT_scale=wsp[4 * e : P, d, :],
                     rhs=words(t0, t1).bitcast(FP8X4),
                     rhs_scale=sg[:, t0:t1],
@@ -275,5 +285,6 @@ def tile_moe_mhm_none_kernel(
         nc.scalar.copy(res[1][:], shared[:])
         nc.sync.dma_start(out_v[:, :, P:T], res[1][:])
         nc.scalar.copy(res[0][:, 0, :], merged[0][0])
+        nc.sync.dma_start(out_v[:, 0, 0:P], res[0][:, 0, :])
         nc.vector.tensor_copy(res[0][:, 1, :], merged[0][1])
-        nc.sync.dma_start(out_v[:, :, 0:P], res[0][:])
+        nc.sync.dma_start(out_v[:, 1, 0:P], res[0][:, 1, :])

from contextlib import ExitStack

import concourse.mybir as mybir
from concourse.masks import make_identity

F32 = mybir.dt.float32
BF16 = mybir.dt.bfloat16
I32 = mybir.dt.int32
U32 = mybir.dt.uint32
U16 = mybir.dt.uint16
U8 = mybir.dt.uint8
FP8X4 = mybir.dt.float8_e4m3fn_x4
MULT = mybir.AluOpType.mult
ADD = mybir.AluOpType.add
COPY = mybir.ActivationFunctionType.Copy

P = 128
D, T, E, C, H, N = 2, 256, 4, 256, 512, 256
Z = D * T
S = E * C
LANES = 4
WORD_WINDOW = 704
BYTE_WINDOW = 704
W = 2 * P
HEAD = 32
FLOPS = 2 * H * H * S + 2 * D * H * N * T


def tile_moe_mhm_none_kernel(
    tc, x_words, x_scales, w_words, w_scales, wm_words, wm_scales, gate, offs, pos1, pos2, out
):
    nc = tc.nc
    with ExitStack() as ctx:
        sb = ctx.enter_context(tc.tile_pool(name="sb", bufs=1))
        slots = ctx.enter_context(tc.tile_pool(name="slots", bufs=1))
        ps = ctx.enter_context(tc.psum_pool(name="ps", bufs=1))

        def tile(shape, dtype, name, tag=None):
            return sb.tile(shape, dtype, name=name, tag=tag or name, align_bytes=64)

        def bank(shape, number, name):
            return ps.tile(shape, F32, name=name, tag="bank%d" % number)

        offs_sb = tile([P, S // 16], U16, "offs_sb")
        pos_sb = [tile([P, Z // 16], U16, "pos%d_sb" % r) for r in range(2)]
        xw = tile([P, WORD_WINDOW], I32, "xw")
        xs = tile([P, BYTE_WINDOW], U8, "xs")
        ww_head = tile([P, 2, HEAD], I32, "ww_head")
        ww_rest = tile([P, 2, H - HEAD], I32, "ww_rest")
        ww2 = slots.tile([P, S + C], I32, name="ww2", align_bytes=64, offset=4 * S - 2 * C)
        ww3 = tile([P, H], I32, "ww3")
        ws = tile([P, H], U8, "ws")
        mw = tile([P, D, N], I32, "mw")
        ms = tile([P, N], U8, "ms")
        gate_sb = tile([P, 2, Z - P], F32, "gate_sb")
        gate_col = tile([P, 2], F32, "gate_col")

        nc.vector.memset(xs[:].bitcast(I32), 0)
        nc.gpsimd.memset(ws[:].bitcast(I32), 0)
        nc.vector.memset(ms[:].bitcast(I32), 0)
        nc.vector.memset(xw[:, Z:WORD_WINDOW], 0)

        nc.sync.dma_start(
            xw[:, 0:Z].rearrange("p (o t) -> p o t", o=D),
            x_words.rearrange("o p t d -> p o (t d)").bitcast(I32),
        )
        nc.sync.dma_start(offs_sb[:], offs)
        w_rows = w_words[:, 0].rearrange("e p l d -> p e (l d)").bitcast(I32)
        nc.sync.dma_start(ww_head[:], w_rows[:, 0:2, 0:HEAD])
        for q in range(4):
            nc.sync.dma_start(
                xs[32 * q : 32 * q + 4, 0:Z].bitcast(I32).rearrange("r (o t) -> r o t", o=D),
                x_scales[:, 4 * q : 4 * q + 4, :].bitcast(I32).rearrange("o r t -> r o t"),
            )
        nc.sync.dma_start(ww_rest[:], w_rows[:, 0:2, HEAD:H])
        for q in range(4):
            nc.sync.dma_start(
                ws[32 * q : 32 * q + 4 * E, :].bitcast(I32),
                w_scales[:, 0, 4 * q : 4 * q + 4, :].bitcast(I32),
            )
        nc.sync.dma_start(ww2[:, 0:H], w_rows[:, 2, :])
        nc.sync.dma_start(ww3[:], w_rows[:, 3, :])
        nc.sync.dma_start(pos_sb[0][:], pos1)
        nc.sync.dma_start(pos_sb[1][:], pos2)
        for r in (1, 0):
            nc.sync.dma_start(gate_sb[:, r, :], gate[r, :, P:Z])
        nc.sync.dma_start(gate_col[:], gate[:, 0, 0:P].rearrange("r z -> z r"), allow_slow_non_contiguous=True)
        for o in range(D):
            nc.sync.dma_start(mw[:, o, :], wm_words[o].rearrange("p n d -> p (n d)").bitcast(I32))
            for q in range(4):
                nc.sync.dma_start(
                    ms[32 * q + 4 * o : 32 * q + 4 * o + 4, :].bitcast(I32),
                    wm_scales[o, 4 * q : 4 * q + 4, :].bitcast(I32),
                )

        ident = tile([P, P], F32, "ident")
        make_identity(nc, ident[:])

        wp01 = [tile([P, 2, 2 * P], U32, "wp01_%d" % u) for u in range(2)]
        wp2 = tile([P, LANES, P], U32, "wp2")
        wp3 = tile([P, LANES, P], I32, "wp3")
        wsp = tile([P, LANES, P], U8, "wsp")
        ws_lanes = ws[:].rearrange("p (m d) -> p d m", d=LANES)
        for d in range(LANES):
            nc.gpsimd.tensor_copy(
                wp01[d // 2][:, d % 2, :].rearrange("p (e c) -> p e c", e=2)[:, :, 0 : HEAD // LANES],
                ww_head[:].bitcast(U32).rearrange("p e (c d) -> p e c d", d=LANES)[:, :, :, d],
            )
        for u in range(2):
            nc.scalar.copy(
                wp01[u][:].rearrange("p d (e c) -> p e c d", e=2)[:, :, HEAD // LANES :, :],
                ww_rest[:].bitcast(U32).rearrange("p e (c d) -> p e c d", d=LANES)[:, :, :, 2 * u : 2 * u + 2],
            )
        nc.scalar.copy(
            wp2[:].rearrange("p d c -> p c d"), ww2[:, 0:H].bitcast(U32).rearrange("p (c d) -> p c d", d=LANES)
        )
        steps = ((0, 1), (1, 2), (2, LANES))
        for d0, d1 in steps:
            nc.gpsimd.tensor_copy(wsp[:, d0:d1, :], ws_lanes[:, d0:d1, :])
        for d0, d1 in steps:
            nc.gpsimd.tensor_copy(wp3[:, d0:d1, :], ww3[:].rearrange("p (c d) -> p d c", d=LANES)[:, d0:d1, :])

        xg = [tile([P, 2 * C], U32, "xg0"), tile([P, 2 * C], U32, "xg1", "ww_head")]
        sg = tile([P, S], U8, "sg")

        def words(s0, s1):
            k = s0 // (2 * C)
            return xg[k][:, s0 - 2 * C * k : s1 - 2 * C * k]

        def gather_words(s0, s1):
            nc.vector.tensor_copy(words(s0, s1), xw[:].bitcast(U32).indirect(offs_sb[:, s0 // 16 : s1 // 16]))

        def gather_bytes(s0, s1):
            nc.vector.tensor_copy(sg[:, s0:s1], xs[:].indirect(offs_sb[:, s0 // 16 : s1 // 16]))

        pieces = [(2 * C, 3 * C), (3 * C, S - C // 2), (S - C // 2, S)]
        gather_words(0, 2 * C)
        gather_bytes(0, 2 * C)
        gather_bytes(2 * C, S)
        for s0, s1 in pieces:
            gather_words(s0, s1)

        y = [slots.tile([P, S], F32, name="y%d" % d, align_bytes=64, offset=4 * S * d) for d in range(LANES)]

        def multiply(d, s0, s1, number):
            acc = bank([P, s1 - s0], number, "yacc%d_%d" % (d, s0))
            for t0 in range(s0, s1, C)[:: -1 if number == 7 else 1]:
                t1 = min(t0 + C, s1)
                e = t0 // C
                cols = slice(e % 2 * P, (e % 2 + 1) * P)
                nc.tensor.matmul_mx(
                    out=acc[:, t0 - s0 : t1 - s0],
                    lhsT=(wp01[d // 2][:, d % 2, cols] if e < 2 else (wp2, wp3)[e - 2][:, d, :]).bitcast(FP8X4),
                    lhsT_scale=wsp[4 * e : P, d, :],
                    rhs=words(t0, t1).bitcast(FP8X4),
                    rhs_scale=sg[:, t0:t1],
                    start=True,
                    stop=True,
                )
            return acc

        def product(d, s0, s1, number, copy_out):
            copy_out(y[d][:, s0:s1], multiply(d, s0, s1, number)[:])

        for d in range(2):
            product(d, 0, 2 * C, d, nc.scalar.copy)
        product(2, 0, C, 6, nc.scalar.copy)
        lane2 = multiply(2, C, 2 * C, 2)
        for i, (s0, s1) in enumerate(pieces):
            product(0, s0, s1, 3 + i, nc.scalar.copy if i else nc.vector.tensor_copy)
        nc.vector.tensor_copy(y[2][:, C : 2 * C], lane2[:])

        def empty(copy, d, s0, s1, acc):
            copy(y[d][:, s0:s1], acc[:])

        rest = [multiply(*a) for a in ((1, 2 * C, S, 7), (2, 2 * C, S, 4), (3, 0, 2 * C, 5), (3, 2 * C, S, 2))]

        first = tile([P, LANES, Z - P], F32, "first")
        second = tile([P, LANES, Z - P], F32, "second")
        plain1 = tile([P, LANES, W], F32, "plain1")
        plain2 = [tile([P, P], F32, "plain2_%d" % d) for d in range(LANES)]
        scaled0 = [tile([P, 2, 2, P], F32, "scaled0_%d" % u) for u in range(2)]
        turned0 = [bank([P, 2, 2, P], u, "turned0_%d" % u) for u in range(2)]
        back0 = [bank([P, 2, P], (3, 5)[u], "back0_%d" % u) for u in range(2)]

        def fetch(d):
            nc.vector.tensor_tensor(second[:, d, :], y[d][:].indirect(pos_sb[1][:, P // 16 : Z // 16]), gate_sb[:, 1, :], MULT)
            nc.vector.tensor_tensor(
                first[:, d, W - P :], y[d][:].indirect(pos_sb[0][:, W // 16 : Z // 16]), gate_sb[:, 0, W - P :], MULT
            )

        def pick1(d):
            u, e = divmod(d, 2)
            nc.scalar.activation(plain1[:, d, :], y[d][:].indirect(pos_sb[0][:, 0 : W // 16]), COPY)
            nc.tensor.transpose(turned0[u][:, 0, e, :], plain1[:, d, 0:P], ident[:])

        def pick2(d):
            u, e = divmod(d, 2)
            nc.scalar.activation(plain2[d][:], y[d][:].indirect(pos_sb[1][:, 0 : P // 16]), COPY)
            nc.tensor.transpose(turned0[u][:, 1, e, :], plain2[d][:], ident[:])

        def scale0(u):
            for r in range(2):
                nc.scalar.activation(scaled0[u][:, r], turned0[u][:, r], COPY, scale=gate_col[:, r : r + 1])
                for e in range(2):
                    nc.tensor.matmul(
                        back0[u][:, e, :],
                        lhsT=scaled0[u][:, r, e, :],
                        rhs=ident[:],
                        is_transpose=True,
                        start=(r, e) == (0, 0),
                        stop=(r, e) == (1, 1),
                    )

        codes = tile([P, Z], U32, "codes")
        planes = tile([P, Z], U8, "planes")

        def add(values, a, b):
            nc.vector.tensor_tensor(
                values.rearrange("p (c i d) -> p c d i", i=4, d=LANES),
                a.rearrange("p d (c i) -> p c d i", i=4),
                b.rearrange("p d (c i) -> p c d i", i=4),
                ADD,
            )

        def quantise(z0, z1, values):
            nc.vector.quantize_mx(out=codes[:, z0:z1].bitcast(FP8X4), scales=planes[:, z0:z1], in_=values)

        shared = bank([P, 2, P], 1, "merged1")
        merged = [[bank([P, P], b, "merged0_%d" % b)[:] for b in (6, 7)], [shared[:, 0], shared[:, 1]]]

        def merge(g):
            o, half = divmod(g, 2)
            for nh in range(2):
                cols = slice(nh * P, (nh + 1) * P)
                nc.tensor.matmul_mx(
                    out=merged[half][nh],
                    lhsT=mw[:, o, cols].bitcast(FP8X4),
                    lhsT_scale=ms[4 * o : P, cols],
                    rhs=codes[:, g * P : (g + 1) * P].bitcast(FP8X4),
                    rhs_scale=planes[:, g * P : (g + 1) * P],
                    start=(g == 2 or (g, nh) == (3, 0)),
                    stop=(g == 0 or (g, nh) == (1, 1)),
                )

        empty(nc.scalar.copy, 1, 2 * C, S, rest[0])
        fetch(0)
        pick1(0)
        pick2(0)
        empty(nc.scalar.copy, 2, 2 * C, S, rest[1])
        fetch(1)
        pick1(1)
        pick2(1)
        empty(nc.scalar.copy, 3, 0, 2 * C, rest[2])
        empty(nc.scalar.copy, 3, 2 * C, S, rest[3])
        fetch(2)
        fetch(3)
        pick1(2)
        pick1(3)
        pick2(2)
        pick2(3)
        scale0(0)
        scale0(1)
        grouped = [tile([P, H], BF16, "grouped%d" % g) for g in range(4)]
        for u in range(2):
            nc.scalar.copy(
                grouped[0][:].rearrange("p (z u e) -> p z u e", u=2, e=2)[:, :, u, :],
                back0[u][:].rearrange("p e z -> p z e"),
            )
        nc.vector.tensor_tensor(
            first[:, :, 0 : W - P],
            plain1[:, :, P:W],
            gate_sb[:, 0:1, 0 : W - P].to_broadcast([P, LANES, W - P]),
            MULT,
        )
        for g in (3, 1, 2):
            cols = slice((g - 1) * P, g * P)
            add(grouped[g][:], first[:, :, cols], second[:, :, cols])
        for g in (3, 1, 2, 0):
            quantise(g * P, (g + 1) * P, grouped[g][:])
            merge(g)

        out_v = out.rearrange("(nh p) t -> p nh t", p=P)
        res = [tile([P, 2, P], F32, "res%d" % half) for half in range(2)]
        nc.scalar.copy(res[1][:], shared[:])
        nc.sync.dma_start(out_v[:, :, P:T], res[1][:])
        nc.scalar.copy(res[0][:, 0, :], merged[0][0])
        nc.sync.dma_start(out_v[:, 0, 0:P], res[0][:, 0, :])
        nc.vector.tensor_copy(res[0][:, 1, :], merged[0][1])
        nc.sync.dma_start(out_v[:, 1, 0:P], res[0][:, 1, :])
